import numpy as np
import ml_dtypes


def mxq(x, axis, fmt="e4m3"):
    dtype, down = {"e4m3": (ml_dtypes.float8_e4m3fn, 7), "e5m2": (ml_dtypes.float8_e5m2, 14)}[fmt]
    v = np.moveaxis(np.asarray(x, np.float32).astype(ml_dtypes.bfloat16).astype(np.float64), axis, -1)
    blocks = v.reshape(v.shape[:-1] + (-1, 32))
    amax = np.abs(blocks).max(-1, keepdims=True)
    byte = np.maximum(np.where(amax > 0, np.frexp(amax)[1] - 1 + 127, 0) - down, 1)
    scale = np.exp2(byte - 127.0)
    codes = (blocks / scale).astype(np.float32).astype(dtype).astype(np.float64)
    return np.moveaxis((codes * scale).reshape(v.shape), -1, axis)


WIDE = False


def mx_kscale(k):
    if not WIDE:
        return np.ones(k)
    levels = np.array([30, -30])
    if k % 512:
        return np.exp2(np.random.permutation(np.resize(levels, k // 32))).repeat(32)
    a = np.empty((k // 512, 16))
    for p in range(k // 512):
        a[p, :8] = np.random.permutation(np.resize(levels, 8))
        for g in range(8):
            far = levels[np.abs(levels - a[p, g]) >= 10]
            a[p, g + 8] = far[np.random.randint(len(far))]
    return np.exp2(a.ravel()).repeat(32)


BF16 = ml_dtypes.bfloat16


def bf(x):
    return np.asarray(x, np.float32).astype(BF16)


def f64(x):
    return np.asarray(x).astype(np.float64)


E2M1 = np.array([0.0, 0.5, 1.0, 1.5, 2.0, 3.0, 4.0, 6.0, -0.0, -0.5, -1.0, -1.5, -2.0, -3.0, -4.0, -6.0])


def pack_weight(w, fmt):
    k, n = w.shape
    w = f64(bf(w)).reshape(k // 32, 32, n)
    amax = np.abs(w).max(1)
    if fmt in ("e4m3", "e5m2"):
        byte = np.frexp(amax)[1] - 1 + 127 - (7 if fmt == "e4m3" else 14)
    else:
        mant, ex = np.frexp(amax / 6.0)
        byte = np.where(mant > 0.5, ex, ex - 1) + 127
    byte = np.clip(np.where(amax > 0, byte, 1), 1, 254)
    scaled = (w * np.exp2(127.0 - byte)[:, None, :]).reshape(k, n).astype(np.float32)
    by_word = np.ascontiguousarray(scaled.reshape(k // 512, 128, 4, n).transpose(0, 1, 3, 2))
    if fmt in ("e4m3", "e5m2"):
        words = by_word.astype(ml_dtypes.float8_e4m3fn if fmt == "e4m3" else ml_dtypes.float8_e5m2).view(np.uint8)
    else:
        c = by_word.astype(ml_dtypes.float4_e2m1fn).view(np.uint8) & 0xF
        words = c[..., 0::2] | (c[..., 1::2] << 4)
    return np.ascontiguousarray(words), np.ascontiguousarray(byte.astype(np.uint8).reshape(k // 512, 16, n))


def unpack_weight(words, scales, fmt):
    g, p, n, _ = words.shape
    if fmt in ("e4m3", "e5m2"):
        vals = np.ascontiguousarray(words).view(ml_dtypes.float8_e4m3fn if fmt == "e4m3" else ml_dtypes.float8_e5m2).astype(np.float64)
    else:
        nib = np.empty((g, p, n, 4), np.uint8)
        nib[..., 0::2] = words & 0xF
        nib[..., 1::2] = words >> 4
        vals = E2M1[nib]
    vals = vals * np.repeat(np.exp2(scales.astype(np.float64) - 127.0), 8, axis=1)[..., None]
    return vals.transpose(0, 1, 3, 2).reshape(g * 512, n)


M, K, R = 1024, 2048, 512


def setup_inputs():
    s, t = mx_kscale(K), mx_kscale(M)
    tail = np.exp(0.5 * np.random.standard_normal((K, M)) - 0.25)
    e = f64(bf(2.4 / np.sqrt(K) * np.random.standard_normal((K, M)) * tail))
    g_words, g_scales = pack_weight(e * s[:, None], "e5m2")
    pair = np.exp(0.3 * np.random.standard_normal((M, M)))
    coef = 5.0 / np.sqrt(M) * np.random.standard_normal((M, R))
    return {"g_words": g_words,
            "g_scales": g_scales,
            "errs": bf((e / s[:, None]).T),
            "pair": bf(pair * t),
            "coef": bf(coef / t[:, None]),
            "lam": bf(0.3 * np.random.standard_normal(R))}


def reference(g_words, g_scales, errs, pair, coef, lam):
    g = unpack_weight(g_words, g_scales, "e5m2")
    f = mxq(f64(errs), 1, "e4m3")
    b = g.T @ f.T
    h = b * f64(pair)
    z = mxq(h, 1, "e5m2") @ mxq(f64(coef), 0, "e4m3")
    return z - f64(lam)

@@ -1,0 +1,431 @@
+from contextlib import ExitStack
+
+import concourse.mybir as mybir
+from concourse.masks import make_identity
+
+M, K, R = 1024, 2048, 512
+FLOPS = 2 * M * M * K + 2 * M * M * R
+BYTES = K * M + K * M // 32 + 2 * M * K + 2 * M * M + 2 * M * R + 2 * R + 4 * M * R
+
+F32 = mybir.dt.float32
+BF16 = mybir.dt.bfloat16
+U32 = mybir.dt.uint32
+I32 = mybir.dt.int32
+U8 = mybir.dt.uint8
+E4M3X4 = mybir.dt.float8_e4m3fn_x4
+E5M2X4 = mybir.dt.float8_e5m2_x4
+ALU = mybir.AluOpType
+
+P = 128
+PASS = 512
+GROUPS = K // PASS
+HALVES = M // PASS
+TILES = M // P
+BLOCKS = PASS // P
+
+
+def tile_weighted_diis_residuals_e3_kernel(tc, g_words, g_scales, errs, pair, coef, lam, out):
+    nc = tc.nc
+    with ExitStack() as ctx:
+        keep = ctx.enter_context(tc.tile_pool(name="keep", bufs=1))
+        stage = ctx.enter_context(tc.tile_pool(name="stage", bufs=4))
+        psum = ctx.enter_context(tc.psum_pool(name="psum", bufs=8))
+        ctx.enter_context(tc.manual_schedule())
+
+        g_code = {}
+        g_plane = keep.tile([P, GROUPS, M], U8, align_bytes=64, name="g_plane")
+        pair_sb = {}
+        coef_raw = keep.tile([P, HALVES, 4, R], BF16, align_bytes=64, name="coef_raw")
+        coef_quads = [keep.tile([P, R, 4], BF16, align_bytes=64, name=f"coef_quads{j}") for j in range(HALVES)]
+        coef_code = [keep.tile([P, R], U32, align_bytes=64, name=f"coef_code{j}") for j in range(HALVES)]
+        coef_plane = [keep.tile([P, R], U8, align_bytes=64, name=f"coef_plane{j}") for j in range(HALVES)]
+        lam_sb = keep.tile([P, R], BF16, align_bytes=64, name="lam_sb")
+        ident = keep.tile([P, P], F32, align_bytes=64, name="ident")
+        e_code = [[keep.tile([P, PASS], U32, align_bytes=64, name=f"e_code{j}{g}") for g in range(GROUPS)] for j in range(HALVES)]
+        e_plane = [[keep.tile([P, PASS], U8, align_bytes=64, name=f"e_plane{j}{g}") for g in range(GROUPS)] for j in range(HALVES)]
+        h_code = [[keep.tile([P, 2 * P], U32, align_bytes=64, name=f"h_code{j}{q}") for q in range(4)] for j in range(HALVES)]
+        h_plane = [[keep.tile([P, 2 * P], U8, align_bytes=64, name=f"h_plane{j}{q}") for q in range(4)] for j in range(HALVES)]
+        h_sb = [[keep.tile([P, PASS], BF16, align_bytes=64, name=f"h{j}{i}") for i in range(TILES)] for j in range(HALVES)]
+
+        make_identity(nc, ident[:])
+
+        def warm_setup():
+            zero = keep.tile([P, PASS], BF16, align_bytes=64, name="zero")
+            wm = keep.tile([P, PASS], U32, align_bytes=64, name="warm_moving")
+            wmp = keep.tile([P, PASS], U8, align_bytes=64, name="warm_moving_plane")
+            ws = keep.tile([P, P], U32, align_bytes=64, name="warm_stationary")
+            wsp = keep.tile([P, P], U8, align_bytes=64, name="warm_stationary_plane")
+            nc.vector.memset(zero[:].bitcast(I32), 0)
+            nc.vector.memset(g_plane[:].bitcast(I32), 0)
+            for w in range(4):
+                cols = slice(w * P, (w + 1) * P)
+                nc.vector.quantize_mx(out=wm[:, cols].bitcast(E4M3X4), scales=wmp[:, cols], in_=zero[:])
+            nc.vector.quantize_mx(out=ws[:].bitcast(E5M2X4), scales=wsp[:], in_=zero[:])
+            return wm, wmp, ws, wsp
+
+        def warm(n):
+            wm, wmp, ws, wsp = warm_tiles
+            bank = psum.tile([P, PASS], F32, name="bank")
+            for w in range(n):
+                nc.tensor.matmul_mx(out=bank[:], lhsT=ws[:].bitcast(E5M2X4), lhsT_scale=wsp[:], rhs=wm[:].bitcast(E4M3X4), rhs_scale=wmp[:], start=True, stop=True)
+
+        warm_tiles = warm_setup()
+
+        e_raw = {}
+
+        def load_errs(j, rt):
+            t = keep.tile([P, K], BF16, align_bytes=64, name=f"e_raw{j}{rt}")
+            nc.sync.dma_start(out=t[:], in_=errs[j * PASS + rt * P : j * PASS + (rt + 1) * P, :])
+            e_raw[j, rt] = t
+
+        def load_g(i0, ni, g0, ng):
+            t = keep.tile([P, ng, ni * P], U32, align_bytes=64, name=f"g_code{i0}{g0}")
+            nc.sync.dma_start(
+                out=t[:].bitcast(I32),
+                in_=g_words[g0 : g0 + ng].rearrange("g p n t -> p g (n t)")[:, :, i0 * 4 * P : (i0 + ni) * 4 * P].bitcast(I32),
+            )
+            for i in range(i0, i0 + ni):
+                for g in range(g0, g0 + ng):
+                    g_code[i, g] = (t, g0, i0)
+        def load_scales():
+            for quad in range(4):
+                nc.sync.dma_start(
+                    out=g_plane[32 * quad : 32 * quad + 4, :, :].bitcast(I32),
+                    in_=g_scales[:, 4 * quad : 4 * quad + 4, :].rearrange("g r n -> r g n").bitcast(I32),
+                )
+
+        def load_pair(h, j):
+            pair_sb[h, j] = keep.tile([P, BLOCKS, PASS], BF16, align_bytes=64, name=f"pair{h}{j}")
+            nc.sync.dma_start(
+                out=pair_sb[h, j][:],
+                in_=pair[h * PASS : (h + 1) * PASS, j * PASS : (j + 1) * PASS].rearrange("(i p) j -> p i j", p=P),
+            )
+
+        def load_coef():
+            nc.sync.dma_start(out=coef_raw[:], in_=coef.rearrange("(j p t) r -> p j t r", p=P, t=4))
+
+        def load_lam():
+            nc.sync.dma_start(out=lam_sb[:], in_=lam.partition_broadcast(P))
+
+        load_errs(0, 0)
+        load_scales()
+        load_errs(0, 1)
+        load_errs(0, 2)
+        load_errs(0, 3)
+        load_g(0, 8, 0, 1)
+        load_g(0, 8, 1, 1)
+        load_g(0, 8, 2, 1)
+        load_g(0, 8, 3, 1)
+        load_pair(0, 0)
+        load_errs(1, 0)
+        load_errs(1, 1)
+        load_pair(1, 0)
+        load_errs(1, 2)
+        load_errs(1, 3)
+        load_pair(0, 1)
+        load_pair(1, 1)
+        load_coef()
+        load_lam()
+
+        split = {}
+        e_quads = {}
+
+        def move(engine, dst, src):
+            if engine == "V":
+                nc.vector.tensor_copy(out=dst, in_=src)
+            else:
+                nc.scalar.copy(out=dst, in_=src)
+
+        def quad_words(quads, col):
+            words = quads.rearrange("p n t -> p (n t)").bitcast(F32)
+            return words[:, 2 * col : 2 * (col + 2 * P)].rearrange("p (b r u) -> p b r u", b=2, u=2)
+
+        e_bank = {}
+
+        def shuf(j, rt, kh, engine):
+            t = stage.tile([P, 2, 2, P], F32, align_bytes=64, name="split", bufs=8)
+            src = e_raw[j, rt][:].bitcast(F32)[:, kh * PASS : (kh + 1) * PASS].rearrange("p (g w u) -> p g u w", g=2, u=2)
+            move(engine, t[:], src)
+            split[j, rt, kh] = t
+
+        def turn(j, g, rt):
+            if (j, g, rt // 2) not in e_bank:
+                bank = psum.tile([P, 4, P], F32, name="bank")
+                e_bank[j, g, rt // 2] = bank
+            for u in range(2):
+                if (j, rt, g // 2) in split:
+                    word = split[j, rt, g // 2][:, g % 2, u, :]
+                else:
+                    word = e_raw[j, rt][:].bitcast(F32)[:, 2 * P * g + u : 2 * P * (g + 1) : 2]
+                nc.tensor.transpose(e_bank[j, g, rt // 2][:, 2 * (rt % 2) + u, :], word, ident[:])
+
+        def gather(j, g, c, engine):
+            if (j, g) not in e_quads:
+                e_quads[j, g] = keep.tile([P, PASS, 4], BF16, align_bytes=64, name=f"e_quads{j}{g}")
+            move(engine, quad_words(e_quads[j, g][:], 2 * c * P), e_bank[j, g, c][:].rearrange("p (b u) r -> p b r u", u=2))
+
+        def quant(j, g, c):
+            cols = slice(2 * c * P, 2 * (c + 1) * P)
+            nc.vector.quantize_mx(
+                out=e_code[j][g][:, cols].bitcast(E4M3X4),
+                scales=e_plane[j][g][:, cols],
+                in_=e_quads[j, g][:, cols, :].rearrange("p n t -> p (n t)"),
+            )
+
+        accs = {}
+
+        def overlap(j, i, g):
+            if g == 0:
+                accs[j, i] = psum.tile([P, PASS], F32, name="bank")
+            t, g0, i0 = g_code[i, g]
+            nc.tensor.matmul_mx(
+                out=accs[j, i][:],
+                lhsT=t[:, g - g0, (i - i0) * P : (i - i0 + 1) * P].bitcast(E5M2X4),
+                lhsT_scale=g_plane[:, g, i * P : (i + 1) * P],
+                rhs=e_code[j][g][:].bitcast(E4M3X4),
+                rhs_scale=e_plane[j][g][:],
+                start=(g == 0),
+                stop=(g == GROUPS - 1),
+            )
+
+        def units(j, i, part):
+            for g in {"F": (0, 1, 2, 3), "0": (0,), "1": (1,), "2": (2,), "3": (3,)}[part]:
+                overlap(j, i, g)
+
+        def weight(j, i):
+            nc.vector.tensor_tensor(
+                out=h_sb[j][i][:].rearrange("p (u w e) -> p u w e", u=2, e=2),
+                in0=accs[j, i][:].rearrange("p (w u e) -> p u w e", u=2, e=2),
+                in1=pair_sb[i // BLOCKS, j][:, i % BLOCKS, :].rearrange("p (w u e) -> p u w e", u=2, e=2),
+                op=ALU.mult,
+            )
+
+        h_bank = {}
+        h_quads = {}
+
+        def turn_h(j, i):
+            q, a = divmod(i, 2)
+            if (j, q) not in h_bank:
+                h_bank[j, q] = psum.tile([P, 4, P], F32, name="bank")
+            words = h_sb[j][i][:].bitcast(F32)
+            for u in range(2):
+                nc.tensor.transpose(h_bank[j, q][:, 2 * a + u, :], words[:, u * P : (u + 1) * P], ident[:])
+
+        def out_h(j, q, engine="A"):
+            h_quads[j, q] = stage.tile([P, 2 * P, 4], BF16, align_bytes=64, name="h_quads", bufs=8)
+            move(engine, quad_words(h_quads[j, q][:], 0), h_bank[j, q][:].rearrange("p (b u) r -> p b r u", u=2))
+
+        def quant_h(j, q):
+            nc.vector.quantize_mx(
+                out=h_code[j][q][:].bitcast(E5M2X4), scales=h_plane[j][q][:], in_=h_quads[j, q][:].rearrange("p n t -> p (n t)")
+            )
+
+        def coef_copy(j, c, engine="A"):
+            cols = slice(c * R // 2, (c + 1) * R // 2)
+            move(engine, coef_quads[j][:, cols, :], coef_raw[:, j, :, cols].rearrange("p t n -> p n t"))
+
+        def coef_quantize(j):
+            nc.vector.quantize_mx(
+                out=coef_code[j][:].bitcast(E4M3X4), scales=coef_plane[j][:], in_=coef_quads[j][:].rearrange("p n t -> p (n t)")
+            )
+
+        def zmm(i):
+            accs[2, i] = psum.tile([P, PASS], F32, name="bank")
+            cols = slice((i % 2) * P, (i % 2 + 1) * P)
+            for j in range(HALVES):
+                nc.tensor.matmul_mx(
+                    out=accs[2, i][:],
+                    lhsT=h_code[j][i // 2][:, cols].bitcast(E5M2X4),
+                    lhsT_scale=h_plane[j][i // 2][:, cols],
+                    rhs=coef_code[j][:].bitcast(E4M3X4),
+                    rhs_scale=coef_plane[j][:],
+                    start=(j == 0),
+                    stop=(j == HALVES - 1),
+                )
+
+        def store_last(i):
+            for c in range(2):
+                cols = slice(c * R // 2, (c + 1) * R // 2)
+                res = keep.tile([P, R // 2], F32, align_bytes=64, name=f"res_last{c}")
+                nc.vector.tensor_tensor(out=res[:], in0=accs[2, i][:, cols], in1=lam_sb[:, cols], op=ALU.subtract)
+                nc.sync.dma_start(out=out[i * P : (i + 1) * P, cols], in_=res[:])
+
+        def store(i):
+            res = keep.tile([P, R], F32, align_bytes=64, name=f"res{i}")
+            nc.vector.tensor_tensor(out=res[:], in0=accs[2, i][:], in1=lam_sb[:], op=ALU.subtract)
+            nc.sync.dma_start(out=out[i * P : (i + 1) * P, :], in_=res[:])
+
+        warm(2)
+        turn(0, 0, 0)
+        turn(0, 1, 0)
+        turn(0, 2, 0)
+        turn(0, 3, 0)
+        warm(1)
+        turn(0, 0, 1)
+        turn(0, 1, 1)
+        turn(0, 2, 1)
+        gather(0, 0, 0, "A")
+        turn(0, 3, 1)
+        gather(0, 1, 0, "V")
+        gather(0, 2, 0, "A")
+        warm(1)
+        turn(0, 0, 2)
+        gather(0, 3, 0, "V")
+        turn(0, 1, 2)
+        turn(0, 2, 2)
+        turn(0, 3, 2)
+        quant(0, 0, 0)
+        quant(0, 1, 0)
+        turn(0, 0, 3)
+        turn(0, 1, 3)
+        turn(0, 2, 3)
+        gather(0, 0, 1, "A")
+        turn(0, 3, 3)
+        gather(0, 1, 1, "V")
+        gather(0, 2, 1, "A")
+        quant(0, 0, 1)
+        gather(0, 3, 1, "V")
+        warm(2)
+        units(0, 0, "0")
+        units(0, 1, "0")
+        quant(0, 1, 1)
+        units(0, 2, "0")
+        quant(0, 2, 0)
+        units(0, 3, "0")
+        quant(0, 3, 0)
+        units(0, 0, "1")
+        quant(0, 2, 1)
+        units(0, 1, "1")
+        quant(0, 3, 1)
+        units(0, 2, "1")
+        units(0, 3, "1")
+        units(0, 0, "2")
+        units(0, 1, "2")
+        units(0, 2, "2")
+        units(0, 3, "2")
+        units(0, 0, "3")
+        units(0, 1, "3")
+        units(0, 2, "3")
+        weight(0, 0)
+        units(0, 3, "3")
+        weight(0, 1)
+        shuf(1, 0, 1, "A")
+        shuf(1, 0, 0, "V")
+        units(0, 4, "F")
+        units(0, 5, "F")
+        shuf(1, 1, 1, "A")
+        shuf(1, 1, 0, "V")
+        weight(0, 2)
+        turn(1, 0, 0)
+        turn(1, 0, 1)
+        turn(1, 1, 0)
+        weight(0, 3)
+        turn(1, 1, 1)
+        gather(1, 0, 0, "A")
+        turn(1, 2, 0)
+        turn(1, 2, 1)
+        turn(1, 3, 0)
+        gather(1, 1, 0, "V")
+        turn(1, 3, 1)
+        gather(1, 2, 0, "A")
+        weight(0, 4)
+        shuf(1, 2, 0, "A")
+        gather(1, 3, 0, "V")
+        units(0, 6, "F")
+        shuf(1, 2, 1, "A")
+        weight(0, 5)
+        turn(1, 0, 2)
+        turn(1, 1, 2)
+        shuf(1, 3, 1, "A")
+        shuf(1, 3, 0, "V")
+        turn(1, 2, 2)
+        weight(0, 6)
+        turn(1, 3, 2)
+        turn_h(0, 0)
+        turn_h(0, 1)
+        quant(1, 0, 0)
+        turn_h(0, 2)
+        turn_h(0, 3)
+        out_h(0, 0, "A")
+        quant(1, 1, 0)
+        turn(1, 0, 3)
+        turn(1, 1, 3)
+        quant(1, 2, 0)
+        turn(1, 2, 3)
+        turn(1, 3, 3)
+        gather(1, 0, 1, "A")
+        quant(1, 3, 0)
+        gather(1, 1, 1, "V")
+        gather(1, 2, 1, "A")
+        quant(1, 0, 1)
+        units(0, 7, "F")
+        gather(1, 3, 1, "A")
+        quant(1, 1, 1)
+        quant(1, 2, 1)
+        out_h(0, 1, "A")
+        quant(1, 3, 1)
+        quant_h(0, 0)
+        units(1, 0, "F")
+        weight(0, 7)
+        quant_h(0, 1)
+        coef_copy(0, 1, "A")
+        weight(1, 0)
+        units(1, 1, "F")
+        turn_h(0, 4)
+        turn_h(0, 5)
+        weight(1, 1)
+        turn_h(0, 6)
+        turn_h(0, 7)
+        out_h(0, 2, "A")
+        coef_copy(0, 0, "V")
+        out_h(0, 3, "A")
+        quant_h(0, 2)
+        units(1, 2, "F")
+        coef_copy(1, 1, "A")
+        quant_h(0, 3)
+        weight(1, 2)
+        units(1, 3, "F")
+        coef_quantize(0)
+        weight(1, 3)
+        units(1, 4, "F")
+        coef_copy(1, 0, "V")
+        weight(1, 4)
+        units(1, 5, "F")
+        coef_quantize(1)
+        turn_h(1, 0)
+        turn_h(1, 1)
+        turn_h(1, 2)
+        turn_h(1, 3)
+        weight(1, 5)
+        out_h(1, 0, "A")
+        out_h(1, 1, "A")
+        quant_h(1, 0)
+        units(1, 6, "F")
+        quant_h(1, 1)
+        weight(1, 6)
+        units(1, 7, "F")
+        zmm(0)
+        weight(1, 7)
+        zmm(1)
+        store(0)
+        turn_h(1, 4)
+        turn_h(1, 5)
+        store(1)
+        turn_h(1, 6)
+        turn_h(1, 7)
+        out_h(1, 2, "A")
+        zmm(2)
+        out_h(1, 3, "A")
+        quant_h(1, 2)
+        zmm(3)
+        quant_h(1, 3)
+        zmm(4)
+        store(2)
+        zmm(5)
+        store(3)
+        zmm(6)
+        store(4)
+        zmm(7)
+        store(5)
+        store(6)
+        store_last(7)

@@ -29,106 +29,11 @@ def tile_weighted_diis_residuals_e3_kernel(tc, g_words, g_scales, errs, pair, co
     with ExitStack() as ctx:
         keep = ctx.enter_context(tc.tile_pool(name="keep", bufs=1))
         stage = ctx.enter_context(tc.tile_pool(name="stage", bufs=4))
-        psum = ctx.enter_context(tc.psum_pool(name="psum", bufs=8))
+        psum = ctx.enter_context(tc.psum_pool(name="psum", bufs=1))
         ctx.enter_context(tc.manual_schedule())
 
-        g_code = {}
-        g_plane = keep.tile([P, GROUPS, M], U8, align_bytes=64, name="g_plane")
-        pair_sb = {}
-        coef_raw = keep.tile([P, HALVES, 4, R], BF16, align_bytes=64, name="coef_raw")
-        coef_quads = [keep.tile([P, R, 4], BF16, align_bytes=64, name=f"coef_quads{j}") for j in range(HALVES)]
-        coef_code = [keep.tile([P, R], U32, align_bytes=64, name=f"coef_code{j}") for j in range(HALVES)]
-        coef_plane = [keep.tile([P, R], U8, align_bytes=64, name=f"coef_plane{j}") for j in range(HALVES)]
-        lam_sb = keep.tile([P, R], BF16, align_bytes=64, name="lam_sb")
-        ident = keep.tile([P, P], F32, align_bytes=64, name="ident")
-        e_code = [[keep.tile([P, PASS], U32, align_bytes=64, name=f"e_code{j}{g}") for g in range(GROUPS)] for j in range(HALVES)]
-        e_plane = [[keep.tile([P, PASS], U8, align_bytes=64, name=f"e_plane{j}{g}") for g in range(GROUPS)] for j in range(HALVES)]
-        h_code = [[keep.tile([P, 2 * P], U32, align_bytes=64, name=f"h_code{j}{q}") for q in range(4)] for j in range(HALVES)]
-        h_plane = [[keep.tile([P, 2 * P], U8, align_bytes=64, name=f"h_plane{j}{q}") for q in range(4)] for j in range(HALVES)]
-        h_sb = [[keep.tile([P, PASS], BF16, align_bytes=64, name=f"h{j}{i}") for i in range(TILES)] for j in range(HALVES)]
-
-        make_identity(nc, ident[:])
-
-        def warm_setup():
-            zero = keep.tile([P, PASS], BF16, align_bytes=64, name="zero")
-            wm = keep.tile([P, PASS], U32, align_bytes=64, name="warm_moving")
-            wmp = keep.tile([P, PASS], U8, align_bytes=64, name="warm_moving_plane")
-            ws = keep.tile([P, P], U32, align_bytes=64, name="warm_stationary")
-            wsp = keep.tile([P, P], U8, align_bytes=64, name="warm_stationary_plane")
-            nc.vector.memset(zero[:].bitcast(I32), 0)
-            nc.vector.memset(g_plane[:].bitcast(I32), 0)
-            for w in range(4):
-                cols = slice(w * P, (w + 1) * P)
-                nc.vector.quantize_mx(out=wm[:, cols].bitcast(E4M3X4), scales=wmp[:, cols], in_=zero[:])
-            nc.vector.quantize_mx(out=ws[:].bitcast(E5M2X4), scales=wsp[:], in_=zero[:])
-            return wm, wmp, ws, wsp
-
-        def warm(n):
-            wm, wmp, ws, wsp = warm_tiles
-            bank = psum.tile([P, PASS], F32, name="bank")
-            for w in range(n):
-                nc.tensor.matmul_mx(out=bank[:], lhsT=ws[:].bitcast(E5M2X4), lhsT_scale=wsp[:], rhs=wm[:].bitcast(E4M3X4), rhs_scale=wmp[:], start=True, stop=True)
-
-        warm_tiles = warm_setup()
-
-        e_raw = {}
-
-        def load_errs(j, rt):
-            t = keep.tile([P, K], BF16, align_bytes=64, name=f"e_raw{j}{rt}")
-            nc.sync.dma_start(out=t[:], in_=errs[j * PASS + rt * P : j * PASS + (rt + 1) * P, :])
-            e_raw[j, rt] = t
-
-        def load_g(i0, ni, g0, ng):
-            t = keep.tile([P, ng, ni * P], U32, align_bytes=64, name=f"g_code{i0}{g0}")
-            nc.sync.dma_start(
-                out=t[:].bitcast(I32),
-                in_=g_words[g0 : g0 + ng].rearrange("g p n t -> p g (n t)")[:, :, i0 * 4 * P : (i0 + ni) * 4 * P].bitcast(I32),
-            )
-            for i in range(i0, i0 + ni):
-                for g in range(g0, g0 + ng):
-                    g_code[i, g] = (t, g0, i0)
-        def load_scales():
-            for quad in range(4):
-                nc.sync.dma_start(
-                    out=g_plane[32 * quad : 32 * quad + 4, :, :].bitcast(I32),
-                    in_=g_scales[:, 4 * quad : 4 * quad + 4, :].rearrange("g r n -> r g n").bitcast(I32),
-                )
-
-        def load_pair(h, j):
-            pair_sb[h, j] = keep.tile([P, BLOCKS, PASS], BF16, align_bytes=64, name=f"pair{h}{j}")
-            nc.sync.dma_start(
-                out=pair_sb[h, j][:],
-                in_=pair[h * PASS : (h + 1) * PASS, j * PASS : (j + 1) * PASS].rearrange("(i p) j -> p i j", p=P),
-            )
-
-        def load_coef():
-            nc.sync.dma_start(out=coef_raw[:], in_=coef.rearrange("(j p t) r -> p j t r", p=P, t=4))
-
-        def load_lam():
-            nc.sync.dma_start(out=lam_sb[:], in_=lam.partition_broadcast(P))
-
-        load_errs(0, 0)
-        load_scales()
-        load_errs(0, 1)
-        load_errs(0, 2)
-        load_errs(0, 3)
-        load_g(0, 8, 0, 1)
-        load_g(0, 8, 1, 1)
-        load_g(0, 8, 2, 1)
-        load_g(0, 8, 3, 1)
-        load_pair(0, 0)
-        load_errs(1, 0)
-        load_errs(1, 1)
-        load_pair(1, 0)
-        load_errs(1, 2)
-        load_errs(1, 3)
-        load_pair(0, 1)
-        load_pair(1, 1)
-        load_coef()
-        load_lam()
-
-        split = {}
-        e_quads = {}
+        def sb(shape, dtype, name):
+            return keep.tile(shape, dtype, align_bytes=64, name=name)
 
         def move(engine, dst, src):
             if engine == "V":
@@ -136,296 +41,337 @@ def tile_weighted_diis_residuals_e3_kernel(tc, g_words, g_scales, errs, pair, co
             else:
                 nc.scalar.copy(out=dst, in_=src)
 
-        def quad_words(quads, col):
-            words = quads.rearrange("p n t -> p (n t)").bitcast(F32)
-            return words[:, 2 * col : 2 * (col + 2 * P)].rearrange("p (b r u) -> p b r u", b=2, u=2)
+        ident = sb([P, P], F32, "ident")
+        make_identity(nc, ident[:])
 
-        e_bank = {}
+        e_raw, e_pair, g_code, g_plane, pair_sb = {}, {}, {}, {}, {}
 
-        def shuf(j, rt, kh, engine):
-            t = stage.tile([P, 2, 2, P], F32, align_bytes=64, name="split", bufs=8)
-            src = e_raw[j, rt][:].bitcast(F32)[:, kh * PASS : (kh + 1) * PASS].rearrange("p (g w u) -> p g u w", g=2, u=2)
-            move(engine, t[:], src)
-            split[j, rt, kh] = t
+        def load_errs(j, rt, g0, ng):
+            t = sb([P, ng * PASS], BF16, f"e_raw{j}{rt}{g0}")
+            rows = slice(j * PASS + rt * P, j * PASS + (rt + 1) * P)
+            nc.sync.dma_start(out=t[:], in_=errs[rows, g0 * PASS : (g0 + ng) * PASS])
+            e_pair[j, rt, g0] = t[:].bitcast(F32)
+            for g in range(g0, g0 + ng):
+                e_raw[j, rt, g] = t[:].bitcast(F32)[:, (g - g0) * 2 * P : (g - g0 + 1) * 2 * P]
 
-        def turn(j, g, rt):
-            if (j, g, rt // 2) not in e_bank:
-                bank = psum.tile([P, 4, P], F32, name="bank")
-                e_bank[j, g, rt // 2] = bank
+        def load_errs_rows(j, rt0, nr, g):
+            t = sb([P, nr, PASS], BF16, f"e_rows{j}{rt0}{g}")
+            rows = slice(j * PASS + rt0 * P, j * PASS + (rt0 + nr) * P)
+            nc.sync.dma_start(out=t[:], in_=errs[rows, g * PASS : (g + 1) * PASS].rearrange("(a p) k -> p a k", p=P))
+            for rt in range(rt0, rt0 + nr):
+                e_raw[j, rt, g] = t[:, rt - rt0, :].bitcast(F32)
+
+        def load_g(g, i0, ni):
+            t = sb([P, ni * P], U32, f"g_code{g}{i0}")
+            nc.sync.dma_start(
+                out=t[:].bitcast(I32), in_=g_words[g].rearrange("p n t -> p (n t)")[:, i0 * 4 * P : (i0 + ni) * 4 * P].bitcast(I32)
+            )
+            for i in range(i0, i0 + ni):
+                g_code[i, g] = t[:, (i - i0) * P : (i - i0 + 1) * P]
+
+        def clear_plane(g0, ng):
+            t = sb([P, ng, M], U8, f"g_plane{g0}")
+            nc.vector.memset(t[:].bitcast(I32), 0)
+            for g in range(g0, g0 + ng):
+                g_plane[g] = (t, g0)
+
+        def load_scales(g0, ng):
+            t = g_plane[g0][0]
+            for r in range(4):
+                nc.sync.dma_start(
+                    out=t[r:P:32, :, :].bitcast(I32),
+                    in_=g_scales[g0 : g0 + ng, r:16:4, :].rearrange("g q n -> q g n").bitcast(I32),
+                )
+
+        def load_pair(j, i0, ni):
+            t = sb([P, ni, PASS], BF16, f"pair{j}{i0}")
+            nc.sync.dma_start(
+                out=t[:], in_=pair[i0 * P : (i0 + ni) * P, j * PASS : (j + 1) * PASS].rearrange("(i p) n -> p i n", p=P)
+            )
+            for i in range(i0, i0 + ni):
+                pair_sb[j, i] = t[:, i - i0, :]
+
+        coef_raw = {}
+
+        def load_coef(j):
+            coef_raw[j] = sb([P, 4, R], BF16, f"coef_raw{j}")
+            nc.sync.dma_start(out=coef_raw[j][:], in_=coef[j * PASS : (j + 1) * PASS, :].rearrange("(p t) r -> p t r", t=4))
+
+        lam_sb = sb([P, R], BF16, "lam_sb")
+
+        def load_lam():
+            nc.sync.dma_start(out=lam_sb[:], in_=lam.partition_broadcast(P))
+
+        def bank(b, shape):
+            return psum.tile(shape, F32, name=f"bank{b}", tag=f"bank{b}")
+
+        sorted_words, e_bank, e_quads, e_code, e_plane = {}, {}, {}, {}, {}
+
+        def sort_words(j, rt, g0, engine):
+            t = stage.tile([P, 2, 2, P], F32, align_bytes=64, name="sorted", bufs=8)
+            move(engine, t[:], e_pair[j, rt, g0].rearrange("p (g w u) -> p g u w", g=2, u=2))
+            for g in (g0, g0 + 1):
+                sorted_words[j, rt, g] = t[:, g - g0]
+
+        def turn(j, g, rt, b):
+            if rt % 2 == 0:
+                e_bank[j, g, rt // 2] = bank(b, [P, 4, P])
             for u in range(2):
-                if (j, rt, g // 2) in split:
-                    word = split[j, rt, g // 2][:, g % 2, u, :]
+                if (j, rt, g) in sorted_words:
+                    word = sorted_words[j, rt, g][:, u, :]
                 else:
-                    word = e_raw[j, rt][:].bitcast(F32)[:, 2 * P * g + u : 2 * P * (g + 1) : 2]
+                    word = e_raw[j, rt, g][:, u : 2 * P : 2]
                 nc.tensor.transpose(e_bank[j, g, rt // 2][:, 2 * (rt % 2) + u, :], word, ident[:])
 
+        def interleave(engine, src, n):
+            t = stage.tile([P, 2 * P, 4], BF16, align_bytes=64, name="quads", bufs=8)
+            words = t[:].rearrange("p n t -> p (n t)").bitcast(F32)[:, : 2 * n * P]
+            move(engine, words.rearrange("p (b r u) -> p b r u", b=n, u=2), src[:, : 2 * n, :].rearrange("p (b u) r -> p b r u", u=2))
+            return t
+
         def gather(j, g, c, engine):
-            if (j, g) not in e_quads:
-                e_quads[j, g] = keep.tile([P, PASS, 4], BF16, align_bytes=64, name=f"e_quads{j}{g}")
-            move(engine, quad_words(e_quads[j, g][:], 2 * c * P), e_bank[j, g, c][:].rearrange("p (b u) r -> p b r u", u=2))
+            e_quads[j, g, c] = interleave(engine, e_bank[j, g, c], 2)
 
         def quant(j, g, c):
+            if c == 0:
+                e_code[j, g] = sb([P, PASS], U32, f"e_code{j}{g}")
+                e_plane[j, g] = sb([P, PASS], U8, f"e_plane{j}{g}")
             cols = slice(2 * c * P, 2 * (c + 1) * P)
             nc.vector.quantize_mx(
-                out=e_code[j][g][:, cols].bitcast(E4M3X4),
-                scales=e_plane[j][g][:, cols],
-                in_=e_quads[j, g][:, cols, :].rearrange("p n t -> p (n t)"),
+                out=e_code[j, g][:, cols].bitcast(E4M3X4),
+                scales=e_plane[j, g][:, cols],
+                in_=e_quads[j, g, c][:].rearrange("p n t -> p (n t)"),
             )
 
-        accs = {}
+        acc = {}
 
-        def overlap(j, i, g):
+        def overlap(j, i, g, b=None):
             if g == 0:
-                accs[j, i] = psum.tile([P, PASS], F32, name="bank")
-            t, g0, i0 = g_code[i, g]
+                acc[j, i] = bank(b, [P, PASS])
+            t, g0 = g_plane[g]
             nc.tensor.matmul_mx(
-                out=accs[j, i][:],
-                lhsT=t[:, g - g0, (i - i0) * P : (i - i0 + 1) * P].bitcast(E5M2X4),
-                lhsT_scale=g_plane[:, g, i * P : (i + 1) * P],
-                rhs=e_code[j][g][:].bitcast(E4M3X4),
-                rhs_scale=e_plane[j][g][:],
+                out=acc[j, i][:],
+                lhsT=g_code[i, g].bitcast(E5M2X4),
+                lhsT_scale=t[:, g - g0, i * P : (i + 1) * P],
+                rhs=e_code[j, g][:].bitcast(E4M3X4),
+                rhs_scale=e_plane[j, g][:],
                 start=(g == 0),
                 stop=(g == GROUPS - 1),
             )
 
-        def units(j, i, part):
-            for g in {"F": (0, 1, 2, 3), "0": (0,), "1": (1,), "2": (2,), "3": (3,)}[part]:
-                overlap(j, i, g)
+        h_sb, h_bank, h_quads, h_code = {}, {}, {}, {}
 
         def weight(j, i):
+            h_sb[j, i] = sb([P, PASS], BF16, f"h{j}{i}")
             nc.vector.tensor_tensor(
-                out=h_sb[j][i][:].rearrange("p (u w e) -> p u w e", u=2, e=2),
-                in0=accs[j, i][:].rearrange("p (w u e) -> p u w e", u=2, e=2),
-                in1=pair_sb[i // BLOCKS, j][:, i % BLOCKS, :].rearrange("p (w u e) -> p u w e", u=2, e=2),
+                out=h_sb[j, i][:].rearrange("p (u w e) -> p u w e", u=2, e=2),
+                in0=acc[j, i][:].rearrange("p (w u e) -> p u w e", u=2, e=2),
+                in1=pair_sb[j, i].rearrange("p (w u e) -> p u w e", u=2, e=2),
                 op=ALU.mult,
             )
 
-        h_bank = {}
-        h_quads = {}
+        def turn_h(units, b):
+            h_bank[units] = bank(b, [P, 4, P])
+            for a, unit in enumerate(units):
+                words = h_sb[unit][:].bitcast(F32)
+                for u in range(2):
+                    nc.tensor.transpose(h_bank[units][:, 2 * a + u, :], words[:, u * P : (u + 1) * P], ident[:])
 
-        def turn_h(j, i):
-            q, a = divmod(i, 2)
-            if (j, q) not in h_bank:
-                h_bank[j, q] = psum.tile([P, 4, P], F32, name="bank")
-            words = h_sb[j][i][:].bitcast(F32)
-            for u in range(2):
-                nc.tensor.transpose(h_bank[j, q][:, 2 * a + u, :], words[:, u * P : (u + 1) * P], ident[:])
+        def gather_h(units, engine):
+            h_quads[units] = interleave(engine, h_bank[units], len(units))
 
-        def out_h(j, q, engine="A"):
-            h_quads[j, q] = stage.tile([P, 2 * P, 4], BF16, align_bytes=64, name="h_quads", bufs=8)
-            move(engine, quad_words(h_quads[j, q][:], 0), h_bank[j, q][:].rearrange("p (b u) r -> p b r u", u=2))
+        def quant_h(units):
+            n = len(units) * P
+            name = "".join(f"{j}{i}" for j, i in units)
+            code = sb([P, n], U32, "h_code" + name)
+            plane = sb([P, n], U8, "h_plane" + name)
+            nc.vector.quantize_mx(out=code[:].bitcast(E5M2X4), scales=plane[:], in_=h_quads[units][:, :n, :].rearrange("p n t -> p (n t)"))
+            for a, unit in enumerate(units):
+                h_code[unit] = (code[:, a * P : (a + 1) * P], plane[:, a * P : (a + 1) * P])
 
-        def quant_h(j, q):
-            nc.vector.quantize_mx(
-                out=h_code[j][q][:].bitcast(E5M2X4), scales=h_plane[j][q][:], in_=h_quads[j, q][:].rearrange("p n t -> p (n t)")
-            )
+        coef_quads, coef_code, coef_plane = {}, {}, {}
 
-        def coef_copy(j, c, engine="A"):
+        def coef_copy(j, c, engine):
+            coef_quads[j, c] = sb([P, R // 2, 4], BF16, f"coef_quads{j}{c}")
+            move(engine, coef_quads[j, c][:], coef_raw[j][:, :, c * R // 2 : (c + 1) * R // 2].rearrange("p t n -> p n t"))
+
+        def coef_quantize(j, c):
+            if c == 0:
+                coef_code[j] = sb([P, R], U32, f"coef_code{j}")
+                coef_plane[j] = sb([P, R], U8, f"coef_plane{j}")
             cols = slice(c * R // 2, (c + 1) * R // 2)
-            move(engine, coef_quads[j][:, cols, :], coef_raw[:, j, :, cols].rearrange("p t n -> p n t"))
-
-        def coef_quantize(j):
             nc.vector.quantize_mx(
-                out=coef_code[j][:].bitcast(E4M3X4), scales=coef_plane[j][:], in_=coef_quads[j][:].rearrange("p n t -> p (n t)")
+                out=coef_code[j][:, cols].bitcast(E4M3X4), scales=coef_plane[j][:, cols], in_=coef_quads[j, c][:].rearrange("p n t -> p (n t)")
             )
 
-        def zmm(i):
-            accs[2, i] = psum.tile([P, PASS], F32, name="bank")
-            cols = slice((i % 2) * P, (i % 2 + 1) * P)
-            for j in range(HALVES):
-                nc.tensor.matmul_mx(
-                    out=accs[2, i][:],
-                    lhsT=h_code[j][i // 2][:, cols].bitcast(E5M2X4),
-                    lhsT_scale=h_plane[j][i // 2][:, cols],
-                    rhs=coef_code[j][:].bitcast(E4M3X4),
-                    rhs_scale=coef_plane[j][:],
-                    start=(j == 0),
-                    stop=(j == HALVES - 1),
-                )
+        res_acc = {}
 
-        def store_last(i):
-            for c in range(2):
-                cols = slice(c * R // 2, (c + 1) * R // 2)
-                res = keep.tile([P, R // 2], F32, align_bytes=64, name=f"res_last{c}")
-                nc.vector.tensor_tensor(out=res[:], in0=accs[2, i][:, cols], in1=lam_sb[:, cols], op=ALU.subtract)
+        def mix(i, j, b=None):
+            if j == 0:
+                res_acc[i] = bank(b, [P, R])
+            code, plane = h_code[j, i]
+            nc.tensor.matmul_mx(
+                out=res_acc[i][:],
+                lhsT=code.bitcast(E5M2X4),
+                lhsT_scale=plane,
+                rhs=coef_code[j][:].bitcast(E4M3X4),
+                rhs_scale=coef_plane[j][:],
+                start=(j == 0),
+                stop=(j == HALVES - 1),
+            )
+
+        def store(i, parts=1):
+            for c in range(parts):
+                cols = slice(c * R // parts, (c + 1) * R // parts)
+                res = sb([P, R // parts], F32, f"res{i}{c}")
+                nc.vector.tensor_tensor(out=res[:], in0=res_acc[i][:, cols], in1=lam_sb[:, cols], op=ALU.subtract)
                 nc.sync.dma_start(out=out[i * P : (i + 1) * P, cols], in_=res[:])
 
-        def store(i):
-            res = keep.tile([P, R], F32, align_bytes=64, name=f"res{i}")
-            nc.vector.tensor_tensor(out=res[:], in0=accs[2, i][:], in1=lam_sb[:], op=ALU.subtract)
-            nc.sync.dma_start(out=out[i * P : (i + 1) * P, :], in_=res[:])
 
-        warm(2)
-        turn(0, 0, 0)
-        turn(0, 1, 0)
-        turn(0, 2, 0)
-        turn(0, 3, 0)
-        warm(1)
-        turn(0, 0, 1)
-        turn(0, 1, 1)
-        turn(0, 2, 1)
+        clear_plane(0, 2)
+        clear_plane(2, 2)
+        for rt in range(4):
+            load_errs(0, rt, 0, 2)
+        load_scales(0, 2)
+        load_g(0, 0, 4)
+        load_g(1, 0, 4)
+        for rt in range(4):
+            load_errs(0, rt, 2, 2)
+        load_g(0, 4, 4)
+        load_g(1, 4, 4)
+        load_scales(2, 2)
+        load_g(2, 0, 8)
+        load_g(3, 0, 8)
+        load_pair(0, 0, 2)
+        load_pair(0, 2, 2)
+        for rt in range(4):
+            load_errs(1, rt, 0, 2)
+        load_pair(0, 4, 2)
+        for rt in range(4):
+            load_errs(1, rt, 2, 2)
+        load_pair(0, 6, 2)
+        load_pair(1, 0, 4)
+        load_coef(0)
+        load_coef(1)
+        load_pair(1, 4, 4)
+        load_lam()
+
+        def turn_pair(j, g0, c, b0):
+            for rt in (2 * c, 2 * c + 1):
+                for g in (g0, g0 + 1):
+                    turn(j, g, rt, b0 + g - g0)
+
+        def passes(j, tiles, groups, b0=0):
+            for g in groups:
+                for i in tiles:
+                    overlap(j, i, g, b0 + i - tiles[0])
+
+        def both(i):
+            return ((0, i), (1, i))
+
+        def h_run(tiles, banks):
+            for i, b in zip(tiles, banks):
+                turn_h(both(i), b)
+                gather_h(both(i), "A")
+
+        def mix_run(tiles, banks):
+            for i, b in zip(tiles, banks):
+                mix(i, 0, b)
+                mix(i, 1)
+
+        turn_pair(0, 0, 0, 4)
         gather(0, 0, 0, "A")
-        turn(0, 3, 1)
         gather(0, 1, 0, "V")
-        gather(0, 2, 0, "A")
-        warm(1)
-        turn(0, 0, 2)
-        gather(0, 3, 0, "V")
-        turn(0, 1, 2)
-        turn(0, 2, 2)
-        turn(0, 3, 2)
         quant(0, 0, 0)
-        quant(0, 1, 0)
-        turn(0, 0, 3)
-        turn(0, 1, 3)
-        turn(0, 2, 3)
+        turn(0, 0, 2, 6)
+        turn(0, 0, 3, 6)
         gather(0, 0, 1, "A")
-        turn(0, 3, 3)
-        gather(0, 1, 1, "V")
-        gather(0, 2, 1, "A")
+        quant(0, 1, 0)
+        turn(0, 1, 2, 7)
+        turn(0, 1, 3, 7)
+        gather(0, 1, 1, "A")
         quant(0, 0, 1)
-        gather(0, 3, 1, "V")
-        warm(2)
-        units(0, 0, "0")
-        units(0, 1, "0")
         quant(0, 1, 1)
-        units(0, 2, "0")
-        quant(0, 2, 0)
-        units(0, 3, "0")
-        quant(0, 3, 0)
-        units(0, 0, "1")
-        quant(0, 2, 1)
-        units(0, 1, "1")
-        quant(0, 3, 1)
-        units(0, 2, "1")
-        units(0, 3, "1")
-        units(0, 0, "2")
-        units(0, 1, "2")
-        units(0, 2, "2")
-        units(0, 3, "2")
-        units(0, 0, "3")
-        units(0, 1, "3")
-        units(0, 2, "3")
-        weight(0, 0)
-        units(0, 3, "3")
-        weight(0, 1)
-        shuf(1, 0, 1, "A")
-        shuf(1, 0, 0, "V")
-        units(0, 4, "F")
-        units(0, 5, "F")
-        shuf(1, 1, 1, "A")
-        shuf(1, 1, 0, "V")
-        weight(0, 2)
-        turn(1, 0, 0)
-        turn(1, 0, 1)
-        turn(1, 1, 0)
-        weight(0, 3)
-        turn(1, 1, 1)
-        gather(1, 0, 0, "A")
-        turn(1, 2, 0)
-        turn(1, 2, 1)
-        turn(1, 3, 0)
-        gather(1, 1, 0, "V")
-        turn(1, 3, 1)
-        gather(1, 2, 0, "A")
+        passes(0, range(4), (0, 1))
+        for rt in range(4):
+            sort_words(0, rt, 2, "V")
+        for c in range(2):
+            turn_pair(0, 2, c, 4 + 2 * c)
+            gather(0, 2, c, "A")
+            gather(0, 3, c, "V")
+        passes(0, range(4, 6), (0, 1), 4)
+        passes(0, range(6, 8), (0, 1), 6)
+        for g in (2, 3):
+            for c in range(2):
+                quant(0, g, c)
+        for i in range(6):
+            passes(0, [i], (2, 3))
+            if i < 4:
+                weight(0, i)
+                sort_words(1, i, 0, "A")
+        for c in range(2):
+            turn_pair(1, 0, c, 2 * c)
+            gather(1, 0, c, "A")
+            gather(1, 1, c, "VA"[c])
+        passes(0, [6], (2, 3))
+        passes(0, [7], (2, 3))
+        sort_words(1, 0, 2, "V")
         weight(0, 4)
-        shuf(1, 2, 0, "A")
-        gather(1, 3, 0, "V")
-        units(0, 6, "F")
-        shuf(1, 2, 1, "A")
+        sort_words(1, 1, 2, "V")
         weight(0, 5)
-        turn(1, 0, 2)
-        turn(1, 1, 2)
-        shuf(1, 3, 1, "A")
-        shuf(1, 3, 0, "V")
-        turn(1, 2, 2)
-        weight(0, 6)
-        turn(1, 3, 2)
-        turn_h(0, 0)
-        turn_h(0, 1)
+        sort_words(1, 2, 2, "V")
         quant(1, 0, 0)
-        turn_h(0, 2)
-        turn_h(0, 3)
-        out_h(0, 0, "A")
-        quant(1, 1, 0)
-        turn(1, 0, 3)
-        turn(1, 1, 3)
-        quant(1, 2, 0)
-        turn(1, 2, 3)
-        turn(1, 3, 3)
-        gather(1, 0, 1, "A")
-        quant(1, 3, 0)
-        gather(1, 1, 1, "V")
-        gather(1, 2, 1, "A")
         quant(1, 0, 1)
-        units(0, 7, "F")
-        gather(1, 3, 1, "A")
+        quant(1, 1, 0)
         quant(1, 1, 1)
-        quant(1, 2, 1)
-        out_h(0, 1, "A")
-        quant(1, 3, 1)
-        quant_h(0, 0)
-        units(1, 0, "F")
+        for c in range(2):
+            turn_pair(1, 2, c, 2 * c)
+            gather(1, 2, c, "A")
+            gather(1, 3, c, "A")
+        weight(0, 6)
         weight(0, 7)
-        quant_h(0, 1)
-        coef_copy(0, 1, "A")
-        weight(1, 0)
-        units(1, 1, "F")
-        turn_h(0, 4)
-        turn_h(0, 5)
-        weight(1, 1)
-        turn_h(0, 6)
-        turn_h(0, 7)
-        out_h(0, 2, "A")
-        coef_copy(0, 0, "V")
-        out_h(0, 3, "A")
-        quant_h(0, 2)
-        units(1, 2, "F")
-        coef_copy(1, 1, "A")
-        quant_h(0, 3)
-        weight(1, 2)
-        units(1, 3, "F")
-        coef_quantize(0)
-        weight(1, 3)
-        units(1, 4, "F")
-        coef_copy(1, 0, "V")
+        passes(1, range(2), (0, 1), 4)
+        passes(1, range(2, 4), (0, 1), 6)
+        for g in (2, 3):
+            for c in range(2):
+                quant(1, g, c)
+        for j in range(2):
+            for c in range(2):
+                coef_copy(j, c, "A")
+        for i in range(4):
+            passes(1, [i], (2, 3))
+            weight(1, i)
+        passes(1, [4], range(4), 0)
+        passes(1, [5], range(4), 1)
         weight(1, 4)
-        units(1, 5, "F")
-        coef_quantize(1)
-        turn_h(1, 0)
-        turn_h(1, 1)
-        turn_h(1, 2)
-        turn_h(1, 3)
+        for j in range(2):
+            for c in range(2):
+                coef_quantize(j, c)
+        h_run(range(4), (2, 3, 4, 5))
         weight(1, 5)
-        out_h(1, 0, "A")
-        out_h(1, 1, "A")
-        quant_h(1, 0)
-        units(1, 6, "F")
-        quant_h(1, 1)
+        passes(1, [6], range(4), 6)
+        quant_h(both(0))
+        quant_h(both(1))
         weight(1, 6)
-        units(1, 7, "F")
-        zmm(0)
-        weight(1, 7)
-        zmm(1)
+        mix_run((0, 1), (7, 0))
+        quant_h(both(2))
+        quant_h(both(3))
+        h_run((4, 5), (1, 2))
         store(0)
-        turn_h(1, 4)
-        turn_h(1, 5)
         store(1)
-        turn_h(1, 6)
-        turn_h(1, 7)
-        out_h(1, 2, "A")
-        zmm(2)
-        out_h(1, 3, "A")
-        quant_h(1, 2)
-        zmm(3)
-        quant_h(1, 3)
-        zmm(4)
+        passes(1, [7], range(4), 3)
+        quant_h(both(4))
+        weight(1, 7)
+        quant_h(both(5))
+        mix_run((2, 3), (4, 5))
         store(2)
-        zmm(5)
+        h_run((6, 7), (6, 7))
         store(3)
-        zmm(6)
+        mix_run((4, 5), (0, 1))
+        quant_h(both(6))
         store(4)
-        zmm(7)
+        quant_h(both(7))
+        mix_run((6, 7), (2, 3))
         store(5)
         store(6)
-        store_last(7)
+        store(7, 2)

@@ -75,10 +75,10 @@ def tile_weighted_diis_residuals_e3_kernel(tc, g_words, g_scales, errs, pair, co
             for g in range(g0, g0 + ng):
                 g_plane[g] = (t, g0)
 
-        def load_scales(g0, ng):
+        def load_scales(g0, ng, queue=nc.sync):
             t = g_plane[g0][0]
             for r in range(4):
-                nc.sync.dma_start(
+                queue.dma_start(
                     out=t[r:P:32, :, :].bitcast(I32),
                     in_=g_scales[g0 : g0 + ng, r:16:4, :].rearrange("g q n -> q g n").bitcast(I32),
                 )
@@ -240,19 +240,20 @@ def tile_weighted_diis_residuals_e3_kernel(tc, g_words, g_scales, errs, pair, co
         load_g(0, 4, 4)
         load_g(1, 4, 4)
         load_scales(2, 2)
-        load_g(2, 0, 8)
-        load_g(3, 0, 8)
-        load_pair(0, 0, 2)
-        load_pair(0, 2, 2)
+        load_g(2, 0, 6)
+        load_g(3, 0, 6)
+        load_pair(0, 0, 3)
+        load_pair(0, 3, 3)
         for rt in range(4):
             load_errs(1, rt, 0, 2)
-        load_pair(0, 4, 2)
+        load_g(2, 6, 2)
+        load_g(3, 6, 2)
+        load_pair(0, 6, 2)
+        load_coef(0)
         for rt in range(4):
             load_errs(1, rt, 2, 2)
-        load_pair(0, 6, 2)
-        load_pair(1, 0, 4)
-        load_coef(0)
         load_coef(1)
+        load_pair(1, 0, 4)
         load_pair(1, 4, 4)
         load_lam()
 
@@ -279,6 +280,18 @@ def tile_weighted_diis_residuals_e3_kernel(tc, g_words, g_scales, errs, pair, co
                 mix(i, 0, b)
                 mix(i, 1)
 
+        def turn_group(j, g, b0):
+            for rt in range(4):
+                turn(j, g, rt, b0 + rt // 2)
+
+        def h_half(j, units, banks, engines="AAAA"):
+            for tiles, b, e in zip(units, banks, engines):
+                turn_h(tuple((j, i) for i in tiles), b)
+                gather_h(tuple((j, i) for i in tiles), e)
+
+        def q_half(j, tiles):
+            quant_h(tuple((j, i) for i in tiles))
+
         turn_pair(0, 0, 0, 4)
         gather(0, 0, 0, "A")
         gather(0, 1, 0, "V")
@@ -304,74 +317,76 @@ def tile_weighted_diis_residuals_e3_kernel(tc, g_words, g_scales, errs, pair, co
         for g in (2, 3):
             for c in range(2):
                 quant(0, g, c)
+
         for i in range(6):
             passes(0, [i], (2, 3))
-            if i < 4:
-                weight(0, i)
-                sort_words(1, i, 0, "A")
-        for c in range(2):
-            turn_pair(1, 0, c, 2 * c)
-            gather(1, 0, c, "A")
-            gather(1, 1, c, "VA"[c])
+            weight(0, i)
+            if 2 <= i < 5:
+                sort_words(1, i - 2, 0, "A")
+        for g in range(2):
+            turn_group(1, g, 2 * g)
+            gather(1, g, 0, "A")
+            gather(1, g, 1, "VA"[g])
         passes(0, [6], (2, 3))
         passes(0, [7], (2, 3))
-        sort_words(1, 0, 2, "V")
-        weight(0, 4)
-        sort_words(1, 1, 2, "V")
-        weight(0, 5)
-        sort_words(1, 2, 2, "V")
-        quant(1, 0, 0)
-        quant(1, 0, 1)
-        quant(1, 1, 0)
-        quant(1, 1, 1)
-        for c in range(2):
-            turn_pair(1, 2, c, 2 * c)
-            gather(1, 2, c, "A")
-            gather(1, 3, c, "A")
+        for g in range(2):
+            for c in range(2):
+                quant(1, g, c)
+        coef_copy(0, 0, "A")
+        coef_copy(0, 1, "A")
         weight(0, 6)
         weight(0, 7)
         passes(1, range(2), (0, 1), 4)
+        h_half(0, ((0, 1), (2, 3), (4, 5), (6, 7)), range(4))
         passes(1, range(2, 4), (0, 1), 6)
+        for rt in range(4):
+            sort_words(1, rt, 2, "V")
+        coef_quantize(0, 0)
+        coef_quantize(0, 1)
+        for q in range(3):
+            q_half(0, (2 * q, 2 * q + 1))
+        for g in (2, 3):
+            turn_group(1, g, 2 * g - 4)
+            gather(1, g, 0, "A")
+            gather(1, g, 1, "VA"[g - 2])
+        passes(1, range(4, 6), (0, 1), 0)
         for g in (2, 3):
             for c in range(2):
                 quant(1, g, c)
-        for j in range(2):
-            for c in range(2):
-                coef_copy(j, c, "A")
-        for i in range(4):
+        q_half(0, (6, 7))
+        coef_copy(1, 0, "A")
+        coef_copy(1, 1, "A")
+
+        passes(1, range(2), (2, 3))
+        weight(1, 0)
+        weight(1, 1)
+        for i in range(2, 6):
             passes(1, [i], (2, 3))
             weight(1, i)
-        passes(1, [4], range(4), 0)
-        passes(1, [5], range(4), 1)
-        weight(1, 4)
-        for j in range(2):
-            for c in range(2):
-                coef_quantize(j, c)
-        h_run(range(4), (2, 3, 4, 5))
-        weight(1, 5)
-        passes(1, [6], range(4), 6)
-        quant_h(both(0))
-        quant_h(both(1))
+        h_half(1, ((0, 1), (2, 3)), (2, 3))
+        coef_quantize(1, 0)
+        coef_quantize(1, 1)
+        passes(1, [6], range(4), 4)
+        q_half(1, (0, 1))
+        q_half(1, (2, 3))
         weight(1, 6)
-        mix_run((0, 1), (7, 0))
-        quant_h(both(2))
-        quant_h(both(3))
-        h_run((4, 5), (1, 2))
+        mix_run((0, 1), (5, 6))
+        h_half(1, ((4, 5), (6,)), (7, 0))
         store(0)
         store(1)
+        mix_run((2, 3), (1, 2))
         passes(1, [7], range(4), 3)
-        quant_h(both(4))
-        weight(1, 7)
-        quant_h(both(5))
-        mix_run((2, 3), (4, 5))
+        q_half(1, (4, 5))
         store(2)
-        h_run((6, 7), (6, 7))
+        q_half(1, (6,))
         store(3)
-        mix_run((4, 5), (0, 1))
-        quant_h(both(6))
+        weight(1, 7)
+        mix_run((4, 5), (4, 5))
+        h_half(1, ((7,),), (6,))
         store(4)
-        quant_h(both(7))
-        mix_run((6, 7), (2, 3))
+        mix_run((6,), (7,))
         store(5)
+        q_half(1, (7,))
+        mix_run((7,), (0,))
         store(6)
         store(7, 2)

@@ -228,6 +228,32 @@ def tile_weighted_diis_residuals_e3_kernel(tc, g_words, g_scales, errs, pair, co
                 nc.sync.dma_start(out=out[i * P : (i + 1) * P, cols], in_=res[:])
 
 
+        def warm_setup():
+            blank = sb([P, 864], U32, "blank")
+            nc.vector.memset(blank[:], 0)
+            zero = blank[:, :64].bitcast(BF16)
+            codes = blank[:, 64:704]
+            planes = blank[:, 704:].bitcast(U8)
+            nc.vector.quantize_mx(out=codes[:, :32].bitcast(E5M2X4), scales=planes[:, :32], in_=zero)
+            nc.vector.quantize_mx(out=codes[:, P : P + 32].bitcast(E4M3X4), scales=planes[:, P : P + 32], in_=zero)
+            return codes, planes
+
+        def warm(n, b):
+            codes, planes = warm_tiles
+            t = bank(b, [P, PASS])
+            for w in range(n):
+                nc.tensor.matmul_mx(
+                    out=t[:],
+                    lhsT=codes[:, :P].bitcast(E5M2X4),
+                    lhsT_scale=planes[:, :P],
+                    rhs=codes[:, P:].bitcast(E4M3X4),
+                    rhs_scale=planes[:, P:],
+                    start=True,
+                    stop=True,
+                )
+
+
+        warm_tiles = warm_setup()
         clear_plane(0, 2)
         clear_plane(2, 2)
         for rt in range(4):
@@ -292,7 +318,12 @@ def tile_weighted_diis_residuals_e3_kernel(tc, g_words, g_scales, errs, pair, co
         def q_half(j, tiles):
             quant_h(tuple((j, i) for i in tiles))
 
-        turn_pair(0, 0, 0, 4)
+        warm(3, 0)
+        turn(0, 0, 0, 4)
+        turn(0, 1, 0, 5)
+        turn(0, 0, 1, 4)
+        turn(0, 1, 1, 5)
+        warm(1, 2)
         gather(0, 0, 0, "A")
         gather(0, 1, 0, "V")
         quant(0, 0, 0)
@@ -302,6 +333,7 @@ def tile_weighted_diis_residuals_e3_kernel(tc, g_words, g_scales, errs, pair, co
         quant(0, 1, 0)
         turn(0, 1, 2, 7)
         turn(0, 1, 3, 7)
+        warm(2, 3)
         gather(0, 1, 1, "A")
         quant(0, 0, 1)
         quant(0, 1, 1)

@@ -46,28 +46,24 @@ def tile_weighted_diis_residuals_e3_kernel(tc, g_words, g_scales, errs, pair, co
 
         e_raw, e_pair, g_code, g_plane, pair_sb = {}, {}, {}, {}, {}
 
-        def load_errs(j, rt, g0, ng):
-            t = sb([P, ng * PASS], BF16, f"e_raw{j}{rt}{g0}")
-            rows = slice(j * PASS + rt * P, j * PASS + (rt + 1) * P)
-            nc.sync.dma_start(out=t[:], in_=errs[rows, g0 * PASS : (g0 + ng) * PASS])
-            e_pair[j, rt, g0] = t[:].bitcast(F32)
-            for g in range(g0, g0 + ng):
-                e_raw[j, rt, g] = t[:].bitcast(F32)[:, (g - g0) * 2 * P : (g - g0 + 1) * 2 * P]
-
-        def load_errs_rows(j, rt0, nr, g):
-            t = sb([P, nr, PASS], BF16, f"e_rows{j}{rt0}{g}")
+        def load_errs(j, rt0, g0, ng, nr=1):
+            t = sb([P, nr, ng * PASS], BF16, f"e_raw{j}{rt0}{g0}")
             rows = slice(j * PASS + rt0 * P, j * PASS + (rt0 + nr) * P)
-            nc.sync.dma_start(out=t[:], in_=errs[rows, g * PASS : (g + 1) * PASS].rearrange("(a p) k -> p a k", p=P))
+            nc.sync.dma_start(out=t[:], in_=errs[rows, g0 * PASS : (g0 + ng) * PASS].rearrange("(a p) k -> p a k", p=P))
             for rt in range(rt0, rt0 + nr):
-                e_raw[j, rt, g] = t[:, rt - rt0, :].bitcast(F32)
+                e_pair[j, rt, g0] = t[:, rt - rt0, :].bitcast(F32)
+                for g in range(g0, g0 + ng):
+                    e_raw[j, rt, g] = e_pair[j, rt, g0][:, (g - g0) * 2 * P : (g - g0 + 1) * 2 * P]
 
-        def load_g(g, i0, ni):
-            t = sb([P, ni * P], U32, f"g_code{g}{i0}")
+        def load_g(g0, i0, ni, ng=1):
+            t = sb([P, ng, ni * P], U32, f"g_code{g0}{i0}")
             nc.sync.dma_start(
-                out=t[:].bitcast(I32), in_=g_words[g].rearrange("p n t -> p (n t)")[:, i0 * 4 * P : (i0 + ni) * 4 * P].bitcast(I32)
+                out=t[:].bitcast(I32),
+                in_=g_words[g0 : g0 + ng].rearrange("g p n t -> p g (n t)")[:, :, i0 * 4 * P : (i0 + ni) * 4 * P].bitcast(I32),
             )
-            for i in range(i0, i0 + ni):
-                g_code[i, g] = t[:, (i - i0) * P : (i - i0 + 1) * P]
+            for g in range(g0, g0 + ng):
+                for i in range(i0, i0 + ni):
+                    g_code[i, g] = t[:, g - g0, (i - i0) * P : (i - i0 + 1) * P]
 
         def clear_plane(g0, ng):
             t = sb([P, ng, M], U8, f"g_plane{g0}")
@@ -141,6 +137,22 @@ def tile_weighted_diis_residuals_e3_kernel(tc, g_words, g_scales, errs, pair, co
                 out=e_code[j, g][:, cols].bitcast(E4M3X4),
                 scales=e_plane[j, g][:, cols],
                 in_=e_quads[j, g, c][:].rearrange("p n t -> p (n t)"),
+            )
+
+        def turn_one(j, g, rt, b):
+            e_bank[j, g, "rt", rt] = bank(b, [P, 4, P])
+            for u in range(2):
+                nc.tensor.transpose(e_bank[j, g, "rt", rt][:, u, :], e_raw[j, rt, g][:, u : 2 * P : 2], ident[:])
+
+        def gather_one(j, g, rt, engine):
+            e_quads[j, g, "rt", rt] = interleave(engine, e_bank[j, g, "rt", rt], 1)
+
+        def quant_one(j, g, rt):
+            cols = slice(rt * P, (rt + 1) * P)
+            nc.vector.quantize_mx(
+                out=e_code[j, g][:, cols].bitcast(E4M3X4),
+                scales=e_plane[j, g][:, cols],
+                in_=e_quads[j, g, "rt", rt][:, :P, :].rearrange("p n t -> p (n t)"),
             )
 
         acc = {}
@@ -268,15 +280,16 @@ def tile_weighted_diis_residuals_e3_kernel(tc, g_words, g_scales, errs, pair, co
         load_scales(2, 2)
         load_g(2, 0, 6)
         load_g(3, 0, 6)
-        load_pair(0, 0, 3)
-        load_pair(0, 3, 3)
+        load_pair(0, 0, 4)
         for rt in range(4):
             load_errs(1, rt, 0, 2)
         load_g(2, 6, 2)
         load_g(3, 6, 2)
+        load_pair(0, 4, 2)
         load_pair(0, 6, 2)
-        load_coef(0)
         for rt in range(4):
+            if rt == 2:
+                load_coef(0)
             load_errs(1, rt, 2, 2)
         load_coef(1)
         load_pair(1, 0, 4)
@@ -322,20 +335,21 @@ def tile_weighted_diis_residuals_e3_kernel(tc, g_words, g_scales, errs, pair, co
         turn(0, 0, 0, 4)
         turn(0, 1, 0, 5)
         turn(0, 0, 1, 4)
-        turn(0, 1, 1, 5)
-        warm(1, 2)
         gather(0, 0, 0, "A")
+        turn(0, 1, 1, 5)
         gather(0, 1, 0, "V")
+        turn_one(0, 0, 2, 6)
+        gather_one(0, 0, 2, "A")
         quant(0, 0, 0)
-        turn(0, 0, 2, 6)
-        turn(0, 0, 3, 6)
-        gather(0, 0, 1, "A")
-        quant(0, 1, 0)
-        turn(0, 1, 2, 7)
-        turn(0, 1, 3, 7)
-        warm(2, 3)
+        turn_one(0, 0, 3, 7)
+        gather_one(0, 0, 3, "A")
+        quant_one(0, 0, 2)
+        quant_one(0, 0, 3)
+        turn(0, 1, 2, 3)
+        turn(0, 1, 3, 3)
+        warm(1, 2)
         gather(0, 1, 1, "A")
-        quant(0, 0, 1)
+        quant(0, 1, 0)
         quant(0, 1, 1)
         passes(0, range(4), (0, 1))
         for rt in range(4):
@@ -350,75 +364,81 @@ def tile_weighted_diis_residuals_e3_kernel(tc, g_words, g_scales, errs, pair, co
             for c in range(2):
                 quant(0, g, c)
 
-        for i in range(6):
+        for i in range(5):
             passes(0, [i], (2, 3))
+            if i < 4:
+                weight(0, i)
+        for rt in range(3):
+            sort_words(1, rt, 0, "A")
+        for c in range(2):
+            for g in range(2):
+                turn(1, g, 2 * c, 2 * c + g)
+                turn(1, g, 2 * c + 1, 2 * c + g)
+                gather(1, g, c, "V" if g + c == 0 else "A")
+        for i in range(5, 8):
+            passes(0, [i], (2, 3))
+        quant(1, 0, 0)
+        weight(0, 4)
+        quant(1, 0, 1)
+        quant(1, 1, 0)
+        quant(1, 1, 1)
+        for i in range(5, 8):
             weight(0, i)
-            if 2 <= i < 5:
-                sort_words(1, i - 2, 0, "A")
-        for g in range(2):
-            turn_group(1, g, 2 * g)
-            gather(1, g, 0, "A")
-            gather(1, g, 1, "VA"[g])
-        passes(0, [6], (2, 3))
-        passes(0, [7], (2, 3))
-        for g in range(2):
-            for c in range(2):
-                quant(1, g, c)
-        coef_copy(0, 0, "A")
-        coef_copy(0, 1, "A")
-        weight(0, 6)
-        weight(0, 7)
-        passes(1, range(2), (0, 1), 4)
-        h_half(0, ((0, 1), (2, 3), (4, 5), (6, 7)), range(4))
+        for rt in range(2):
+            sort_words(1, rt, 2, "A")
+        for c in range(2):
+            coef_copy(0, c, "V")
+            sort_words(1, 2 + c, 2, "V")
+        passes(1, range(2), (0, 1), 0)
+        h_half(0, ((0, 1), (2, 3), (4, 5), (6, 7)), range(2, 6))
         passes(1, range(2, 4), (0, 1), 6)
-        for rt in range(4):
-            sort_words(1, rt, 2, "V")
-        coef_quantize(0, 0)
-        coef_quantize(0, 1)
-        for q in range(3):
+        for q in range(4):
             q_half(0, (2 * q, 2 * q + 1))
         for g in (2, 3):
-            turn_group(1, g, 2 * g - 4)
+            turn_group(1, g, 2 * g - 2)
             gather(1, g, 0, "A")
             gather(1, g, 1, "VA"[g - 2])
-        passes(1, range(4, 6), (0, 1), 0)
+        passes(1, range(4, 6), (0, 1), 2)
         for g in (2, 3):
             for c in range(2):
                 quant(1, g, c)
-        q_half(0, (6, 7))
-        coef_copy(1, 0, "A")
-        coef_copy(1, 1, "A")
+        for c in range(2):
+            coef_quantize(0, c)
+            coef_copy(1, c, "A")
 
         passes(1, range(2), (2, 3))
         weight(1, 0)
         weight(1, 1)
         for i in range(2, 6):
             passes(1, [i], (2, 3))
-            weight(1, i)
-        h_half(1, ((0, 1), (2, 3)), (2, 3))
+            if i < 4:
+                weight(1, i)
+        h_half(1, ((0, 1), (2, 3)), (4, 5))
         coef_quantize(1, 0)
         coef_quantize(1, 1)
-        passes(1, [6], range(4), 4)
+        weight(1, 4)
+        passes(1, [6], range(4), 0)
         q_half(1, (0, 1))
+        weight(1, 5)
         q_half(1, (2, 3))
         weight(1, 6)
-        mix_run((0, 1), (5, 6))
-        h_half(1, ((4, 5), (6,)), (7, 0))
+        mix_run((0, 1), (1, 6))
+        h_half(1, ((4, 5), (6,)), (7, 2))
         store(0)
         store(1)
-        mix_run((2, 3), (1, 2))
-        passes(1, [7], range(4), 3)
+        mix_run((2, 3), (3, 4))
+        passes(1, [7], range(4), 5)
         q_half(1, (4, 5))
         store(2)
         q_half(1, (6,))
         store(3)
         weight(1, 7)
-        mix_run((4, 5), (4, 5))
+        mix_run((4, 5), (0, 1))
         h_half(1, ((7,),), (6,))
         store(4)
         mix_run((6,), (7,))
         store(5)
         q_half(1, (7,))
-        mix_run((7,), (0,))
+        mix_run((7,), (2,))
         store(6)
         store(7, 2)

@@ -87,6 +87,13 @@ def tile_weighted_diis_residuals_e3_kernel(tc, g_words, g_scales, errs, pair, co
             for i in range(i0, i0 + ni):
                 pair_sb[j, i] = t[:, i - i0, :]
 
+        def load_pair_rows(i0, ni):
+            t = sb([P, ni, M], BF16, f"pair_rows{i0}")
+            nc.sync.dma_start(out=t[:], in_=pair[i0 * P : (i0 + ni) * P, :].rearrange("(i p) n -> p i n", p=P))
+            for i in range(i0, i0 + ni):
+                for j in range(HALVES):
+                    pair_sb[j, i] = t[:, i - i0, j * PASS : (j + 1) * PASS]
+
         coef_raw = {}
 
         def load_coef(j):
@@ -108,6 +115,11 @@ def tile_weighted_diis_residuals_e3_kernel(tc, g_words, g_scales, errs, pair, co
             move(engine, t[:], e_pair[j, rt, g0].rearrange("p (g w u) -> p g u w", g=2, u=2))
             for g in (g0, g0 + 1):
                 sorted_words[j, rt, g] = t[:, g - g0]
+
+        def sort_one(j, rt, g, engine):
+            t = stage.tile([P, 2, P], F32, align_bytes=64, name="sorted_one", bufs=2)
+            move(engine, t[:], e_raw[j, rt, g].rearrange("p (w u) -> p u w", u=2))
+            sorted_words[j, rt, g] = t
 
         def turn(j, g, rt, b):
             if rt % 2 == 0:
@@ -142,7 +154,11 @@ def tile_weighted_diis_residuals_e3_kernel(tc, g_words, g_scales, errs, pair, co
         def turn_one(j, g, rt, b):
             e_bank[j, g, "rt", rt] = bank(b, [P, 4, P])
             for u in range(2):
-                nc.tensor.transpose(e_bank[j, g, "rt", rt][:, u, :], e_raw[j, rt, g][:, u : 2 * P : 2], ident[:])
+                if (j, rt, g) in sorted_words:
+                    word = sorted_words[j, rt, g][:, u, :]
+                else:
+                    word = e_raw[j, rt, g][:, u : 2 * P : 2]
+                nc.tensor.transpose(e_bank[j, g, "rt", rt][:, u, :], word, ident[:])
 
         def gather_one(j, g, rt, engine):
             e_quads[j, g, "rt", rt] = interleave(engine, e_bank[j, g, "rt", rt], 1)
@@ -332,32 +348,37 @@ def tile_weighted_diis_residuals_e3_kernel(tc, g_words, g_scales, errs, pair, co
             quant_h(tuple((j, i) for i in tiles))
 
         warm(3, 0)
+        for rt in range(3):
+            sort_words(0, rt, 0, "V")
         turn(0, 0, 0, 4)
         turn(0, 1, 0, 5)
         turn(0, 0, 1, 4)
         gather(0, 0, 0, "A")
         turn(0, 1, 1, 5)
-        gather(0, 1, 0, "V")
         turn_one(0, 0, 2, 6)
-        gather_one(0, 0, 2, "A")
-        quant(0, 0, 0)
         turn_one(0, 0, 3, 7)
+        sort_one(0, 3, 1, "V")
+        gather_one(0, 0, 2, "V")
+        quant(0, 0, 0)
         gather_one(0, 0, 3, "A")
         quant_one(0, 0, 2)
         quant_one(0, 0, 3)
+        gather(0, 1, 0, "A")
         turn(0, 1, 2, 3)
         turn(0, 1, 3, 3)
         warm(1, 2)
-        gather(0, 1, 1, "A")
+        gather(0, 1, 1, "V")
         quant(0, 1, 0)
         quant(0, 1, 1)
-        passes(0, range(4), (0, 1))
+        passes(0, range(4), (0,))
+        passes(0, range(2), (1,))
         for rt in range(4):
             sort_words(0, rt, 2, "V")
         for c in range(2):
             turn_pair(0, 2, c, 4 + 2 * c)
             gather(0, 2, c, "A")
             gather(0, 3, c, "V")
+        passes(0, range(2, 4), (1,))
         passes(0, range(4, 6), (0, 1), 4)
         passes(0, range(6, 8), (0, 1), 6)
         for g in (2, 3):

@@ -51,9 +51,11 @@ def tile_weighted_diis_residuals_e3_kernel(tc, g_words, g_scales, errs, pair, co
             rows = slice(j * PASS + rt0 * P, j * PASS + (rt0 + nr) * P)
             nc.sync.dma_start(out=t[:], in_=errs[rows, g0 * PASS : (g0 + ng) * PASS].rearrange("(a p) k -> p a k", p=P))
             for rt in range(rt0, rt0 + nr):
-                e_pair[j, rt, g0] = t[:, rt - rt0, :].bitcast(F32)
+                words = t[:, rt - rt0, :].bitcast(F32)
                 for g in range(g0, g0 + ng):
-                    e_raw[j, rt, g] = e_pair[j, rt, g0][:, (g - g0) * 2 * P : (g - g0 + 1) * 2 * P]
+                    e_raw[j, rt, g] = words[:, (g - g0) * 2 * P : (g - g0 + 1) * 2 * P]
+                    if g % 2 == 0:
+                        e_pair[j, rt, g] = words[:, (g - g0) * 2 * P : (g - g0 + 2) * 2 * P]
 
         def load_g(g0, i0, ni, ng=1):
             t = sb([P, ng, ni * P], U32, f"g_code{g0}{i0}")
@@ -221,7 +223,11 @@ def tile_weighted_diis_residuals_e3_kernel(tc, g_words, g_scales, errs, pair, co
 
         def coef_copy(j, c, engine):
             coef_quads[j, c] = sb([P, R // 2, 4], BF16, f"coef_quads{j}{c}")
-            move(engine, coef_quads[j, c][:], coef_raw[j][:, :, c * R // 2 : (c + 1) * R // 2].rearrange("p t n -> p n t"))
+            move(
+                engine,
+                coef_quads[j, c][:].rearrange("p (a i) t -> p a t i", i=4),
+                coef_raw[j][:, :, c * R // 2 : (c + 1) * R // 2].rearrange("p t (a i) -> p a t i", i=4),
+            )
 
         def coef_quantize(j, c):
             if c == 0:
@@ -291,16 +297,13 @@ def tile_weighted_diis_residuals_e3_kernel(tc, g_words, g_scales, errs, pair, co
         load_g(1, 0, 4)
         for rt in range(4):
             load_errs(0, rt, 2, 2)
-        load_g(0, 4, 4)
-        load_g(1, 4, 4)
+        load_g(0, 4, 4, 2)
         load_scales(2, 2)
-        load_g(2, 0, 6)
-        load_g(3, 0, 6)
+        load_g(2, 0, 6, 2)
         load_pair(0, 0, 4)
         for rt in range(4):
             load_errs(1, rt, 0, 2)
-        load_g(2, 6, 2)
-        load_g(3, 6, 2)
+        load_g(2, 6, 2, 2)
         load_pair(0, 4, 2)
         load_pair(0, 6, 2)
         for rt in range(4):
@@ -389,8 +392,8 @@ def tile_weighted_diis_residuals_e3_kernel(tc, g_words, g_scales, errs, pair, co
             passes(0, [i], (2, 3))
             if i < 4:
                 weight(0, i)
-        for rt in range(3):
-            sort_words(1, rt, 0, "A")
+        for rt in range(4):
+            sort_words(1, rt, 0, "AAAV"[rt])
         for c in range(2):
             for g in range(2):
                 turn(1, g, 2 * c, 2 * c + g)

@@ -288,17 +288,15 @@ def tile_weighted_diis_residuals_e3_kernel(tc, g_words, g_scales, errs, pair, co
 
 
         warm_tiles = warm_setup()
-        clear_plane(0, 2)
-        clear_plane(2, 2)
+        clear_plane(0, 4)
         for rt in range(4):
             load_errs(0, rt, 0, 2)
-        load_scales(0, 2)
+        load_scales(0, 4)
         load_g(0, 0, 4)
         load_g(1, 0, 4)
         for rt in range(4):
             load_errs(0, rt, 2, 2)
         load_g(0, 4, 4, 2)
-        load_scales(2, 2)
         load_g(2, 0, 6, 2)
         load_pair(0, 0, 4)
         for rt in range(4):
@@ -306,10 +304,9 @@ def tile_weighted_diis_residuals_e3_kernel(tc, g_words, g_scales, errs, pair, co
         load_g(2, 6, 2, 2)
         load_pair(0, 4, 2)
         load_pair(0, 6, 2)
-        for rt in range(4):
-            if rt == 2:
-                load_coef(0)
-            load_errs(1, rt, 2, 2)
+        load_errs(1, 0, 2, 2, 2)
+        load_errs(1, 2, 2, 2, 2)
+        load_coef(0)
         load_coef(1)
         load_pair(1, 0, 4)
         load_pair(1, 4, 4)
@@ -350,7 +347,7 @@ def tile_weighted_diis_residuals_e3_kernel(tc, g_words, g_scales, errs, pair, co
         def q_half(j, tiles):
             quant_h(tuple((j, i) for i in tiles))
 
-        warm(3, 0)
+        warm(4, 0)
         for rt in range(3):
             sort_words(0, rt, 0, "V")
         turn(0, 0, 0, 4)
@@ -369,7 +366,7 @@ def tile_weighted_diis_residuals_e3_kernel(tc, g_words, g_scales, errs, pair, co
         gather(0, 1, 0, "A")
         turn(0, 1, 2, 3)
         turn(0, 1, 3, 3)
-        warm(1, 2)
+        warm(2, 2)
         gather(0, 1, 1, "V")
         quant(0, 1, 0)
         quant(0, 1, 1)
@@ -411,12 +408,11 @@ def tile_weighted_diis_residuals_e3_kernel(tc, g_words, g_scales, errs, pair, co
         for rt in range(2):
             sort_words(1, rt, 2, "A")
         for c in range(2):
-            coef_copy(0, c, "V")
             sort_words(1, 2 + c, 2, "V")
         passes(1, range(2), (0, 1), 0)
-        h_half(0, ((0, 1), (2, 3), (4, 5), (6, 7)), range(2, 6))
+        h_half(0, ((0, 1), (2, 3), (4, 5)), range(2, 5))
         passes(1, range(2, 4), (0, 1), 6)
-        for q in range(4):
+        for q in range(3):
             q_half(0, (2 * q, 2 * q + 1))
         for g in (2, 3):
             turn_group(1, g, 2 * g - 2)
@@ -426,9 +422,10 @@ def tile_weighted_diis_residuals_e3_kernel(tc, g_words, g_scales, errs, pair, co
         for g in (2, 3):
             for c in range(2):
                 quant(1, g, c)
-        for c in range(2):
-            coef_quantize(0, c)
-            coef_copy(1, c, "A")
+        for j in range(2):
+            for c in range(2):
+                coef_copy(j, c, "A")
+        coef_quantize(0, 0)
 
         passes(1, range(2), (2, 3))
         weight(1, 0)
@@ -438,6 +435,8 @@ def tile_weighted_diis_residuals_e3_kernel(tc, g_words, g_scales, errs, pair, co
             if i < 4:
                 weight(1, i)
         h_half(1, ((0, 1), (2, 3)), (4, 5))
+        h_half(0, ((6, 7),), (1,))
+        coef_quantize(0, 1)
         coef_quantize(1, 0)
         coef_quantize(1, 1)
         weight(1, 4)
@@ -446,10 +445,11 @@ def tile_weighted_diis_residuals_e3_kernel(tc, g_words, g_scales, errs, pair, co
         weight(1, 5)
         q_half(1, (2, 3))
         weight(1, 6)
-        mix_run((0, 1), (1, 6))
+        mix_run((0, 1), (6, 1))
         h_half(1, ((4, 5), (6,)), (7, 2))
         store(0)
         store(1)
+        q_half(0, (6, 7))
         mix_run((2, 3), (3, 4))
         passes(1, [7], range(4), 5)
         q_half(1, (4, 5))

@@ -288,15 +288,17 @@ def tile_weighted_diis_residuals_e3_kernel(tc, g_words, g_scales, errs, pair, co
 
 
         warm_tiles = warm_setup()
-        clear_plane(0, 4)
+        clear_plane(0, 2)
+        clear_plane(2, 2)
         for rt in range(4):
             load_errs(0, rt, 0, 2)
-        load_scales(0, 4)
+        load_scales(0, 2)
         load_g(0, 0, 4)
         load_g(1, 0, 4)
         for rt in range(4):
             load_errs(0, rt, 2, 2)
         load_g(0, 4, 4, 2)
+        load_scales(2, 2)
         load_g(2, 0, 6, 2)
         load_pair(0, 0, 4)
         for rt in range(4):
@@ -366,7 +368,7 @@ def tile_weighted_diis_residuals_e3_kernel(tc, g_words, g_scales, errs, pair, co
         gather(0, 1, 0, "A")
         turn(0, 1, 2, 3)
         turn(0, 1, 3, 3)
-        warm(2, 2)
+        warm(1, 2)
         gather(0, 1, 1, "V")
         quant(0, 1, 0)
         quant(0, 1, 1)

@@ -20,451 +20,372 @@ P = 128
 PASS = 512
 GROUPS = K // PASS
 HALVES = M // PASS
-TILES = M // P
-BLOCKS = PASS // P
+ROW_TILES = PASS // P
+STAGING = 8
+VECTOR, SCALAR = "vector", "scalar"
 
 
 def tile_weighted_diis_residuals_e3_kernel(tc, g_words, g_scales, errs, pair, coef, lam, out):
     nc = tc.nc
     with ExitStack() as ctx:
         keep = ctx.enter_context(tc.tile_pool(name="keep", bufs=1))
-        stage = ctx.enter_context(tc.tile_pool(name="stage", bufs=4))
+        stage = ctx.enter_context(tc.tile_pool(name="stage", bufs=STAGING))
         psum = ctx.enter_context(tc.psum_pool(name="psum", bufs=1))
         ctx.enter_context(tc.manual_schedule())
 
         def sb(shape, dtype, name):
             return keep.tile(shape, dtype, align_bytes=64, name=name)
 
+        def bank(b, shape):
+            return psum.tile(shape, F32, name=f"bank{b}", tag=f"bank{b}")
+
         def move(engine, dst, src):
-            if engine == "V":
+            if engine == VECTOR:
                 nc.vector.tensor_copy(out=dst, in_=src)
             else:
                 nc.scalar.copy(out=dst, in_=src)
 
+        def mx_pass(acc, stationary, stationary_plane, moving, moving_plane, start, stop):
+            nc.tensor.matmul_mx(
+                out=acc,
+                lhsT=stationary.bitcast(E5M2X4),
+                lhsT_scale=stationary_plane,
+                rhs=moving.bitcast(E4M3X4),
+                rhs_scale=moving_plane,
+                start=start,
+                stop=stop,
+            )
+
         ident = sb([P, P], F32, "ident")
         make_identity(nc, ident[:])
+        lam_sb = sb([P, R], BF16, "lam_sb")
 
-        e_raw, e_pair, g_code, g_plane, pair_sb = {}, {}, {}, {}, {}
+        quarter_words, g_code, g_plane, pair_sb, coef_raw = {}, {}, {}, {}, {}
 
-        def load_errs(j, rt0, g0, ng, nr=1):
-            t = sb([P, nr, ng * PASS], BF16, f"e_raw{j}{rt0}{g0}")
-            rows = slice(j * PASS + rt0 * P, j * PASS + (rt0 + nr) * P)
-            nc.sync.dma_start(out=t[:], in_=errs[rows, g0 * PASS : (g0 + ng) * PASS].rearrange("(a p) k -> p a k", p=P))
-            for rt in range(rt0, rt0 + nr):
-                words = t[:, rt - rt0, :].bitcast(F32)
-                for g in range(g0, g0 + ng):
-                    e_raw[j, rt, g] = words[:, (g - g0) * 2 * P : (g - g0 + 1) * 2 * P]
-                    if g % 2 == 0:
-                        e_pair[j, rt, g] = words[:, (g - g0) * 2 * P : (g - g0 + 2) * 2 * P]
+        def load_errs(j, g0, rt0, count=1):
+            t = sb([P, count, 2 * PASS], BF16, f"errs{j}{rt0}{g0}")
+            rows = slice(j * PASS + rt0 * P, j * PASS + (rt0 + count) * P)
+            nc.sync.dma_start(out=t[:], in_=errs[rows, g0 * PASS : (g0 + 2) * PASS].rearrange("(a p) k -> p a k", p=P))
+            for a in range(count):
+                quarter_words[j, rt0 + a, g0] = t[:, a, :].bitcast(F32)
 
-        def load_g(g0, i0, ni, ng=1):
-            t = sb([P, ng, ni * P], U32, f"g_code{g0}{i0}")
-            nc.sync.dma_start(
-                out=t[:].bitcast(I32),
-                in_=g_words[g0 : g0 + ng].rearrange("g p n t -> p g (n t)")[:, :, i0 * 4 * P : (i0 + ni) * 4 * P].bitcast(I32),
-            )
-            for g in range(g0, g0 + ng):
-                for i in range(i0, i0 + ni):
-                    g_code[i, g] = t[:, g - g0, (i - i0) * P : (i - i0 + 1) * P]
+        def load_g(groups, tiles):
+            t = sb([P, len(groups), len(tiles) * P], U32, f"g_code{groups[0]}{tiles[0]}")
+            as_bytes = g_words[groups.start : groups.stop].rearrange("g p n t -> p g (n t)")
+            nc.sync.dma_start(out=t[:].bitcast(I32), in_=as_bytes[:, :, tiles.start * 4 * P : tiles.stop * 4 * P].bitcast(I32))
+            for a, g in enumerate(groups):
+                for b, i in enumerate(tiles):
+                    g_code[i, g] = t[:, a, b * P : (b + 1) * P]
 
-        def clear_plane(g0, ng):
-            t = sb([P, ng, M], U8, f"g_plane{g0}")
+        def clear_planes(g0):
+            t = sb([P, 2, M], U8, f"g_plane{g0}")
             nc.vector.memset(t[:].bitcast(I32), 0)
-            for g in range(g0, g0 + ng):
-                g_plane[g] = (t, g0)
+            g_plane[g0] = t
 
-        def load_scales(g0, ng, queue=nc.sync):
-            t = g_plane[g0][0]
+        def load_scales(g0):
             for r in range(4):
-                queue.dma_start(
-                    out=t[r:P:32, :, :].bitcast(I32),
-                    in_=g_scales[g0 : g0 + ng, r:16:4, :].rearrange("g q n -> q g n").bitcast(I32),
+                nc.sync.dma_start(
+                    out=g_plane[g0][r:P:32, :, :].bitcast(I32),
+                    in_=g_scales[g0 : g0 + 2, r:16:4, :].rearrange("g q n -> q g n").bitcast(I32),
                 )
 
-        def load_pair(j, i0, ni):
-            t = sb([P, ni, PASS], BF16, f"pair{j}{i0}")
-            nc.sync.dma_start(
-                out=t[:], in_=pair[i0 * P : (i0 + ni) * P, j * PASS : (j + 1) * PASS].rearrange("(i p) n -> p i n", p=P)
-            )
-            for i in range(i0, i0 + ni):
-                pair_sb[j, i] = t[:, i - i0, :]
-
-        def load_pair_rows(i0, ni):
-            t = sb([P, ni, M], BF16, f"pair_rows{i0}")
-            nc.sync.dma_start(out=t[:], in_=pair[i0 * P : (i0 + ni) * P, :].rearrange("(i p) n -> p i n", p=P))
-            for i in range(i0, i0 + ni):
-                for j in range(HALVES):
-                    pair_sb[j, i] = t[:, i - i0, j * PASS : (j + 1) * PASS]
-
-        coef_raw = {}
+        def load_pair(j, tiles):
+            t = sb([P, len(tiles), PASS], BF16, f"pair{j}{tiles[0]}")
+            piece = pair[tiles.start * P : tiles.stop * P, j * PASS : (j + 1) * PASS]
+            nc.sync.dma_start(out=t[:], in_=piece.rearrange("(i p) n -> p i n", p=P))
+            for a, i in enumerate(tiles):
+                pair_sb[j, i] = t[:, a, :]
 
         def load_coef(j):
             coef_raw[j] = sb([P, 4, R], BF16, f"coef_raw{j}")
             nc.sync.dma_start(out=coef_raw[j][:], in_=coef[j * PASS : (j + 1) * PASS, :].rearrange("(p t) r -> p t r", t=4))
 
-        lam_sb = sb([P, R], BF16, "lam_sb")
+        sorted_words, errs_bank, errs_quads, errs_code, errs_plane = {}, {}, {}, {}, {}
 
-        def load_lam():
-            nc.sync.dma_start(out=lam_sb[:], in_=lam.partition_broadcast(P))
+        def group_words(j, rt, g):
+            return quarter_words[j, rt, g - g % 2][:, (g % 2) * 2 * P : (g % 2 + 1) * 2 * P]
 
-        def bank(b, shape):
-            return psum.tile(shape, F32, name=f"bank{b}", tag=f"bank{b}")
+        def sort_quarter(j, rt, g0, engine):
+            t = stage.tile([P, 2, 2, P], F32, align_bytes=64, name="sorted")
+            move(engine, t[:], quarter_words[j, rt, g0].rearrange("p (g w u) -> p g u w", g=2, u=2))
+            for a in range(2):
+                sorted_words[j, rt, g0 + a] = t[:, a]
 
-        sorted_words, e_bank, e_quads, e_code, e_plane = {}, {}, {}, {}, {}
-
-        def sort_words(j, rt, g0, engine):
-            t = stage.tile([P, 2, 2, P], F32, align_bytes=64, name="sorted", bufs=8)
-            move(engine, t[:], e_pair[j, rt, g0].rearrange("p (g w u) -> p g u w", g=2, u=2))
-            for g in (g0, g0 + 1):
-                sorted_words[j, rt, g] = t[:, g - g0]
-
-        def sort_one(j, rt, g, engine):
-            t = stage.tile([P, 2, P], F32, align_bytes=64, name="sorted_one", bufs=2)
-            move(engine, t[:], e_raw[j, rt, g].rearrange("p (w u) -> p u w", u=2))
+        def sort_group(j, rt, g, engine):
+            t = stage.tile([P, 2, P], F32, align_bytes=64, name="sorted_group", bufs=2)
+            move(engine, t[:], group_words(j, rt, g).rearrange("p (w u) -> p u w", u=2))
             sorted_words[j, rt, g] = t
 
-        def turn(j, g, rt, b):
-            if rt % 2 == 0:
-                e_bank[j, g, rt // 2] = bank(b, [P, 4, P])
+        def turn(j, g, rt, rts, b):
+            if rt == rts[0]:
+                errs_bank[j, g, rts] = bank(b, [P, 4, P])
             for u in range(2):
                 if (j, rt, g) in sorted_words:
-                    word = sorted_words[j, rt, g][:, u, :]
+                    words = sorted_words[j, rt, g][:, u, :]
                 else:
-                    word = e_raw[j, rt, g][:, u : 2 * P : 2]
-                nc.tensor.transpose(e_bank[j, g, rt // 2][:, 2 * (rt % 2) + u, :], word, ident[:])
+                    words = group_words(j, rt, g)[:, u : 2 * P : 2]
+                nc.tensor.transpose(errs_bank[j, g, rts][:, 2 * (rt - rts[0]) + u, :], words, ident[:])
 
-        def interleave(engine, src, n):
-            t = stage.tile([P, 2 * P, 4], BF16, align_bytes=64, name="quads", bufs=8)
-            words = t[:].rearrange("p n t -> p (n t)").bitcast(F32)[:, : 2 * n * P]
-            move(engine, words.rearrange("p (b r u) -> p b r u", b=n, u=2), src[:, : 2 * n, :].rearrange("p (b u) r -> p b r u", u=2))
-            return t
-
-        def gather(j, g, c, engine):
-            e_quads[j, g, c] = interleave(engine, e_bank[j, g, c], 2)
-
-        def quant(j, g, c):
-            if c == 0:
-                e_code[j, g] = sb([P, PASS], U32, f"e_code{j}{g}")
-                e_plane[j, g] = sb([P, PASS], U8, f"e_plane{j}{g}")
-            cols = slice(2 * c * P, 2 * (c + 1) * P)
-            nc.vector.quantize_mx(
-                out=e_code[j, g][:, cols].bitcast(E4M3X4),
-                scales=e_plane[j, g][:, cols],
-                in_=e_quads[j, g, c][:].rearrange("p n t -> p (n t)"),
+        def gathered(engine, source, count):
+            t = stage.tile([P, 2 * P, 4], BF16, align_bytes=64, name="quads")
+            words = t[:].rearrange("p n t -> p (n t)").bitcast(F32)[:, : 2 * count * P]
+            move(
+                engine,
+                words.rearrange("p (b r u) -> p b r u", b=count, u=2),
+                source[:, : 2 * count, :].rearrange("p (b u) r -> p b r u", u=2),
             )
+            return t[:, : count * P, :].rearrange("p n t -> p (n t)")
 
-        def turn_one(j, g, rt, b):
-            e_bank[j, g, "rt", rt] = bank(b, [P, 4, P])
-            for u in range(2):
-                if (j, rt, g) in sorted_words:
-                    word = sorted_words[j, rt, g][:, u, :]
-                else:
-                    word = e_raw[j, rt, g][:, u : 2 * P : 2]
-                nc.tensor.transpose(e_bank[j, g, "rt", rt][:, u, :], word, ident[:])
+        def gather(j, g, rts, engine):
+            errs_quads[j, g, rts] = gathered(engine, errs_bank[j, g, rts], len(rts))
 
-        def gather_one(j, g, rt, engine):
-            e_quads[j, g, "rt", rt] = interleave(engine, e_bank[j, g, "rt", rt], 1)
+        def quantise(j, g, rts):
+            if rts[0] == 0:
+                errs_code[j, g] = sb([P, PASS], U32, f"errs_code{j}{g}")
+                errs_plane[j, g] = sb([P, PASS], U8, f"errs_plane{j}{g}")
+            cols = slice(rts[0] * P, (rts[-1] + 1) * P)
+            nc.vector.quantize_mx(out=errs_code[j, g][:, cols].bitcast(E4M3X4), scales=errs_plane[j, g][:, cols], in_=errs_quads[j, g, rts])
 
-        def quant_one(j, g, rt):
-            cols = slice(rt * P, (rt + 1) * P)
-            nc.vector.quantize_mx(
-                out=e_code[j, g][:, cols].bitcast(E4M3X4),
-                scales=e_plane[j, g][:, cols],
-                in_=e_quads[j, g, "rt", rt][:, :P, :].rearrange("p n t -> p (n t)"),
-            )
+        b_acc, h_sb, h_quads, h_code = {}, {}, {}, {}
 
-        acc = {}
+        def overlaps(j, tiles, groups, first_bank=0):
+            for g in groups:
+                for a, i in enumerate(tiles):
+                    if g == 0:
+                        b_acc[j, i] = bank(first_bank + a, [P, PASS])
+                    plane = g_plane[g - g % 2][:, g % 2, i * P : (i + 1) * P]
+                    mx_pass(b_acc[j, i][:], g_code[i, g], plane, errs_code[j, g][:], errs_plane[j, g][:], g == 0, g == GROUPS - 1)
 
-        def overlap(j, i, g, b=None):
-            if g == 0:
-                acc[j, i] = bank(b, [P, PASS])
-            t, g0 = g_plane[g]
-            nc.tensor.matmul_mx(
-                out=acc[j, i][:],
-                lhsT=g_code[i, g].bitcast(E5M2X4),
-                lhsT_scale=t[:, g - g0, i * P : (i + 1) * P],
-                rhs=e_code[j, g][:].bitcast(E4M3X4),
-                rhs_scale=e_plane[j, g][:],
-                start=(g == 0),
-                stop=(g == GROUPS - 1),
-            )
-
-        h_sb, h_bank, h_quads, h_code = {}, {}, {}, {}
-
-        def weight(j, i):
+        def weigh(j, i):
             h_sb[j, i] = sb([P, PASS], BF16, f"h{j}{i}")
             nc.vector.tensor_tensor(
                 out=h_sb[j, i][:].rearrange("p (u w e) -> p u w e", u=2, e=2),
-                in0=acc[j, i][:].rearrange("p (w u e) -> p u w e", u=2, e=2),
+                in0=b_acc[j, i][:].rearrange("p (w u e) -> p u w e", u=2, e=2),
                 in1=pair_sb[j, i].rearrange("p (w u e) -> p u w e", u=2, e=2),
                 op=ALU.mult,
             )
 
-        def turn_h(units, b):
-            h_bank[units] = bank(b, [P, 4, P])
-            for a, unit in enumerate(units):
-                words = h_sb[unit][:].bitcast(F32)
+        def turn_h(j, tiles, b):
+            t = bank(b, [P, 4, P])
+            for a, i in enumerate(tiles):
+                words = h_sb[j, i][:].bitcast(F32)
                 for u in range(2):
-                    nc.tensor.transpose(h_bank[units][:, 2 * a + u, :], words[:, u * P : (u + 1) * P], ident[:])
+                    nc.tensor.transpose(t[:, 2 * a + u, :], words[:, u * P : (u + 1) * P], ident[:])
+            h_quads[j, tiles] = gathered(SCALAR, t, len(tiles))
 
-        def gather_h(units, engine):
-            h_quads[units] = interleave(engine, h_bank[units], len(units))
+        def quantise_h(j, tiles):
+            code = sb([P, len(tiles) * P], U32, f"h_code{j}{tiles[0]}")
+            plane = sb([P, len(tiles) * P], U8, f"h_plane{j}{tiles[0]}")
+            nc.vector.quantize_mx(out=code[:].bitcast(E5M2X4), scales=plane[:], in_=h_quads[j, tiles])
+            for a, i in enumerate(tiles):
+                h_code[j, i] = (code[:, a * P : (a + 1) * P], plane[:, a * P : (a + 1) * P])
 
-        def quant_h(units):
-            n = len(units) * P
-            name = "".join(f"{j}{i}" for j, i in units)
-            code = sb([P, n], U32, "h_code" + name)
-            plane = sb([P, n], U8, "h_plane" + name)
-            nc.vector.quantize_mx(out=code[:].bitcast(E5M2X4), scales=plane[:], in_=h_quads[units][:, :n, :].rearrange("p n t -> p (n t)"))
-            for a, unit in enumerate(units):
-                h_code[unit] = (code[:, a * P : (a + 1) * P], plane[:, a * P : (a + 1) * P])
+        coef_quads, coef_code, coef_plane, out_acc = {}, {}, {}, {}
 
-        coef_quads, coef_code, coef_plane = {}, {}, {}
-
-        def coef_copy(j, c, engine):
+        def interleave_coef(j, c):
             coef_quads[j, c] = sb([P, R // 2, 4], BF16, f"coef_quads{j}{c}")
             move(
-                engine,
+                SCALAR,
                 coef_quads[j, c][:].rearrange("p (a i) t -> p a t i", i=4),
                 coef_raw[j][:, :, c * R // 2 : (c + 1) * R // 2].rearrange("p t (a i) -> p a t i", i=4),
             )
 
-        def coef_quantize(j, c):
+        def quantise_coef(j, c):
             if c == 0:
                 coef_code[j] = sb([P, R], U32, f"coef_code{j}")
                 coef_plane[j] = sb([P, R], U8, f"coef_plane{j}")
             cols = slice(c * R // 2, (c + 1) * R // 2)
             nc.vector.quantize_mx(
-                out=coef_code[j][:, cols].bitcast(E4M3X4), scales=coef_plane[j][:, cols], in_=coef_quads[j, c][:].rearrange("p n t -> p (n t)")
+                out=coef_code[j][:, cols].bitcast(E4M3X4),
+                scales=coef_plane[j][:, cols],
+                in_=coef_quads[j, c][:].rearrange("p n t -> p (n t)"),
             )
 
-        res_acc = {}
-
-        def mix(i, j, b=None):
-            if j == 0:
-                res_acc[i] = bank(b, [P, R])
-            code, plane = h_code[j, i]
-            nc.tensor.matmul_mx(
-                out=res_acc[i][:],
-                lhsT=code.bitcast(E5M2X4),
-                lhsT_scale=plane,
-                rhs=coef_code[j][:].bitcast(E4M3X4),
-                rhs_scale=coef_plane[j][:],
-                start=(j == 0),
-                stop=(j == HALVES - 1),
-            )
+        def mix(i, b):
+            out_acc[i] = bank(b, [P, R])
+            for j in range(HALVES):
+                code, plane = h_code[j, i]
+                mx_pass(out_acc[i][:], code, plane, coef_code[j][:], coef_plane[j][:], j == 0, j == HALVES - 1)
 
         def store(i, parts=1):
             for c in range(parts):
                 cols = slice(c * R // parts, (c + 1) * R // parts)
                 res = sb([P, R // parts], F32, f"res{i}{c}")
-                nc.vector.tensor_tensor(out=res[:], in0=res_acc[i][:, cols], in1=lam_sb[:, cols], op=ALU.subtract)
+                nc.vector.tensor_tensor(out=res[:], in0=out_acc[i][:, cols], in1=lam_sb[:, cols], op=ALU.subtract)
                 nc.sync.dma_start(out=out[i * P : (i + 1) * P, cols], in_=res[:])
 
+        zero_words = 64
+        blank = sb([P, zero_words + (P + PASS) + (P + PASS) // 4], U32, "blank")
+        nc.vector.memset(blank[:], 0)
+        zeros = blank[:, :zero_words].bitcast(BF16)
+        warm_code = blank[:, zero_words : zero_words + P + PASS]
+        warm_plane = blank[:, zero_words + P + PASS :].bitcast(U8)
+        for first, fmt in ((0, E5M2X4), (P, E4M3X4)):
+            cols = slice(first, first + zero_words // 2)
+            nc.vector.quantize_mx(out=warm_code[:, cols].bitcast(fmt), scales=warm_plane[:, cols], in_=zeros)
 
-        def warm_setup():
-            blank = sb([P, 864], U32, "blank")
-            nc.vector.memset(blank[:], 0)
-            zero = blank[:, :64].bitcast(BF16)
-            codes = blank[:, 64:704]
-            planes = blank[:, 704:].bitcast(U8)
-            nc.vector.quantize_mx(out=codes[:, :32].bitcast(E5M2X4), scales=planes[:, :32], in_=zero)
-            nc.vector.quantize_mx(out=codes[:, P : P + 32].bitcast(E4M3X4), scales=planes[:, P : P + 32], in_=zero)
-            return codes, planes
-
-        def warm(n, b):
-            codes, planes = warm_tiles
+        def warm_up(count, b):
             t = bank(b, [P, PASS])
-            for w in range(n):
-                nc.tensor.matmul_mx(
-                    out=t[:],
-                    lhsT=codes[:, :P].bitcast(E5M2X4),
-                    lhsT_scale=planes[:, :P],
-                    rhs=codes[:, P:].bitcast(E4M3X4),
-                    rhs_scale=planes[:, P:],
-                    start=True,
-                    stop=True,
-                )
+            for n in range(count):
+                mx_pass(t[:], warm_code[:, :P], warm_plane[:, :P], warm_code[:, P:], warm_plane[:, P:], True, True)
 
-
-        warm_tiles = warm_setup()
-        clear_plane(0, 2)
-        clear_plane(2, 2)
-        for rt in range(4):
-            load_errs(0, rt, 0, 2)
-        load_scales(0, 2)
-        load_g(0, 0, 4)
-        load_g(1, 0, 4)
-        for rt in range(4):
-            load_errs(0, rt, 2, 2)
-        load_g(0, 4, 4, 2)
-        load_scales(2, 2)
-        load_g(2, 0, 6, 2)
-        load_pair(0, 0, 4)
-        for rt in range(4):
-            load_errs(1, rt, 0, 2)
-        load_g(2, 6, 2, 2)
-        load_pair(0, 4, 2)
-        load_pair(0, 6, 2)
-        load_errs(1, 0, 2, 2, 2)
-        load_errs(1, 2, 2, 2, 2)
+        clear_planes(0)
+        clear_planes(2)
+        for rt in range(ROW_TILES):
+            load_errs(0, 0, rt)
+        load_scales(0)
+        load_g(range(0, 1), range(0, 4))
+        load_g(range(1, 2), range(0, 4))
+        for rt in range(ROW_TILES):
+            load_errs(0, 2, rt)
+        load_g(range(0, 2), range(4, 8))
+        load_scales(2)
+        load_g(range(2, 4), range(0, 6))
+        load_pair(0, range(0, 4))
+        for rt in range(ROW_TILES):
+            load_errs(1, 0, rt)
+        load_g(range(2, 4), range(6, 8))
+        load_pair(0, range(4, 6))
+        load_pair(0, range(6, 8))
+        load_errs(1, 2, 0, 2)
+        load_errs(1, 2, 2, 2)
         load_coef(0)
         load_coef(1)
-        load_pair(1, 0, 4)
-        load_pair(1, 4, 4)
-        load_lam()
+        load_pair(1, range(0, 4))
+        load_pair(1, range(4, 8))
+        nc.sync.dma_start(out=lam_sb[:], in_=lam.partition_broadcast(P))
 
-        def turn_pair(j, g0, c, b0):
-            for rt in (2 * c, 2 * c + 1):
-                for g in (g0, g0 + 1):
-                    turn(j, g, rt, b0 + g - g0)
+        front, back = (0, 1), (2, 3)
 
-        def passes(j, tiles, groups, b0=0):
-            for g in groups:
-                for i in tiles:
-                    overlap(j, i, g, b0 + i - tiles[0])
-
-        def both(i):
-            return ((0, i), (1, i))
-
-        def h_run(tiles, banks):
-            for i, b in zip(tiles, banks):
-                turn_h(both(i), b)
-                gather_h(both(i), "A")
-
-        def mix_run(tiles, banks):
-            for i, b in zip(tiles, banks):
-                mix(i, 0, b)
-                mix(i, 1)
-
-        def turn_group(j, g, b0):
-            for rt in range(4):
-                turn(j, g, rt, b0 + rt // 2)
-
-        def h_half(j, units, banks, engines="AAAA"):
-            for tiles, b, e in zip(units, banks, engines):
-                turn_h(tuple((j, i) for i in tiles), b)
-                gather_h(tuple((j, i) for i in tiles), e)
-
-        def q_half(j, tiles):
-            quant_h(tuple((j, i) for i in tiles))
-
-        warm(4, 0)
+        warm_up(4, 0)
         for rt in range(3):
-            sort_words(0, rt, 0, "V")
-        turn(0, 0, 0, 4)
-        turn(0, 1, 0, 5)
-        turn(0, 0, 1, 4)
-        gather(0, 0, 0, "A")
-        turn(0, 1, 1, 5)
-        turn_one(0, 0, 2, 6)
-        turn_one(0, 0, 3, 7)
-        sort_one(0, 3, 1, "V")
-        gather_one(0, 0, 2, "V")
-        quant(0, 0, 0)
-        gather_one(0, 0, 3, "A")
-        quant_one(0, 0, 2)
-        quant_one(0, 0, 3)
-        gather(0, 1, 0, "A")
-        turn(0, 1, 2, 3)
-        turn(0, 1, 3, 3)
-        warm(1, 2)
-        gather(0, 1, 1, "V")
-        quant(0, 1, 0)
-        quant(0, 1, 1)
-        passes(0, range(4), (0,))
-        passes(0, range(2), (1,))
-        for rt in range(4):
-            sort_words(0, rt, 2, "V")
-        for c in range(2):
-            turn_pair(0, 2, c, 4 + 2 * c)
-            gather(0, 2, c, "A")
-            gather(0, 3, c, "V")
-        passes(0, range(2, 4), (1,))
-        passes(0, range(4, 6), (0, 1), 4)
-        passes(0, range(6, 8), (0, 1), 6)
-        for g in (2, 3):
-            for c in range(2):
-                quant(0, g, c)
+            sort_quarter(0, rt, 0, VECTOR)
+        turn(0, 0, 0, front, 4)
+        turn(0, 1, 0, front, 5)
+        turn(0, 0, 1, front, 4)
+        gather(0, 0, front, SCALAR)
+        turn(0, 1, 1, front, 5)
+        turn(0, 0, 2, (2,), 6)
+        turn(0, 0, 3, (3,), 7)
+        sort_group(0, 3, 1, VECTOR)
+        gather(0, 0, (2,), VECTOR)
+        quantise(0, 0, front)
+        gather(0, 0, (3,), SCALAR)
+        quantise(0, 0, (2,))
+        quantise(0, 0, (3,))
+        gather(0, 1, front, SCALAR)
+        turn(0, 1, 2, back, 3)
+        turn(0, 1, 3, back, 3)
+        warm_up(1, 2)
+        gather(0, 1, back, VECTOR)
+        quantise(0, 1, front)
+        quantise(0, 1, back)
 
-        for i in range(5):
-            passes(0, [i], (2, 3))
+        held = 2
+        overlaps(0, range(0, 4), [0])
+        overlaps(0, range(0, held), [1])
+        for rt in range(ROW_TILES):
+            sort_quarter(0, rt, 2, VECTOR)
+        for c, rts in enumerate((front, back)):
+            for rt in rts:
+                turn(0, 2, rt, rts, 4 + 2 * c)
+                turn(0, 3, rt, rts, 5 + 2 * c)
+            gather(0, 2, rts, SCALAR)
+            gather(0, 3, rts, VECTOR)
+        overlaps(0, range(held, 4), [1])
+        overlaps(0, range(4, 6), [0, 1], 4)
+        overlaps(0, range(6, 8), [0, 1], 6)
+        for g in (2, 3):
+            quantise(0, g, front)
+            quantise(0, g, back)
+
+        cover = 5
+        for i in range(cover):
+            overlaps(0, [i], [2, 3])
             if i < 4:
-                weight(0, i)
-        for rt in range(4):
-            sort_words(1, rt, 0, "AAAV"[rt])
-        for c in range(2):
-            for g in range(2):
-                turn(1, g, 2 * c, 2 * c + g)
-                turn(1, g, 2 * c + 1, 2 * c + g)
-                gather(1, g, c, "V" if g + c == 0 else "A")
+                weigh(0, i)
+        for rt in range(3):
+            sort_quarter(1, rt, 0, SCALAR)
+        sort_group(1, 3, 1, VECTOR)
+        for c, rts in enumerate((front, back)):
+            for g in (0, 1):
+                for rt in rts:
+                    turn(1, g, rt, rts, 2 * c + g)
+                gather(1, g, rts, VECTOR if g + c == 0 else SCALAR)
+        for i in range(cover, 8):
+            overlaps(0, [i], [2, 3])
+        quantise(1, 0, front)
+        weigh(0, 4)
+        quantise(1, 0, back)
+        quantise(1, 1, front)
+        quantise(1, 1, back)
         for i in range(5, 8):
-            passes(0, [i], (2, 3))
-        quant(1, 0, 0)
-        weight(0, 4)
-        quant(1, 0, 1)
-        quant(1, 1, 0)
-        quant(1, 1, 1)
-        for i in range(5, 8):
-            weight(0, i)
-        for rt in range(2):
-            sort_words(1, rt, 2, "A")
-        for c in range(2):
-            sort_words(1, 2 + c, 2, "V")
-        passes(1, range(2), (0, 1), 0)
-        h_half(0, ((0, 1), (2, 3), (4, 5)), range(2, 5))
-        passes(1, range(2, 4), (0, 1), 6)
+            weigh(0, i)
+
+        for rt in range(ROW_TILES):
+            sort_quarter(1, rt, 2, SCALAR if rt < 2 else VECTOR)
+        overlaps(1, range(0, 2), [0, 1], 0)
         for q in range(3):
-            q_half(0, (2 * q, 2 * q + 1))
+            turn_h(0, (2 * q, 2 * q + 1), 2 + q)
+        overlaps(1, range(2, 4), [0, 1], 6)
+        for q in range(3):
+            quantise_h(0, (2 * q, 2 * q + 1))
         for g in (2, 3):
-            turn_group(1, g, 2 * g - 2)
-            gather(1, g, 0, "A")
-            gather(1, g, 1, "VA"[g - 2])
-        passes(1, range(4, 6), (0, 1), 2)
+            for c, rts in enumerate((front, back)):
+                for rt in rts:
+                    turn(1, g, rt, rts, 2 * g - 2 + c)
+            gather(1, g, front, SCALAR)
+            gather(1, g, back, VECTOR if g == 2 else SCALAR)
+        overlaps(1, range(4, 6), [0, 1], 2)
         for g in (2, 3):
-            for c in range(2):
-                quant(1, g, c)
-        for j in range(2):
-            for c in range(2):
-                coef_copy(j, c, "A")
-        coef_quantize(0, 0)
+            quantise(1, g, front)
+            quantise(1, g, back)
+        for j in range(HALVES):
+            interleave_coef(j, 0)
+            interleave_coef(j, 1)
+        quantise_coef(0, 0)
 
-        passes(1, range(2), (2, 3))
-        weight(1, 0)
-        weight(1, 1)
+        overlaps(1, range(0, 2), [2, 3])
+        weigh(1, 0)
+        weigh(1, 1)
         for i in range(2, 6):
-            passes(1, [i], (2, 3))
+            overlaps(1, [i], [2, 3])
             if i < 4:
-                weight(1, i)
-        h_half(1, ((0, 1), (2, 3)), (4, 5))
-        h_half(0, ((6, 7),), (1,))
-        coef_quantize(0, 1)
-        coef_quantize(1, 0)
-        coef_quantize(1, 1)
-        weight(1, 4)
-        passes(1, [6], range(4), 0)
-        q_half(1, (0, 1))
-        weight(1, 5)
-        q_half(1, (2, 3))
-        weight(1, 6)
-        mix_run((0, 1), (6, 1))
-        h_half(1, ((4, 5), (6,)), (7, 2))
+                weigh(1, i)
+        turn_h(1, (0, 1), 4)
+        turn_h(1, (2, 3), 5)
+        turn_h(0, (6, 7), 1)
+        quantise_coef(0, 1)
+        quantise_coef(1, 0)
+        quantise_coef(1, 1)
+        weigh(1, 4)
+        overlaps(1, [6], range(GROUPS), 0)
+        quantise_h(1, (0, 1))
+        weigh(1, 5)
+        quantise_h(1, (2, 3))
+        weigh(1, 6)
+        mix(0, 6)
+        mix(1, 1)
+        turn_h(1, (4, 5), 7)
+        turn_h(1, (6,), 2)
         store(0)
         store(1)
-        q_half(0, (6, 7))
-        mix_run((2, 3), (3, 4))
-        passes(1, [7], range(4), 5)
-        q_half(1, (4, 5))
+        quantise_h(0, (6, 7))
+        mix(2, 3)
+        mix(3, 4)
+        overlaps(1, [7], range(GROUPS), 5)
+        quantise_h(1, (4, 5))
         store(2)
-        q_half(1, (6,))
+        quantise_h(1, (6,))
         store(3)
-        weight(1, 7)
-        mix_run((4, 5), (0, 1))
-        h_half(1, ((7,),), (6,))
+        weigh(1, 7)
+        mix(4, 0)
+        mix(5, 1)
+        turn_h(1, (7,), 6)
         store(4)
-        mix_run((6,), (7,))
+        mix(6, 7)
         store(5)
-        q_half(1, (7,))
-        mix_run((7,), (2,))
+        quantise_h(1, (7,))
+        mix(7, 2)
         store(6)
-        store(7, 2)
+        store(7, parts=2)

@@ -60,14 +60,16 @@ def tile_weighted_diis_residuals_e3_kernel(tc, g_words, g_scales, errs, pair, co
         make_identity(nc, ident[:])
         lam_sb = sb([P, R], BF16, "lam_sb")
 
-        quarter_words, g_code, g_plane, pair_sb, coef_raw = {}, {}, {}, {}, {}
+        raw_words, g_code, g_plane, pair_sb, coef_raw = {}, {}, {}, {}, {}
 
-        def load_errs(j, g0, rt0, count=1):
-            t = sb([P, count, 2 * PASS], BF16, f"errs{j}{rt0}{g0}")
-            rows = slice(j * PASS + rt0 * P, j * PASS + (rt0 + count) * P)
-            nc.sync.dma_start(out=t[:], in_=errs[rows, g0 * PASS : (g0 + 2) * PASS].rearrange("(a p) k -> p a k", p=P))
-            for a in range(count):
-                quarter_words[j, rt0 + a, g0] = t[:, a, :].bitcast(F32)
+        def load_errs(j, groups, rts):
+            t = sb([P, len(rts), len(groups) * PASS], BF16, f"errs{j}{rts[0]}{groups[0]}")
+            rows = slice(j * PASS + rts.start * P, j * PASS + rts.stop * P)
+            nc.sync.dma_start(out=t[:], in_=errs[rows, groups.start * PASS : groups.stop * PASS].rearrange("(a p) k -> p a k", p=P))
+            words = t[:].rearrange("p a k -> p (a k)").bitcast(F32)
+            for a, rt in enumerate(rts):
+                for b, g in enumerate(groups):
+                    raw_words[j, rt, g] = (words, a * len(groups) + b)
 
         def load_g(groups, tiles):
             t = sb([P, len(groups), len(tiles) * P], U32, f"g_code{groups[0]}{tiles[0]}")
@@ -102,19 +104,16 @@ def tile_weighted_diis_residuals_e3_kernel(tc, g_words, g_scales, errs, pair, co
 
         sorted_words, errs_bank, errs_quads, errs_code, errs_plane = {}, {}, {}, {}, {}
 
-        def group_words(j, rt, g):
-            return quarter_words[j, rt, g - g % 2][:, (g % 2) * 2 * P : (g % 2 + 1) * 2 * P]
+        def group_words(j, rt, g, count=1):
+            words, place = raw_words[j, rt, g]
+            return words[:, place * 2 * P : (place + count) * 2 * P]
 
-        def sort_quarter(j, rt, g0, engine):
+        def sort(j, pieces, engine):
             t = stage.tile([P, 2, 2, P], F32, align_bytes=64, name="sorted")
-            move(engine, t[:], quarter_words[j, rt, g0].rearrange("p (g w u) -> p g u w", g=2, u=2))
-            for a in range(2):
-                sorted_words[j, rt, g0 + a] = t[:, a]
-
-        def sort_group(j, rt, g, engine):
-            t = stage.tile([P, 2, P], F32, align_bytes=64, name="sorted_group", bufs=2)
-            move(engine, t[:], group_words(j, rt, g).rearrange("p (w u) -> p u w", u=2))
-            sorted_words[j, rt, g] = t
+            rt, g = pieces[0]
+            move(engine, t[:, : len(pieces)], group_words(j, rt, g, len(pieces)).rearrange("p (a w u) -> p a u w", a=len(pieces), u=2))
+            for a, (rt, g) in enumerate(pieces):
+                sorted_words[j, rt, g] = t[:, a]
 
         def turn(j, g, rt, rts, b):
             if rt == rts[0]:
@@ -148,11 +147,11 @@ def tile_weighted_diis_residuals_e3_kernel(tc, g_words, g_scales, errs, pair, co
 
         b_acc, h_sb, h_quads, h_code = {}, {}, {}, {}
 
-        def overlaps(j, tiles, groups, first_bank=0):
+        def overlaps(j, tiles, groups, banks=None):
             for g in groups:
                 for a, i in enumerate(tiles):
                     if g == 0:
-                        b_acc[j, i] = bank(first_bank + a, [P, PASS])
+                        b_acc[j, i] = bank(banks[a], [P, PASS])
                     plane = g_plane[g - g % 2][:, g % 2, i * P : (i + 1) * P]
                     mx_pass(b_acc[j, i][:], g_code[i, g], plane, errs_code[j, g][:], errs_plane[j, g][:], g == 0, g == GROUPS - 1)
 
@@ -165,13 +164,13 @@ def tile_weighted_diis_residuals_e3_kernel(tc, g_words, g_scales, errs, pair, co
                 op=ALU.mult,
             )
 
-        def turn_h(j, tiles, b):
+        def turn_h(j, tiles, b, engine=SCALAR):
             t = bank(b, [P, 4, P])
             for a, i in enumerate(tiles):
                 words = h_sb[j, i][:].bitcast(F32)
                 for u in range(2):
                     nc.tensor.transpose(t[:, 2 * a + u, :], words[:, u * P : (u + 1) * P], ident[:])
-            h_quads[j, tiles] = gathered(SCALAR, t, len(tiles))
+            h_quads[j, tiles] = gathered(engine, t, len(tiles))
 
         def quantise_h(j, tiles):
             code = sb([P, len(tiles) * P], U32, f"h_code{j}{tiles[0]}")
@@ -229,63 +228,69 @@ def tile_weighted_diis_residuals_e3_kernel(tc, g_words, g_scales, errs, pair, co
             for n in range(count):
                 mx_pass(t[:], warm_code[:, :P], warm_plane[:, :P], warm_code[:, P:], warm_plane[:, P:], True, True)
 
+        front, back = range(0, 2), range(2, 4)
         clear_planes(0)
         clear_planes(2)
-        for rt in range(ROW_TILES):
-            load_errs(0, 0, rt)
+        load_errs(0, range(0, 2), range(0, 1))
+        load_errs(0, range(0, 2), range(1, 2))
+        load_errs(0, range(0, 2), range(2, 3))
+        load_errs(0, range(0, 2), range(3, 4))
         load_scales(0)
         load_g(range(0, 1), range(0, 4))
         load_g(range(1, 2), range(0, 4))
-        for rt in range(ROW_TILES):
-            load_errs(0, 2, rt)
+        load_errs(0, range(2, 4), range(0, 1))
+        load_errs(0, range(2, 4), range(1, 2))
+        load_errs(0, range(2, 4), range(2, 3))
+        load_errs(0, range(2, 4), range(3, 4))
         load_g(range(0, 2), range(4, 8))
-        load_scales(2)
-        load_g(range(2, 4), range(0, 6))
-        load_pair(0, range(0, 4))
-        for rt in range(ROW_TILES):
-            load_errs(1, 0, rt)
-        load_g(range(2, 4), range(6, 8))
-        load_pair(0, range(4, 6))
-        load_pair(0, range(6, 8))
-        load_errs(1, 2, 0, 2)
-        load_errs(1, 2, 2, 2)
-        load_coef(0)
-        load_coef(1)
-        load_pair(1, range(0, 4))
-        load_pair(1, range(4, 8))
-        nc.sync.dma_start(out=lam_sb[:], in_=lam.partition_broadcast(P))
 
-        front, back = (0, 1), (2, 3)
 
         warm_up(4, 0)
         for rt in range(3):
-            sort_quarter(0, rt, 0, VECTOR)
+            sort(0, [(rt, 0), (rt, 1)], VECTOR)
         turn(0, 0, 0, front, 4)
         turn(0, 1, 0, front, 5)
         turn(0, 0, 1, front, 4)
         gather(0, 0, front, SCALAR)
         turn(0, 1, 1, front, 5)
-        turn(0, 0, 2, (2,), 6)
-        turn(0, 0, 3, (3,), 7)
-        sort_group(0, 3, 1, VECTOR)
-        gather(0, 0, (2,), VECTOR)
+        turn(0, 0, 2, range(2, 3), 6)
+        turn(0, 0, 3, range(3, 4), 7)
+        sort(0, [(3, 1)], VECTOR)
+        gather(0, 0, range(2, 3), VECTOR)
         quantise(0, 0, front)
-        gather(0, 0, (3,), SCALAR)
-        quantise(0, 0, (2,))
-        quantise(0, 0, (3,))
+        gather(0, 0, range(3, 4), SCALAR)
+        quantise(0, 0, range(2, 3))
+        quantise(0, 0, range(3, 4))
         gather(0, 1, front, SCALAR)
         turn(0, 1, 2, back, 3)
         turn(0, 1, 3, back, 3)
         warm_up(1, 2)
+        load_scales(2)
+        load_g(range(2, 4), range(0, 6))
+        load_pair(0, range(0, 4))
+        load_errs(1, range(0, 2), range(0, 1))
+        load_errs(1, range(0, 2), range(1, 2))
+        load_errs(1, range(0, 2), range(2, 3))
+        load_errs(1, range(0, 2), range(3, 4))
+        load_g(range(2, 4), range(6, 8))
+        load_pair(0, range(4, 6))
+        load_errs(1, range(2, 4), range(0, 2))
+        load_errs(1, range(2, 4), range(2, 4))
+        load_pair(0, range(6, 8))
+        load_coef(0)
+        load_pair(1, range(0, 4))
+        load_coef(1)
+        load_pair(1, range(4, 8))
+        nc.sync.dma_start(out=lam_sb[:], in_=lam.partition_broadcast(P))
         gather(0, 1, back, VECTOR)
         quantise(0, 1, front)
         quantise(0, 1, back)
 
         held = 2
-        overlaps(0, range(0, 4), [0])
+        overlaps(0, range(0, 4), [0], range(0, 4))
         overlaps(0, range(0, held), [1])
         for rt in range(ROW_TILES):
-            sort_quarter(0, rt, 2, VECTOR)
+            sort(0, [(rt, 2), (rt, 3)], VECTOR)
         for c, rts in enumerate((front, back)):
             for rt in rts:
                 turn(0, 2, rt, rts, 4 + 2 * c)
@@ -293,8 +298,8 @@ def tile_weighted_diis_residuals_e3_kernel(tc, g_words, g_scales, errs, pair, co
             gather(0, 2, rts, SCALAR)
             gather(0, 3, rts, VECTOR)
         overlaps(0, range(held, 4), [1])
-        overlaps(0, range(4, 6), [0, 1], 4)
-        overlaps(0, range(6, 8), [0, 1], 6)
+        overlaps(0, range(4, 6), [0, 1], (4, 5))
+        overlaps(0, range(6, 8), [0, 1], (6, 7))
         for g in (2, 3):
             quantise(0, g, front)
             quantise(0, g, back)
@@ -305,8 +310,8 @@ def tile_weighted_diis_residuals_e3_kernel(tc, g_words, g_scales, errs, pair, co
             if i < 4:
                 weigh(0, i)
         for rt in range(3):
-            sort_quarter(1, rt, 0, SCALAR)
-        sort_group(1, 3, 1, VECTOR)
+            sort(1, [(rt, 0), (rt, 1)], SCALAR)
+        sort(1, [(3, 1)], VECTOR)
         for c, rts in enumerate((front, back)):
             for g in (0, 1):
                 for rt in rts:
@@ -319,24 +324,22 @@ def tile_weighted_diis_residuals_e3_kernel(tc, g_words, g_scales, errs, pair, co
         quantise(1, 0, back)
         quantise(1, 1, front)
         quantise(1, 1, back)
-        for i in range(5, 8):
-            weigh(0, i)
+        weigh(0, 5)
 
+        overlaps(1, range(0, 2), [0, 1], (0, 1))
         for rt in range(ROW_TILES):
-            sort_quarter(1, rt, 2, SCALAR if rt < 2 else VECTOR)
-        overlaps(1, range(0, 2), [0, 1], 0)
-        for q in range(3):
-            turn_h(0, (2 * q, 2 * q + 1), 2 + q)
-        overlaps(1, range(2, 4), [0, 1], 6)
-        for q in range(3):
-            quantise_h(0, (2 * q, 2 * q + 1))
-        for g in (2, 3):
-            for c, rts in enumerate((front, back)):
+            sort(1, [(rt, 2), (rt, 3)], SCALAR if rt < 2 else VECTOR)
+        for c, rts in enumerate((front, back)):
+            for g in (2, 3):
                 for rt in rts:
-                    turn(1, g, rt, rts, 2 * g - 2 + c)
-            gather(1, g, front, SCALAR)
-            gather(1, g, back, VECTOR if g == 2 else SCALAR)
-        overlaps(1, range(4, 6), [0, 1], 2)
+                    turn(1, g, rt, rts, 2 * c + g)
+                if (c, g) != (1, 2):
+                    gather(1, g, rts, SCALAR)
+        weigh(0, 6)
+        weigh(0, 7)
+        gather(1, 2, back, VECTOR)
+        for i, b in ((2, 6), (3, 7), (4, 2), (5, 3)):
+            overlaps(1, [i], [0, 1], (b,))
         for g in (2, 3):
             quantise(1, g, front)
             quantise(1, g, back)
@@ -346,46 +349,51 @@ def tile_weighted_diis_residuals_e3_kernel(tc, g_words, g_scales, errs, pair, co
         quantise_coef(0, 0)
 
         overlaps(1, range(0, 2), [2, 3])
-        weigh(1, 0)
-        weigh(1, 1)
         for i in range(2, 6):
             overlaps(1, [i], [2, 3])
-            if i < 4:
-                weigh(1, i)
-        turn_h(1, (0, 1), 4)
-        turn_h(1, (2, 3), 5)
-        turn_h(0, (6, 7), 1)
         quantise_coef(0, 1)
+        weigh(1, 0)
+        for i in range(1, 4):
+            weigh(1, i)
+        turn_h(0, (0, 1), 4)
+        turn_h(0, (2, 3), 5)
+        turn_h(1, (0, 1), 0)
+        turn_h(1, (2, 3), 1)
+        turn_h(0, (4, 5), 6)
+        turn_h(0, (6, 7), 7)
+        weigh(1, 4)
         quantise_coef(1, 0)
         quantise_coef(1, 1)
-        weigh(1, 4)
-        overlaps(1, [6], range(GROUPS), 0)
-        quantise_h(1, (0, 1))
         weigh(1, 5)
+        overlaps(1, [6], range(GROUPS), (2,))
+        quantise_h(0, (0, 1))
+        quantise_h(1, (0, 1))
+        quantise_h(0, (2, 3))
         quantise_h(1, (2, 3))
         weigh(1, 6)
-        mix(0, 6)
-        mix(1, 1)
-        turn_h(1, (4, 5), 7)
-        turn_h(1, (6,), 2)
+        mix(0, 3)
+        mix(1, 4)
+        turn_h(1, (4, 5), 5)
+        turn_h(1, (6,), 0)
+        quantise_h(0, (4, 5))
+        quantise_h(0, (6, 7))
         store(0)
         store(1)
-        quantise_h(0, (6, 7))
-        mix(2, 3)
-        mix(3, 4)
-        overlaps(1, [7], range(GROUPS), 5)
-        quantise_h(1, (4, 5))
+        mix(2, 1)
+        mix(3, 6)
+        overlaps(1, [7], range(GROUPS), (7,))
         store(2)
+        quantise_h(1, (4, 5))
         quantise_h(1, (6,))
         store(3)
         weigh(1, 7)
-        mix(4, 0)
-        mix(5, 1)
-        turn_h(1, (7,), 6)
+        mix(4, 2)
+        mix(5, 3)
+        turn_h(1, (7,), 4)
         store(4)
-        mix(6, 7)
+        mix(6, 5)
         store(5)
         quantise_h(1, (7,))
-        mix(7, 2)
+        mix(7, 0)
         store(6)
         store(7, parts=2)

@@ -84,9 +84,9 @@ def tile_weighted_diis_residuals_e3_kernel(tc, g_words, g_scales, errs, pair, co
             nc.vector.memset(t[:].bitcast(I32), 0)
             g_plane[g0] = t
 
-        def load_scales(g0):
+        def load_scales(g0, queue):
             for r in range(4):
-                nc.sync.dma_start(
+                queue.dma_start(
                     out=g_plane[g0][r:P:32, :, :].bitcast(I32),
                     in_=g_scales[g0 : g0 + 2, r:16:4, :].rearrange("g q n -> q g n").bitcast(I32),
                 )
@@ -235,7 +235,8 @@ def tile_weighted_diis_residuals_e3_kernel(tc, g_words, g_scales, errs, pair, co
         load_errs(0, range(0, 2), range(1, 2))
         load_errs(0, range(0, 2), range(2, 3))
         load_errs(0, range(0, 2), range(3, 4))
-        load_scales(0)
+        load_scales(0, nc.sync)
+        load_scales(2, nc.gpsimd)
         load_g(range(0, 1), range(0, 4))
         load_g(range(1, 2), range(0, 4))
         load_errs(0, range(2, 4), range(0, 1))
@@ -265,7 +266,6 @@ def tile_weighted_diis_residuals_e3_kernel(tc, g_words, g_scales, errs, pair, co
         turn(0, 1, 2, back, 3)
         turn(0, 1, 3, back, 3)
         warm_up(1, 2)
-        load_scales(2)
         load_g(range(2, 4), range(0, 6))
         load_pair(0, range(0, 4))
         load_errs(1, range(0, 2), range(0, 1))

@@ -130,8 +130,8 @@ def tile_weighted_diis_residuals_e3_kernel(tc, g_words, g_scales, errs, pair, co
             words = t[:].rearrange("p n t -> p (n t)").bitcast(F32)[:, : 2 * count * P]
             move(
                 engine,
-                words.rearrange("p (b r u) -> p b r u", b=count, u=2),
-                source[:, : 2 * count, :].rearrange("p (b u) r -> p b r u", u=2),
+                words.rearrange("p (b c i u) -> p b c u i", b=count, i=2, u=2),
+                source[:, : 2 * count, :].rearrange("p (b u) (c i) -> p b c u i", u=2, i=2),
             )
             return t[:, : count * P, :].rearrange("p n t -> p (n t)")
 

@@ -60,16 +60,15 @@ def tile_weighted_diis_residuals_e3_kernel(tc, g_words, g_scales, errs, pair, co
         make_identity(nc, ident[:])
         lam_sb = sb([P, R], BF16, "lam_sb")
 
-        raw_words, g_code, g_plane, pair_sb, coef_raw = {}, {}, {}, {}, {}
+        raw_words, g_code, g_plane, plane_tile, pair_sb, coef_raw = {}, {}, {}, {}, {}, {}
 
-        def load_errs(j, groups, rts):
-            t = sb([P, len(rts), len(groups) * PASS], BF16, f"errs{j}{rts[0]}{groups[0]}")
-            rows = slice(j * PASS + rts.start * P, j * PASS + rts.stop * P)
-            nc.sync.dma_start(out=t[:], in_=errs[rows, groups.start * PASS : groups.stop * PASS].rearrange("(a p) k -> p a k", p=P))
-            words = t[:].rearrange("p a k -> p (a k)").bitcast(F32)
-            for a, rt in enumerate(rts):
-                for b, g in enumerate(groups):
-                    raw_words[j, rt, g] = (words, a * len(groups) + b)
+        def load_errs(j, groups, rt):
+            t = sb([P, len(groups) * PASS], BF16, f"errs{j}{rt}{groups[0]}")
+            u, h = divmod(rt, 2)
+            first = j * PASS + h * 2 * P + u
+            nc.sync.dma_start(out=t[:], in_=errs[first : first + 2 * P - 1 : 2, groups.start * PASS : groups.stop * PASS])
+            for b, g in enumerate(groups):
+                raw_words[j, rt, g] = (t[:].bitcast(F32), b)
 
         def load_g(groups, tiles):
             t = sb([P, len(groups), len(tiles) * P], U32, f"g_code{groups[0]}{tiles[0]}")
@@ -79,24 +78,26 @@ def tile_weighted_diis_residuals_e3_kernel(tc, g_words, g_scales, errs, pair, co
                 for b, i in enumerate(tiles):
                     g_code[i, g] = t[:, a, b * P : (b + 1) * P]
 
-        def clear_planes(g0):
-            t = sb([P, 2, M], U8, f"g_plane{g0}")
+        def clear_plane(groups, tiles):
+            t = sb([P, len(groups), len(tiles) * P], U8, f"g_plane{groups[0]}{tiles[0]}")
             nc.vector.memset(t[:].bitcast(I32), 0)
-            g_plane[g0] = t
+            plane_tile[groups, tiles] = t
+            for a, g in enumerate(groups):
+                for b, i in enumerate(tiles):
+                    g_plane[i, g] = t[:, a, b * P : (b + 1) * P]
 
-        def load_scales(g0, queue):
+        def load_scales(groups, tiles, queue):
             for r in range(4):
-                queue.dma_start(
-                    out=g_plane[g0][r:P:32, :, :].bitcast(I32),
-                    in_=g_scales[g0 : g0 + 2, r:16:4, :].rearrange("g q n -> q g n").bitcast(I32),
-                )
+                rows = g_scales[groups.start : groups.stop, r:16:4, tiles.start * P : tiles.stop * P]
+                queue.dma_start(out=plane_tile[groups, tiles][r:P:32, :, :].bitcast(I32), in_=rows.rearrange("g q n -> q g n").bitcast(I32))
 
-        def load_pair(j, tiles):
-            t = sb([P, len(tiles), PASS], BF16, f"pair{j}{tiles[0]}")
-            piece = pair[tiles.start * P : tiles.stop * P, j * PASS : (j + 1) * PASS]
+        def load_pair(halves, tiles):
+            t = sb([P, len(tiles), len(halves) * PASS], BF16, f"pair{halves[0]}{tiles[0]}")
+            piece = pair[tiles.start * P : tiles.stop * P, halves.start * PASS : halves.stop * PASS]
             nc.sync.dma_start(out=t[:], in_=piece.rearrange("(i p) n -> p i n", p=P))
-            for a, i in enumerate(tiles):
-                pair_sb[j, i] = t[:, a, :]
+            for b, j in enumerate(halves):
+                for a, i in enumerate(tiles):
+                    pair_sb[j, i] = (t[:, :, b * PASS : (b + 1) * PASS], a)
 
         def load_coef(j):
             coef_raw[j] = sb([P, 4, R], BF16, f"coef_raw{j}")
@@ -115,15 +116,20 @@ def tile_weighted_diis_residuals_e3_kernel(tc, g_words, g_scales, errs, pair, co
             for a, (rt, g) in enumerate(pieces):
                 sorted_words[j, rt, g] = t[:, a]
 
-        def turn(j, g, rt, rts, b):
-            if rt == rts[0]:
-                errs_bank[j, g, rts] = bank(b, [P, 4, P])
+        def turn(j, pieces, b):
+            t = bank(b, [P, 4, P])
+            for a, piece in enumerate(pieces):
+                errs_bank[j, piece] = (t, a)
+
+        def turn_piece(j, piece):
+            t, a = errs_bank[j, piece]
+            rt, g = piece
             for u in range(2):
                 if (j, rt, g) in sorted_words:
                     words = sorted_words[j, rt, g][:, u, :]
                 else:
                     words = group_words(j, rt, g)[:, u : 2 * P : 2]
-                nc.tensor.transpose(errs_bank[j, g, rts][:, 2 * (rt - rts[0]) + u, :], words, ident[:])
+                nc.tensor.transpose(t[:, 2 * a + u, :], words, ident[:])
 
         def gathered(engine, source, count):
             t = stage.tile([P, 2 * P, 4], BF16, align_bytes=64, name="quads")
@@ -131,46 +137,82 @@ def tile_weighted_diis_residuals_e3_kernel(tc, g_words, g_scales, errs, pair, co
             move(
                 engine,
                 words.rearrange("p (b c i u) -> p b c u i", b=count, i=2, u=2),
-                source[:, : 2 * count, :].rearrange("p (b u) (c i) -> p b c u i", u=2, i=2),
+                source.rearrange("p (b u) (c i) -> p b c u i", u=2, i=2),
             )
             return t[:, : count * P, :].rearrange("p n t -> p (n t)")
 
-        def gather(j, g, rts, engine):
-            errs_quads[j, g, rts] = gathered(engine, errs_bank[j, g, rts], len(rts))
+        def gather(j, pieces, engine):
+            t, a = errs_bank[j, pieces[0]]
+            quads = gathered(engine, t[:, 2 * a : 2 * (a + len(pieces)), :], len(pieces))
+            for c, piece in enumerate(pieces):
+                errs_quads[j, piece] = (quads, c)
 
-        def quantise(j, g, rts):
-            if rts[0] == 0:
+        def quantise(j, pieces):
+            rt, g = pieces[0]
+            if (j, g) not in errs_code:
                 errs_code[j, g] = sb([P, PASS], U32, f"errs_code{j}{g}")
                 errs_plane[j, g] = sb([P, PASS], U8, f"errs_plane{j}{g}")
-            cols = slice(rts[0] * P, (rts[-1] + 1) * P)
-            nc.vector.quantize_mx(out=errs_code[j, g][:, cols].bitcast(E4M3X4), scales=errs_plane[j, g][:, cols], in_=errs_quads[j, g, rts])
-
-        b_acc, h_sb, h_quads, h_code = {}, {}, {}, {}
-
-        def overlaps(j, tiles, groups, banks=None):
-            for g in groups:
-                for a, i in enumerate(tiles):
-                    if g == 0:
-                        b_acc[j, i] = bank(banks[a], [P, PASS])
-                    plane = g_plane[g - g % 2][:, g % 2, i * P : (i + 1) * P]
-                    mx_pass(b_acc[j, i][:], g_code[i, g], plane, errs_code[j, g][:], errs_plane[j, g][:], g == 0, g == GROUPS - 1)
-
-        def weigh(j, i):
-            h_sb[j, i] = sb([P, PASS], BF16, f"h{j}{i}")
-            nc.vector.tensor_tensor(
-                out=h_sb[j, i][:].rearrange("p (u w e) -> p u w e", u=2, e=2),
-                in0=b_acc[j, i][:].rearrange("p (w u e) -> p u w e", u=2, e=2),
-                in1=pair_sb[j, i].rearrange("p (w u e) -> p u w e", u=2, e=2),
-                op=ALU.mult,
+            cols = slice(rt * P, (rt + len(pieces)) * P)
+            quads, c = errs_quads[j, pieces[0]]
+            nc.vector.quantize_mx(
+                out=errs_code[j, g][:, cols].bitcast(E4M3X4), scales=errs_plane[j, g][:, cols], in_=quads[:, c * PASS : (c + len(pieces)) * PASS]
             )
 
-        def turn_h(j, tiles, b, engine=SCALAR):
-            t = bank(b, [P, 4, P])
+        def of_group(rts, g):
+            return [(rt, g) for rt in rts]
+
+        def of_row_tile(rt, groups):
+            return [(rt, g) for g in groups]
+
+        b_acc, strip_acc, h_sb, h_bank, h_quads, h_code = {}, {}, {}, {}, {}, {}
+
+        def overlaps(j, tiles, groups, banks=None, rts=range(ROW_TILES)):
+            cols = slice(rts.start * P, rts.stop * P)
+            for g in groups:
+                for a, i in enumerate(tiles):
+                    first = g == 0 and rts.start == 0
+                    last = g == GROUPS - 1 and rts.stop == ROW_TILES
+                    if first:
+                        b_acc[j, i] = bank(banks[a], [P, PASS])
+                    mx_pass(b_acc[j, i][:, cols], g_code[i, g], g_plane[i, g], errs_code[j, g][:, cols], errs_plane[j, g][:, cols], first, last)
+
+        def strip(u, tiles, b):
+            acc = bank(b, [P, len(tiles), 2 * P])
+            strip_acc[u, tiles] = acc
+            cols = slice(u * 2 * P, (u + 1) * 2 * P)
+            for g in range(GROUPS):
+                for a, i in enumerate(tiles):
+                    first, last = (g, a) == (0, 0), (g, a) == (GROUPS - 1, len(tiles) - 1)
+                    mx_pass(acc[:, a, :], g_code[i, g], g_plane[i, g], errs_code[1, g][:, cols], errs_plane[1, g][:, cols], first, last)
+
+        def weigh(i):
+            t, a = pair_sb[0, i]
+            h = sb([P, 2, 2 * P], BF16, f"h0{i}")
+            nc.vector.tensor_tensor(
+                out=h[:],
+                in0=b_acc[0, i][:].rearrange("p (u c) -> p u c", u=2),
+                in1=t[:, a, :].rearrange("p (c u) -> p u c", u=2),
+                op=ALU.mult,
+            )
+            for u in range(2):
+                h_sb[0, i, u] = h[:, u, :]
+
+        def weigh_strip(u, tiles):
+            t, a = pair_sb[1, tiles[0]]
+            h = sb([P, len(tiles), 2 * P], BF16, f"h1{tiles[0]}{u}")
+            nc.vector.tensor_tensor(out=h[:], in0=strip_acc[u, tiles][:], in1=t[:, a : a + len(tiles), u:PASS:2], op=ALU.mult)
             for a, i in enumerate(tiles):
-                words = h_sb[j, i][:].bitcast(F32)
-                for u in range(2):
-                    nc.tensor.transpose(t[:, 2 * a + u, :], words[:, u * P : (u + 1) * P], ident[:])
-            h_quads[j, tiles] = gathered(engine, t, len(tiles))
+                h_sb[1, i, u] = h[:, a, :]
+
+        def turn_h(j, tiles, b, parities=range(2)):
+            if parities[0] == 0:
+                h_bank[j, tiles] = bank(b, [P, 4, P])
+            for a, i in enumerate(tiles):
+                for u in parities:
+                    nc.tensor.transpose(h_bank[j, tiles][:, 2 * a + u, :], h_sb[j, i, u].bitcast(F32), ident[:])
+
+        def gather_h(j, tiles, engine=SCALAR):
+            h_quads[j, tiles] = gathered(engine, h_bank[j, tiles][:, : 2 * len(tiles), :], len(tiles))
 
         def quantise_h(j, tiles):
             code = sb([P, len(tiles) * P], U32, f"h_code{j}{tiles[0]}")
@@ -181,12 +223,12 @@ def tile_weighted_diis_residuals_e3_kernel(tc, g_words, g_scales, errs, pair, co
 
         coef_quads, coef_code, coef_plane, out_acc = {}, {}, {}, {}
 
-        def interleave_coef(j, c):
+        def interleave_coef(j, c, engine=SCALAR):
             coef_quads[j, c] = sb([P, R // 2, 4], BF16, f"coef_quads{j}{c}")
             move(
-                SCALAR,
-                coef_quads[j, c][:].rearrange("p (a i) t -> p a t i", i=4),
-                coef_raw[j][:, :, c * R // 2 : (c + 1) * R // 2].rearrange("p t (a i) -> p a t i", i=4),
+                engine,
+                coef_quads[j, c][:].rearrange("p (a i) (u e) -> p a u e i", i=4, u=2),
+                coef_raw[j][:, :, c * R // 2 : (c + 1) * R // 2].rearrange("p (e u) (a i) -> p a u e i", i=4, u=2),
             )
 
         def quantise_coef(j, c):
@@ -200,18 +242,23 @@ def tile_weighted_diis_residuals_e3_kernel(tc, g_words, g_scales, errs, pair, co
                 in_=coef_quads[j, c][:].rearrange("p n t -> p (n t)"),
             )
 
-        def mix(i, b):
-            out_acc[i] = bank(b, [P, R])
-            for j in range(HALVES):
+        def mix(i, banks, halves=range(HALVES)):
+            width = R // len(banks)
+            for j in halves:
                 code, plane = h_code[j, i]
-                mx_pass(out_acc[i][:], code, plane, coef_code[j][:], coef_plane[j][:], j == 0, j == HALVES - 1)
+                for c, b in enumerate(banks):
+                    if j == 0:
+                        out_acc[i, c] = bank(b, [P, width])
+                    cols = slice(c * width, (c + 1) * width)
+                    mx_pass(out_acc[i, c][:], code, plane, coef_code[j][:, cols], coef_plane[j][:, cols], j == 0, j == HALVES - 1)
 
-        def store(i, parts=1):
-            for c in range(parts):
-                cols = slice(c * R // parts, (c + 1) * R // parts)
-                res = sb([P, R // parts], F32, f"res{i}{c}")
-                nc.vector.tensor_tensor(out=res[:], in0=out_acc[i][:, cols], in1=lam_sb[:, cols], op=ALU.subtract)
-                nc.sync.dma_start(out=out[i * P : (i + 1) * P, cols], in_=res[:])
+        def store(i, c=0):
+            acc = out_acc[i, c]
+            width = acc.shape[1]
+            cols = slice(c * width, (c + 1) * width)
+            res = sb([P, width], F32, f"res{i}{c}")
+            nc.vector.tensor_tensor(out=res[:], in0=acc[:], in1=lam_sb[:, cols], op=ALU.subtract)
+            nc.sync.dma_start(out=out[i * P : (i + 1) * P, cols], in_=res[:])
 
         zero_words = 64
         blank = sb([P, zero_words + (P + PASS) + (P + PASS) // 4], U32, "blank")
@@ -229,171 +276,195 @@ def tile_weighted_diis_residuals_e3_kernel(tc, g_words, g_scales, errs, pair, co
                 mx_pass(t[:], warm_code[:, :P], warm_plane[:, :P], warm_code[:, P:], warm_plane[:, P:], True, True)
 
         front, back = range(0, 2), range(2, 4)
-        clear_planes(0)
-        clear_planes(2)
-        load_errs(0, range(0, 2), range(0, 1))
-        load_errs(0, range(0, 2), range(1, 2))
-        load_errs(0, range(0, 2), range(2, 3))
-        load_errs(0, range(0, 2), range(3, 4))
-        load_scales(0, nc.sync)
-        load_scales(2, nc.gpsimd)
-        load_g(range(0, 1), range(0, 4))
-        load_g(range(1, 2), range(0, 4))
-        load_errs(0, range(2, 4), range(0, 1))
-        load_errs(0, range(2, 4), range(1, 2))
-        load_errs(0, range(2, 4), range(2, 3))
-        load_errs(0, range(2, 4), range(3, 4))
-        load_g(range(0, 2), range(4, 8))
+        near, far = range(0, 4), range(4, 8)
+        low, high = range(0, 2), range(2, 4)
+        clear_plane(low, near)
+        clear_plane(high, near)
+        clear_plane(range(GROUPS), far)
 
+        def load_quarter(j, groups):
+            for rt in range(ROW_TILES):
+                load_errs(j, groups, rt)
 
-        warm_up(4, 0)
-        for rt in range(3):
-            sort(0, [(rt, 0), (rt, 1)], VECTOR)
-        turn(0, 0, 0, front, 4)
-        turn(0, 1, 0, front, 5)
-        turn(0, 0, 1, front, 4)
-        gather(0, 0, front, SCALAR)
-        turn(0, 1, 1, front, 5)
-        turn(0, 0, 2, range(2, 3), 6)
-        turn(0, 0, 3, range(3, 4), 7)
-        sort(0, [(3, 1)], VECTOR)
-        gather(0, 0, range(2, 3), VECTOR)
-        quantise(0, 0, front)
-        gather(0, 0, range(3, 4), SCALAR)
-        quantise(0, 0, range(2, 3))
-        quantise(0, 0, range(3, 4))
-        gather(0, 1, front, SCALAR)
-        turn(0, 1, 2, back, 3)
-        turn(0, 1, 3, back, 3)
-        warm_up(1, 2)
-        load_g(range(2, 4), range(0, 6))
-        load_pair(0, range(0, 4))
-        load_errs(1, range(0, 2), range(0, 1))
-        load_errs(1, range(0, 2), range(1, 2))
-        load_errs(1, range(0, 2), range(2, 3))
-        load_errs(1, range(0, 2), range(3, 4))
-        load_g(range(2, 4), range(6, 8))
-        load_pair(0, range(4, 6))
-        load_errs(1, range(2, 4), range(0, 2))
-        load_errs(1, range(2, 4), range(2, 4))
-        load_pair(0, range(6, 8))
+        load_quarter(0, low)
+        load_scales(low, near, nc.sync)
+        load_g(range(0, 1), near)
+        load_g(range(1, 2), near)
+        load_quarter(0, high)
+        load_scales(high, near, nc.sync)
+        load_g(range(2, 3), near)
+        load_g(range(3, 4), near)
+        load_scales(range(GROUPS), far, nc.sync)
+        load_g(low, far)
+        load_pair(range(0, 1), near)
+        load_g(high, range(4, 6))
+        for groups in (low, high):
+            for rt in front:
+                load_errs(1, groups, rt)
+        load_g(high, range(6, 8))
+        load_pair(range(HALVES), range(4, 6))
+        load_pair(range(HALVES), range(6, 8))
+        for rt in back:
+            load_errs(1, range(GROUPS), rt)
+        load_pair(range(1, 2), near)
         load_coef(0)
-        load_pair(1, range(0, 4))
         load_coef(1)
-        load_pair(1, range(4, 8))
         nc.sync.dma_start(out=lam_sb[:], in_=lam.partition_broadcast(P))
-        gather(0, 1, back, VECTOR)
-        quantise(0, 1, front)
-        quantise(0, 1, back)
 
-        held = 2
-        overlaps(0, range(0, 4), [0], range(0, 4))
-        overlaps(0, range(0, held), [1])
-        for rt in range(ROW_TILES):
-            sort(0, [(rt, 2), (rt, 3)], VECTOR)
-        for c, rts in enumerate((front, back)):
-            for rt in rts:
-                turn(0, 2, rt, rts, 4 + 2 * c)
-                turn(0, 3, rt, rts, 5 + 2 * c)
-            gather(0, 2, rts, SCALAR)
-            gather(0, 3, rts, VECTOR)
-        overlaps(0, range(held, 4), [1])
-        overlaps(0, range(4, 6), [0, 1], (4, 5))
-        overlaps(0, range(6, 8), [0, 1], (6, 7))
-        for g in (2, 3):
-            quantise(0, g, front)
-            quantise(0, g, back)
-
-        cover = 5
-        for i in range(cover):
-            overlaps(0, [i], [2, 3])
-            if i < 4:
-                weigh(0, i)
+        warm_up(3, 0)
         for rt in range(3):
-            sort(1, [(rt, 0), (rt, 1)], SCALAR)
-        sort(1, [(3, 1)], VECTOR)
-        for c, rts in enumerate((front, back)):
-            for g in (0, 1):
-                for rt in rts:
-                    turn(1, g, rt, rts, 2 * c + g)
-                gather(1, g, rts, VECTOR if g + c == 0 else SCALAR)
-        for i in range(cover, 8):
-            overlaps(0, [i], [2, 3])
-        quantise(1, 0, front)
-        weigh(0, 4)
-        quantise(1, 0, back)
-        quantise(1, 1, front)
-        quantise(1, 1, back)
-        weigh(0, 5)
+            sort(0, of_row_tile(rt, low), VECTOR)
+        sort(0, [(3, 1)], VECTOR)
+        for g in low:
+            turn(0, of_group(front, g), 4 + g)
+            for piece in of_group(front, g):
+                turn_piece(0, piece)
+            gather(0, of_group(front, g), SCALAR)
+        warm_up(1, 1)
+        for g in low:
+            turn(0, of_group(back, g), 6 + g)
+        for piece in ((2, 0), (2, 1), (3, 0), (3, 1)):
+            turn_piece(0, piece)
+        quantise(0, of_group(front, 0))
+        quantise(0, of_group(front, 1))
+        gather(0, of_group(back, 0), SCALAR)
+        gather(0, of_group(back, 1), SCALAR)
+        quantise(0, of_group(back, 0))
+        overlaps(0, near, [0], near, front)
+        overlaps(0, near, [1], rts=front)
+        overlaps(0, near, [0], rts=back)
 
-        overlaps(1, range(0, 2), [0, 1], (0, 1))
-        for rt in range(ROW_TILES):
-            sort(1, [(rt, 2), (rt, 3)], SCALAR if rt < 2 else VECTOR)
+        sort(0, of_row_tile(0, high), VECTOR)
+        quantise(0, of_group(back, 1))
+        for rt in (1, 2):
+            sort(0, of_row_tile(rt, high), VECTOR)
+        sort(0, [(3, 3)], VECTOR)
         for c, rts in enumerate((front, back)):
-            for g in (2, 3):
-                for rt in rts:
-                    turn(1, g, rt, rts, 2 * c + g)
-                if (c, g) != (1, 2):
-                    gather(1, g, rts, SCALAR)
-        weigh(0, 6)
-        weigh(0, 7)
-        gather(1, 2, back, VECTOR)
-        for i, b in ((2, 6), (3, 7), (4, 2), (5, 3)):
-            overlaps(1, [i], [0, 1], (b,))
-        for g in (2, 3):
-            quantise(1, g, front)
-            quantise(1, g, back)
-        for j in range(HALVES):
-            interleave_coef(j, 0)
-            interleave_coef(j, 1)
-        quantise_coef(0, 0)
+            for g in high:
+                turn(0, of_group(rts, g), 2 + 2 * c + g)
+        for piece in ((0, 2), (0, 3), (1, 2)):
+            turn_piece(0, piece)
+        gather(0, of_group(front, 2), SCALAR)
+        turn_piece(0, (1, 3))
+        gather(0, of_group(front, 3), VECTOR)
+        for piece in ((2, 2), (2, 3), (3, 2), (3, 3)):
+            turn_piece(0, piece)
+        gather(0, of_group(back, 2), SCALAR)
+        gather(0, of_group(back, 3), SCALAR)
+        for rts in (front, back):
+            for g in high:
+                quantise(0, of_group(rts, g))
+        overlaps(0, near, [1], rts=back)
+        overlaps(0, near, high, rts=front)
+        for i in near:
+            overlaps(0, [i], high, rts=back)
+        for i in near:
+            weigh(i)
 
-        overlaps(1, range(0, 2), [2, 3])
-        for i in range(2, 6):
-            overlaps(1, [i], [2, 3])
-        quantise_coef(0, 1)
-        weigh(1, 0)
-        for i in range(1, 4):
-            weigh(1, i)
-        turn_h(0, (0, 1), 4)
-        turn_h(0, (2, 3), 5)
-        turn_h(1, (0, 1), 0)
-        turn_h(1, (2, 3), 1)
+        overlaps(0, far, low, far)
+        for i in (4, 5):
+            overlaps(0, [i], high)
+        sort(1, of_row_tile(0, low), SCALAR)
+        sort(1, of_row_tile(1, low), SCALAR)
+        sort(1, of_row_tile(0, high), SCALAR)
+        sort(1, [(1, 3)], VECTOR)
+        for g in range(GROUPS):
+            turn(1, of_group(front, g), g)
+        for groups in (low, high):
+            for piece in ((0, groups[0]), (1, groups[0])):
+                turn_piece(1, piece)
+            gather(1, of_group(front, groups[0]), SCALAR)
+            for piece in ((0, groups[1]), (1, groups[1])):
+                turn_piece(1, piece)
+            gather(1, of_group(front, groups[1]), VECTOR if groups == low else SCALAR)
+        for g in range(GROUPS):
+            quantise(1, of_group(front, g))
+        for i in (6, 7):
+            overlaps(0, [i], high)
+        for i in far:
+            weigh(i)
+        for b, tiles in enumerate(((4, 5), (6, 7), (0, 1))):
+            strip(0, tiles, b)
+
+        sort(1, of_row_tile(2, low), SCALAR)
+        sort(1, of_row_tile(2, high), SCALAR)
+        sort(1, of_row_tile(3, low), SCALAR)
+        weigh_strip(0, (4, 5))
+        weigh_strip(0, (6, 7))
+        sort(1, of_row_tile(3, high), VECTOR)
+        for rt in back:
+            for c, groups in enumerate((low, high)):
+                turn(1, of_row_tile(rt, groups), 2 * rt + c)
+                for piece in of_row_tile(rt, groups):
+                    turn_piece(1, piece)
+                gather(1, of_row_tile(rt, groups), VECTOR if (rt, c) == (2, 1) else SCALAR)
+        for rt in back:
+            for g in range(GROUPS):
+                quantise(1, [(rt, g)])
+        strip(0, (2, 3), 3)
+        interleave_coef(0, 0)
+        interleave_coef(0, 1)
+        interleave_coef(1, 0)
+        strip(1, (4, 5), 4)
+        strip(1, (6, 7), 5)
+        weigh_strip(0, (0, 1))
+        weigh_strip(0, (2, 3))
+        weigh_strip(1, (4, 5))
+        interleave_coef(1, 1, VECTOR)
+        weigh_strip(1, (6, 7))
         turn_h(0, (4, 5), 6)
-        turn_h(0, (6, 7), 7)
-        weigh(1, 4)
+        turn_h(1, (4, 5), 7)
+        turn_h(0, (6, 7), 0)
+        turn_h(0, (0, 1), 1)
+        turn_h(0, (2, 3), 2)
+        turn_h(1, (6, 7), 4)
+        gather_h(0, (4, 5))
+        gather_h(1, (4, 5))
+        gather_h(0, (6, 7))
+        gather_h(0, (0, 1))
+        gather_h(1, (6, 7))
+        gather_h(0, (2, 3))
+        quantise_coef(0, 0)
+        quantise_coef(0, 1)
         quantise_coef(1, 0)
-        quantise_coef(1, 1)
-        weigh(1, 5)
-        overlaps(1, [6], range(GROUPS), (2,))
-        quantise_h(0, (0, 1))
-        quantise_h(1, (0, 1))
-        quantise_h(0, (2, 3))
-        quantise_h(1, (2, 3))
-        weigh(1, 6)
-        mix(0, 3)
-        mix(1, 4)
-        turn_h(1, (4, 5), 5)
-        turn_h(1, (6,), 0)
         quantise_h(0, (4, 5))
-        quantise_h(0, (6, 7))
-        store(0)
-        store(1)
-        mix(2, 1)
-        mix(3, 6)
-        overlaps(1, [7], range(GROUPS), (7,))
-        store(2)
+        quantise_coef(1, 1)
         quantise_h(1, (4, 5))
-        quantise_h(1, (6,))
-        store(3)
-        weigh(1, 7)
-        mix(4, 2)
-        mix(5, 3)
-        turn_h(1, (7,), 4)
+        quantise_h(0, (6, 7))
+        quantise_h(0, (0, 1))
+        strip(1, (0, 1), 5)
+        mix(4, (3,))
+        strip(1, (2,), 6)
+        weigh_strip(1, (0, 1))
         store(4)
-        mix(6, 5)
+        weigh_strip(1, (2,))
+        mix(5, (7,))
+        turn_h(1, (0, 1), 0)
+        turn_h(1, (2,), 1)
+        turn_h(1, (3,), 4, range(0, 1))
+        gather_h(1, (0, 1))
+        gather_h(1, (2,))
+        quantise_h(1, (6, 7))
         store(5)
-        quantise_h(1, (7,))
-        mix(7, 0)
+        mix(6, (5,))
+        mix(7, (3,))
+        quantise_h(0, (2, 3))
+        quantise_h(1, (0, 1))
         store(6)
-        store(7, parts=2)
+        quantise_h(1, (2,))
+        store(7)
+        mix(0, (2,))
+        strip(1, (3,), 6)
+        weigh_strip(1, (3,))
+        store(0)
+        mix(1, (7,))
+        turn_h(1, (3,), 4, range(1, 2))
+        gather_h(1, (3,))
+        store(1)
+        mix(2, (0, 1))
+        quantise_h(1, (3,))
+        mix(3, (5, 3))
+        store(2, 0)
+        store(2, 1)
+        store(3, 0)
+        store(3, 1)

@@ -60,15 +60,26 @@ def tile_weighted_diis_residuals_e3_kernel(tc, g_words, g_scales, errs, pair, co
         make_identity(nc, ident[:])
         lam_sb = sb([P, R], BF16, "lam_sb")
 
+        front, back = range(0, 2), range(2, 4)
+        near, far = range(0, 4), range(4, 8)
+        low, high = range(0, 2), range(2, 4)
+        first_half, second_half = range(0, 1), range(1, 2)
+
         raw_words, g_code, g_plane, plane_tile, pair_sb, coef_raw = {}, {}, {}, {}, {}, {}
 
-        def load_errs(j, groups, rt):
-            t = sb([P, len(groups) * PASS], BF16, f"errs{j}{rt}{groups[0]}")
-            u, h = divmod(rt, 2)
-            first = j * PASS + h * 2 * P + u
-            nc.sync.dma_start(out=t[:], in_=errs[first : first + 2 * P - 1 : 2, groups.start * PASS : groups.stop * PASS])
+        def load_errs(groups, rt):
+            t = sb([P, len(groups) * PASS], BF16, f"errs0{rt}{groups[0]}")
+            nc.sync.dma_start(out=t[:], in_=errs[rt * P : (rt + 1) * P, groups.start * PASS : groups.stop * PASS])
             for b, g in enumerate(groups):
-                raw_words[j, rt, g] = (t[:].bitcast(F32), b)
+                raw_words[0, rt, g] = (t[:].bitcast(F32), b)
+
+        def load_strip(h, groups):
+            t = sb([P, 2 * len(groups) * PASS], BF16, f"errs1{h}{groups[0]}")
+            rows = errs[PASS + h * 2 * P : PASS + (h + 1) * 2 * P, groups.start * PASS : groups.stop * PASS]
+            nc.sync.dma_start(out=t[:].rearrange("p (u k) -> p u k", u=2), in_=rows.rearrange("(p u) k -> p u k", u=2))
+            for u in range(2):
+                for b, g in enumerate(groups):
+                    raw_words[1, 2 * h + u, g] = (t[:].bitcast(F32), u * len(groups) + b)
 
         def load_g(groups, tiles):
             t = sb([P, len(groups), len(tiles) * P], U32, f"g_code{groups[0]}{tiles[0]}")
@@ -164,7 +175,7 @@ def tile_weighted_diis_residuals_e3_kernel(tc, g_words, g_scales, errs, pair, co
         def of_row_tile(rt, groups):
             return [(rt, g) for g in groups]
 
-        b_acc, strip_acc, h_sb, h_bank, h_quads, h_code = {}, {}, {}, {}, {}, {}
+        b_acc, strip_acc, h_place, h_sb, h_bank, h_quads, h_code = {}, {}, {}, {}, {}, {}, {}
 
         def overlaps(j, tiles, groups, banks=None, rts=range(ROW_TILES)):
             cols = slice(rts.start * P, rts.stop * P)
@@ -176,39 +187,60 @@ def tile_weighted_diis_residuals_e3_kernel(tc, g_words, g_scales, errs, pair, co
                         b_acc[j, i] = bank(banks[a], [P, PASS])
                     mx_pass(b_acc[j, i][:, cols], g_code[i, g], g_plane[i, g], errs_code[j, g][:, cols], errs_plane[j, g][:, cols], first, last)
 
-        def strip(u, tiles, b):
-            acc = bank(b, [P, len(tiles), 2 * P])
-            strip_acc[u, tiles] = acc
-            cols = slice(u * 2 * P, (u + 1) * 2 * P)
-            for g in range(GROUPS):
+        def strip(h, tiles, b, groups=range(GROUPS)):
+            if groups[0] == 0:
+                strip_acc[h, tiles] = bank(b, [P, len(tiles), 2 * P])
+            cols = slice(h * 2 * P, (h + 1) * 2 * P)
+            for g in groups:
                 for a, i in enumerate(tiles):
                     first, last = (g, a) == (0, 0), (g, a) == (GROUPS - 1, len(tiles) - 1)
-                    mx_pass(acc[:, a, :], g_code[i, g], g_plane[i, g], errs_code[1, g][:, cols], errs_plane[1, g][:, cols], first, last)
+                    acc = strip_acc[h, tiles][:, a, :]
+                    mx_pass(acc, g_code[i, g], g_plane[i, g], errs_code[1, g][:, cols], errs_plane[1, g][:, cols], first, last)
 
         def weigh(i):
             t, a = pair_sb[0, i]
-            h = sb([P, 2, 2 * P], BF16, f"h0{i}")
+            h = sb([P, PASS], BF16, f"h0{i}")
             nc.vector.tensor_tensor(
-                out=h[:],
-                in0=b_acc[0, i][:].rearrange("p (u c) -> p u c", u=2),
-                in1=t[:, a, :].rearrange("p (c u) -> p u c", u=2),
+                out=h[:].rearrange("p (u w e) -> p u w e", u=2, e=2),
+                in0=b_acc[0, i][:].rearrange("p (w u e) -> p u w e", u=2, e=2),
+                in1=t[:, a, :].rearrange("p (w u e) -> p u w e", u=2, e=2),
                 op=ALU.mult,
             )
             for u in range(2):
-                h_sb[0, i, u] = h[:, u, :]
+                h_sb[0, i, u] = h[:, u * 2 * P : (u + 1) * 2 * P]
 
-        def weigh_strip(u, tiles):
+        def weigh_strip(h, tiles):
+            if h == 0:
+                both = sb([P, len(tiles), 2, 2, P], BF16, f"h1{tiles[0]}")
+                for a, i in enumerate(tiles):
+                    h_place[i] = (both, a)
+                    for u in range(2):
+                        h_sb[1, i, u] = both[:, a, u].rearrange("p h c -> p (h c)")
+            both, first = h_place[tiles[0]]
             t, a = pair_sb[1, tiles[0]]
-            h = sb([P, len(tiles), 2 * P], BF16, f"h1{tiles[0]}{u}")
-            nc.vector.tensor_tensor(out=h[:], in0=strip_acc[u, tiles][:], in1=t[:, a : a + len(tiles), u:PASS:2], op=ALU.mult)
-            for a, i in enumerate(tiles):
-                h_sb[1, i, u] = h[:, a, :]
+            nc.vector.tensor_tensor(
+                out=both[:, first : first + len(tiles), :, h, :],
+                in0=strip_acc[h, tiles][:].rearrange("p a (u c) -> p a u c", u=2),
+                in1=t[:, a : a + len(tiles), h * 2 * P : (h + 1) * 2 * P].rearrange("p a (c u) -> p a u c", u=2),
+                op=ALU.mult,
+            )
 
-        def turn_h(j, tiles, b, parities=range(2)):
-            if parities[0] == 0:
-                h_bank[j, tiles] = bank(b, [P, 4, P])
+        def weigh_whole(i):
+            both = sb([P, 2, 2, P], BF16, f"h1{i}")
+            for u in range(2):
+                h_sb[1, i, u] = both[:, u].rearrange("p h c -> p (h c)")
+            t, a = pair_sb[1, i]
+            nc.vector.tensor_tensor(
+                out=both[:].rearrange("p u h c -> p h u c"),
+                in0=b_acc[1, i][:].rearrange("p (h u c) -> p h u c", h=2, u=2),
+                in1=t[:, a, :].rearrange("p (h c u) -> p h u c", h=2, u=2),
+                op=ALU.mult,
+            )
+
+        def turn_h(j, tiles, b):
+            h_bank[j, tiles] = bank(b, [P, 4, P])
             for a, i in enumerate(tiles):
-                for u in parities:
+                for u in range(2):
                     nc.tensor.transpose(h_bank[j, tiles][:, 2 * a + u, :], h_sb[j, i, u].bitcast(F32), ident[:])
 
         def gather_h(j, tiles, engine=SCALAR):
@@ -225,10 +257,11 @@ def tile_weighted_diis_residuals_e3_kernel(tc, g_words, g_scales, errs, pair, co
 
         def interleave_coef(j, c, engine=SCALAR):
             coef_quads[j, c] = sb([P, R // 2, 4], BF16, f"coef_quads{j}{c}")
+            rows = "(u e)" if j == 0 else "(e u)"
             move(
                 engine,
                 coef_quads[j, c][:].rearrange("p (a i) (u e) -> p a u e i", i=4, u=2),
-                coef_raw[j][:, :, c * R // 2 : (c + 1) * R // 2].rearrange("p (e u) (a i) -> p a u e i", i=4, u=2),
+                coef_raw[j][:, :, c * R // 2 : (c + 1) * R // 2].rearrange(f"p {rows} (a i) -> p a u e i", i=4, u=2),
             )
 
         def quantise_coef(j, c):
@@ -260,6 +293,7 @@ def tile_weighted_diis_residuals_e3_kernel(tc, g_words, g_scales, errs, pair, co
             nc.vector.tensor_tensor(out=res[:], in0=acc[:], in1=lam_sb[:, cols], op=ALU.subtract)
             nc.sync.dma_start(out=out[i * P : (i + 1) * P, cols], in_=res[:])
 
+        clear_plane(high, near)
         zero_words = 64
         blank = sb([P, zero_words + (P + PASS) + (P + PASS) // 4], U32, "blank")
         nc.vector.memset(blank[:], 0)
@@ -275,43 +309,39 @@ def tile_weighted_diis_residuals_e3_kernel(tc, g_words, g_scales, errs, pair, co
             for n in range(count):
                 mx_pass(t[:], warm_code[:, :P], warm_plane[:, :P], warm_code[:, P:], warm_plane[:, P:], True, True)
 
-        front, back = range(0, 2), range(2, 4)
-        near, far = range(0, 4), range(4, 8)
-        low, high = range(0, 2), range(2, 4)
         clear_plane(low, near)
-        clear_plane(high, near)
         clear_plane(range(GROUPS), far)
 
-        def load_quarter(j, groups):
+        def load_quarter(groups):
             for rt in range(ROW_TILES):
-                load_errs(j, groups, rt)
+                load_errs(groups, rt)
 
-        load_quarter(0, low)
+        load_quarter(low)
         load_scales(low, near, nc.sync)
+        load_scales(high, near, nc.gpsimd)
+        load_scales(range(GROUPS), far, nc.gpsimd)
         load_g(range(0, 1), near)
         load_g(range(1, 2), near)
-        load_quarter(0, high)
-        load_scales(high, near, nc.sync)
+        load_quarter(high)
         load_g(range(2, 3), near)
         load_g(range(3, 4), near)
-        load_scales(range(GROUPS), far, nc.sync)
+        load_strip(0, low)
+        load_strip(0, high)
+        load_pair(first_half, near)
         load_g(low, far)
-        load_pair(range(0, 1), near)
-        load_g(high, range(4, 6))
-        for groups in (low, high):
-            for rt in front:
-                load_errs(1, groups, rt)
-        load_g(high, range(6, 8))
-        load_pair(range(HALVES), range(4, 6))
-        load_pair(range(HALVES), range(6, 8))
-        for rt in back:
-            load_errs(1, range(GROUPS), rt)
-        load_pair(range(1, 2), near)
+        load_g(high, far)
+        load_pair(first_half, range(4, 7))
+        load_strip(1, low)
+        load_strip(1, high)
+        load_pair(second_half, near)
         load_coef(0)
+        load_pair(first_half, range(7, 8))
+        load_pair(second_half, range(4, 6))
         load_coef(1)
+        load_pair(second_half, range(6, 8))
         nc.sync.dma_start(out=lam_sb[:], in_=lam.partition_broadcast(P))
 
-        warm_up(3, 0)
+        warm_up(4, 0)
         for rt in range(3):
             sort(0, of_row_tile(rt, low), VECTOR)
         sort(0, [(3, 1)], VECTOR)
@@ -320,11 +350,11 @@ def tile_weighted_diis_residuals_e3_kernel(tc, g_words, g_scales, errs, pair, co
             for piece in of_group(front, g):
                 turn_piece(0, piece)
             gather(0, of_group(front, g), SCALAR)
-        warm_up(1, 1)
         for g in low:
             turn(0, of_group(back, g), 6 + g)
         for piece in ((2, 0), (2, 1), (3, 0), (3, 1)):
             turn_piece(0, piece)
+        warm_up(1, 1)
         quantise(0, of_group(front, 0))
         quantise(0, of_group(front, 1))
         gather(0, of_group(back, 0), SCALAR)
@@ -338,7 +368,6 @@ def tile_weighted_diis_residuals_e3_kernel(tc, g_words, g_scales, errs, pair, co
         quantise(0, of_group(back, 1))
         for rt in (1, 2):
             sort(0, of_row_tile(rt, high), VECTOR)
-        sort(0, [(3, 3)], VECTOR)
         for c, rts in enumerate((front, back)):
             for g in high:
                 turn(0, of_group(rts, g), 2 + 2 * c + g)
@@ -346,125 +375,114 @@ def tile_weighted_diis_residuals_e3_kernel(tc, g_words, g_scales, errs, pair, co
             turn_piece(0, piece)
         gather(0, of_group(front, 2), SCALAR)
         turn_piece(0, (1, 3))
-        gather(0, of_group(front, 3), VECTOR)
+        gather(0, of_group(front, 3), SCALAR)
+        sort(0, [(3, 3)], VECTOR)
+        overlaps(0, near, [1], rts=back)
         for piece in ((2, 2), (2, 3), (3, 2), (3, 3)):
             turn_piece(0, piece)
-        gather(0, of_group(back, 2), SCALAR)
+        for g in high:
+            quantise(0, of_group(front, g))
+        gather(0, of_group(back, 2), VECTOR)
         gather(0, of_group(back, 3), SCALAR)
-        for rts in (front, back):
-            for g in high:
-                quantise(0, of_group(rts, g))
-        overlaps(0, near, [1], rts=back)
+        for g in high:
+            quantise(0, of_group(back, g))
         overlaps(0, near, high, rts=front)
-        for i in near:
-            overlaps(0, [i], high, rts=back)
-        for i in near:
-            weigh(i)
+        overlaps(0, near, [2], rts=back)
 
-        overlaps(0, far, low, far)
-        for i in (4, 5):
-            overlaps(0, [i], high)
         sort(1, of_row_tile(0, low), SCALAR)
-        sort(1, of_row_tile(1, low), SCALAR)
-        sort(1, of_row_tile(0, high), SCALAR)
+        sort(1, of_row_tile(1, low), VECTOR)
+        sort(1, [(0, 3)], VECTOR)
         sort(1, [(1, 3)], VECTOR)
         for g in range(GROUPS):
-            turn(1, of_group(front, g), g)
-        for groups in (low, high):
-            for piece in ((0, groups[0]), (1, groups[0])):
+            turn(1, of_group(front, g), 4 + g)
+            for piece in of_group(front, g):
                 turn_piece(1, piece)
-            gather(1, of_group(front, groups[0]), SCALAR)
-            for piece in ((0, groups[1]), (1, groups[1])):
-                turn_piece(1, piece)
-            gather(1, of_group(front, groups[1]), VECTOR if groups == low else SCALAR)
+            gather(1, of_group(front, g), VECTOR if g == 1 else SCALAR)
         for g in range(GROUPS):
             quantise(1, of_group(front, g))
-        for i in (6, 7):
-            overlaps(0, [i], high)
-        for i in far:
+        overlaps(0, near, [3], rts=back)
+        for i in near:
             weigh(i)
-        for b, tiles in enumerate(((4, 5), (6, 7), (0, 1))):
-            strip(0, tiles, b)
+        for g in range(GROUPS):
+            strip(0, (0, 1), 4, [g])
+            strip(0, (2, 3), 5, [g])
 
+        overlaps(0, range(4, 7), low, (6, 7, 0))
+        for i in range(4, 7):
+            overlaps(0, [i], high)
+            weigh(i)
+        strip(0, (4, 5), 1)
         sort(1, of_row_tile(2, low), SCALAR)
-        sort(1, of_row_tile(2, high), SCALAR)
         sort(1, of_row_tile(3, low), SCALAR)
-        weigh_strip(0, (4, 5))
-        weigh_strip(0, (6, 7))
+        sort(1, of_row_tile(2, high), SCALAR)
         sort(1, of_row_tile(3, high), VECTOR)
-        for rt in back:
-            for c, groups in enumerate((low, high)):
-                turn(1, of_row_tile(rt, groups), 2 * rt + c)
-                for piece in of_row_tile(rt, groups):
-                    turn_piece(1, piece)
-                gather(1, of_row_tile(rt, groups), VECTOR if (rt, c) == (2, 1) else SCALAR)
-        for rt in back:
-            for g in range(GROUPS):
-                quantise(1, [(rt, g)])
-        strip(0, (2, 3), 3)
-        interleave_coef(0, 0)
-        interleave_coef(0, 1)
-        interleave_coef(1, 0)
-        strip(1, (4, 5), 4)
-        strip(1, (6, 7), 5)
+        for g, b in enumerate((2, 6, 7, 0)):
+            turn(1, of_group(back, g), b)
+            for piece in of_group(back, g):
+                turn_piece(1, piece)
+            gather(1, of_group(back, g), VECTOR if g == 1 else SCALAR)
+        for g in range(GROUPS):
+            quantise(1, of_group(back, g))
+        overlaps(0, [7], range(GROUPS), (3,))
+        for j in range(HALVES):
+            interleave_coef(j, 0)
+            interleave_coef(j, 1)
+        strip(1, (0, 1), 2)
+        strip(1, (2, 3), 6)
+        strip(1, (4, 5), 7)
         weigh_strip(0, (0, 1))
         weigh_strip(0, (2, 3))
-        weigh_strip(1, (4, 5))
-        interleave_coef(1, 1, VECTOR)
-        weigh_strip(1, (6, 7))
-        turn_h(0, (4, 5), 6)
-        turn_h(1, (4, 5), 7)
-        turn_h(0, (6, 7), 0)
-        turn_h(0, (0, 1), 1)
-        turn_h(0, (2, 3), 2)
-        turn_h(1, (6, 7), 4)
-        gather_h(0, (4, 5))
-        gather_h(1, (4, 5))
-        gather_h(0, (6, 7))
-        gather_h(0, (0, 1))
-        gather_h(1, (6, 7))
-        gather_h(0, (2, 3))
+        weigh_strip(1, (0, 1))
+        weigh(7)
+        weigh_strip(1, (2, 3))
+        weigh_strip(0, (4, 5))
+
+        turn_h(0, (0, 1), 0)
+        turn_h(1, (0, 1), 4)
+        turn_h(0, (2, 3), 5)
+        turn_h(0, (4, 5), 2)
+        turn_h(0, (6, 7), 3)
+        turn_h(1, (2, 3), 6)
+        for j, tiles in ((0, (0, 1)), (1, (0, 1)), (0, (2, 3)), (1, (2, 3)), (0, (4, 5)), (0, (6, 7))):
+            gather_h(j, tiles)
         quantise_coef(0, 0)
         quantise_coef(0, 1)
+        weigh_strip(1, (4, 5))
         quantise_coef(1, 0)
-        quantise_h(0, (4, 5))
         quantise_coef(1, 1)
-        quantise_h(1, (4, 5))
-        quantise_h(0, (6, 7))
+        overlaps(1, [6], range(GROUPS), (1,))
         quantise_h(0, (0, 1))
-        strip(1, (0, 1), 5)
-        mix(4, (3,))
-        strip(1, (2,), 6)
-        weigh_strip(1, (0, 1))
-        store(4)
-        weigh_strip(1, (2,))
-        mix(5, (7,))
-        turn_h(1, (0, 1), 0)
-        turn_h(1, (2,), 1)
-        turn_h(1, (3,), 4, range(0, 1))
-        gather_h(1, (0, 1))
-        gather_h(1, (2,))
-        quantise_h(1, (6, 7))
-        store(5)
-        mix(6, (5,))
-        mix(7, (3,))
-        quantise_h(0, (2, 3))
         quantise_h(1, (0, 1))
-        store(6)
-        quantise_h(1, (2,))
-        store(7)
-        mix(0, (2,))
-        strip(1, (3,), 6)
-        weigh_strip(1, (3,))
+        quantise_h(0, (2, 3))
+        quantise_h(1, (2, 3))
+        weigh_whole(6)
+        mix(0, (7,))
+        mix(1, (0,))
+        turn_h(1, (4, 5), 4)
+        turn_h(1, (6,), 5)
+        gather_h(1, (4, 5))
+        gather_h(1, (6,))
+        quantise_h(0, (4, 5))
+        quantise_h(0, (6, 7))
         store(0)
-        mix(1, (7,))
-        turn_h(1, (3,), 4, range(1, 2))
-        gather_h(1, (3,))
         store(1)
-        mix(2, (0, 1))
-        quantise_h(1, (3,))
-        mix(3, (5, 3))
-        store(2, 0)
-        store(2, 1)
-        store(3, 0)
-        store(3, 1)
+        mix(2, (6,))
+        mix(3, (2,))
+        overlaps(1, [7], range(GROUPS), (3,))
+        store(2)
+        quantise_h(1, (4, 5))
+        quantise_h(1, (6,))
+        store(3)
+        weigh_whole(7)
+        mix(4, (1,))
+        mix(5, (7,))
+        turn_h(1, (7,), 0)
+        gather_h(1, (7,))
+        store(4)
+        mix(6, (4,))
+        store(5)
+        quantise_h(1, (7,))
+        mix(7, (5, 6))
+        store(6)
+        store(7, 0)
+        store(7, 1)

@@ -1,3 +1,4 @@
+import math
 from contextlib import ExitStack
 
 import concourse.mybir as mybir
@@ -23,6 +24,7 @@ HALVES = M // PASS
 ROW_TILES = PASS // P
 STAGING = 8
 VECTOR, SCALAR = "vector", "scalar"
+MOVING, STATIONARY, MOVING_PLANE, STATIONARY_PLANE = 0, 64, 128, 192
 
 
 def tile_weighted_diis_residuals_e3_kernel(tc, g_words, g_scales, errs, pair, coef, lam, out):
@@ -35,6 +37,13 @@ def tile_weighted_diis_residuals_e3_kernel(tc, g_words, g_scales, errs, pair, co
 
         def sb(shape, dtype, name):
             return keep.tile(shape, dtype, align_bytes=64, name=name)
+
+        def placed(shape, dtype, name, past):
+            pad = past // (1 if dtype == U8 else 4)
+            t = keep.tile([P, pad + math.prod(shape[1:])], dtype, align_bytes=256, name=name)
+            if len(shape) == 2:
+                return t[:, pad:]
+            return t[:, pad:].rearrange("p (a b) -> p a b", a=shape[1])
 
         def bank(b, shape):
             return psum.tile(shape, F32, name=f"bank{b}", tag=f"bank{b}")
@@ -82,7 +91,7 @@ def tile_weighted_diis_residuals_e3_kernel(tc, g_words, g_scales, errs, pair, co
                     raw_words[1, 2 * h + u, g] = (t[:].bitcast(F32), u * len(groups) + b)
 
         def load_g(groups, tiles):
-            t = sb([P, len(groups), len(tiles) * P], U32, f"g_code{groups[0]}{tiles[0]}")
+            t = placed([P, len(groups), len(tiles) * P], U32, f"g_code{groups[0]}{tiles[0]}", STATIONARY)
             as_bytes = g_words[groups.start : groups.stop].rearrange("g p n t -> p g (n t)")
             nc.sync.dma_start(out=t[:].bitcast(I32), in_=as_bytes[:, :, tiles.start * 4 * P : tiles.stop * 4 * P].bitcast(I32))
             for a, g in enumerate(groups):
@@ -90,7 +99,7 @@ def tile_weighted_diis_residuals_e3_kernel(tc, g_words, g_scales, errs, pair, co
                     g_code[i, g] = t[:, a, b * P : (b + 1) * P]
 
         def clear_plane(groups, tiles):
-            t = sb([P, len(groups), len(tiles) * P], U8, f"g_plane{groups[0]}{tiles[0]}")
+            t = placed([P, len(groups), len(tiles) * P], U8, f"g_plane{groups[0]}{tiles[0]}", STATIONARY_PLANE)
             nc.vector.memset(t[:].bitcast(I32), 0)
             plane_tile[groups, tiles] = t
             for a, g in enumerate(groups):
@@ -161,8 +170,8 @@ def tile_weighted_diis_residuals_e3_kernel(tc, g_words, g_scales, errs, pair, co
         def quantise(j, pieces):
             rt, g = pieces[0]
             if (j, g) not in errs_code:
-                errs_code[j, g] = sb([P, PASS], U32, f"errs_code{j}{g}")
-                errs_plane[j, g] = sb([P, PASS], U8, f"errs_plane{j}{g}")
+                errs_code[j, g] = placed([P, PASS], U32, f"errs_code{j}{g}", MOVING)
+                errs_plane[j, g] = placed([P, PASS], U8, f"errs_plane{j}{g}", MOVING_PLANE)
             cols = slice(rt * P, (rt + len(pieces)) * P)
             quads, c = errs_quads[j, pieces[0]]
             nc.vector.quantize_mx(
@@ -247,8 +256,8 @@ def tile_weighted_diis_residuals_e3_kernel(tc, g_words, g_scales, errs, pair, co
             h_quads[j, tiles] = gathered(engine, h_bank[j, tiles][:, : 2 * len(tiles), :], len(tiles))
 
         def quantise_h(j, tiles):
-            code = sb([P, len(tiles) * P], U32, f"h_code{j}{tiles[0]}")
-            plane = sb([P, len(tiles) * P], U8, f"h_plane{j}{tiles[0]}")
+            code = placed([P, len(tiles) * P], U32, f"h_code{j}{tiles[0]}", STATIONARY)
+            plane = placed([P, len(tiles) * P], U8, f"h_plane{j}{tiles[0]}", STATIONARY_PLANE)
             nc.vector.quantize_mx(out=code[:].bitcast(E5M2X4), scales=plane[:], in_=h_quads[j, tiles])
             for a, i in enumerate(tiles):
                 h_code[j, i] = (code[:, a * P : (a + 1) * P], plane[:, a * P : (a + 1) * P])
@@ -266,8 +275,8 @@ def tile_weighted_diis_residuals_e3_kernel(tc, g_words, g_scales, errs, pair, co
 
         def quantise_coef(j, c):
             if c == 0:
-                coef_code[j] = sb([P, R], U32, f"coef_code{j}")
-                coef_plane[j] = sb([P, R], U8, f"coef_plane{j}")
+                coef_code[j] = placed([P, R], U32, f"coef_code{j}", MOVING)
+                coef_plane[j] = placed([P, R], U8, f"coef_plane{j}", MOVING_PLANE)
             cols = slice(c * R // 2, (c + 1) * R // 2)
             nc.vector.quantize_mx(
                 out=coef_code[j][:, cols].bitcast(E4M3X4),

@@ -136,6 +136,13 @@ def tile_weighted_diis_residuals_e3_kernel(tc, g_words, g_scales, errs, pair, co
             for a, (rt, g) in enumerate(pieces):
                 sorted_words[j, rt, g] = t[:, a]
 
+        def sort_group(j, rts, g, engine):
+            t = stage.tile([P, 2, 2, P], F32, align_bytes=64, name="sorted")
+            words, place = raw_words[j, rts[0], g]
+            move(engine, t[:], words.rearrange("p (a b w u) -> p a b u w", a=2, b=2, u=2)[:, :, place])
+            for a, rt in enumerate(rts):
+                sorted_words[j, rt, g] = t[:, a]
+
         def turn(j, pieces, b):
             t = bank(b, [P, 4, P])
             for a, piece in enumerate(pieces):
@@ -184,6 +191,7 @@ def tile_weighted_diis_residuals_e3_kernel(tc, g_words, g_scales, errs, pair, co
         def of_row_tile(rt, groups):
             return [(rt, g) for g in groups]
 
+        held = {}
         b_acc, strip_acc, h_place, h_sb, h_bank, h_quads, h_code = {}, {}, {}, {}, {}, {}, {}
 
         def overlaps(j, tiles, groups, banks=None, rts=range(ROW_TILES)):
@@ -233,6 +241,23 @@ def tile_weighted_diis_residuals_e3_kernel(tc, g_words, g_scales, errs, pair, co
                 in1=t[:, a : a + len(tiles), h * 2 * P : (h + 1) * 2 * P].rearrange("p a (c u) -> p a u c", u=2),
                 op=ALU.mult,
             )
+
+        def hold_strip(tiles):
+            held[tiles] = sb([P, len(tiles), 2 * P], F32, f"held{tiles[0]}")
+            nc.scalar.copy(out=held[tiles][:], in_=strip_acc[0, tiles][:])
+
+        def weigh_held(tiles, both):
+            t, first = pair_sb[1, tiles[0]]
+            for a, i in enumerate(tiles):
+                h_place[i] = (both, a)
+                for u in range(2):
+                    h_sb[1, i, u] = both[:, a, u].rearrange("p h c -> p (h c)")
+                nc.gpsimd.tensor_tensor(
+                    out=both[:, a, :, 0, :],
+                    in0=held[tiles][:, a, :].rearrange("p (u c) -> p u c", u=2),
+                    in1=t[:, first + a, : 2 * P].rearrange("p (c u) -> p u c", u=2),
+                    op=ALU.mult,
+                )
 
         def weigh_whole(i):
             both = sb([P, 2, 2, P], BF16, f"h1{i}")
@@ -339,12 +364,12 @@ def tile_weighted_diis_residuals_e3_kernel(tc, g_words, g_scales, errs, pair, co
         load_pair(first_half, near)
         load_g(low, far)
         load_g(high, far)
-        load_pair(first_half, range(4, 7))
+        load_pair(first_half, range(4, 6))
         load_strip(1, low)
         load_strip(1, high)
         load_pair(second_half, near)
         load_coef(0)
-        load_pair(first_half, range(7, 8))
+        load_pair(first_half, range(6, 8))
         load_pair(second_half, range(4, 6))
         load_coef(1)
         load_pair(second_half, range(6, 8))
@@ -385,23 +410,25 @@ def tile_weighted_diis_residuals_e3_kernel(tc, g_words, g_scales, errs, pair, co
         gather(0, of_group(front, 2), SCALAR)
         turn_piece(0, (1, 3))
         gather(0, of_group(front, 3), SCALAR)
+        sort(0, [(3, 2)], VECTOR)
         sort(0, [(3, 3)], VECTOR)
         overlaps(0, near, [1], rts=back)
-        for piece in ((2, 2), (2, 3), (3, 2), (3, 3)):
+        for piece in ((2, 2), (3, 2), (2, 3), (3, 3)):
             turn_piece(0, piece)
         for g in high:
             quantise(0, of_group(front, g))
-        gather(0, of_group(back, 2), VECTOR)
+        gather(0, of_group(back, 2), SCALAR)
         gather(0, of_group(back, 3), SCALAR)
-        for g in high:
-            quantise(0, of_group(back, g))
+        quantise(0, of_group(back, 2))
         overlaps(0, near, high, rts=front)
         overlaps(0, near, [2], rts=back)
 
-        sort(1, of_row_tile(0, low), SCALAR)
+        sort(1, of_row_tile(0, low), VECTOR)
         sort(1, of_row_tile(1, low), VECTOR)
-        sort(1, [(0, 3)], VECTOR)
-        sort(1, [(1, 3)], VECTOR)
+        quantise(0, of_group(back, 3))
+        sort(1, [(0, 2)], VECTOR)
+        sort(1, [(1, 2)], SCALAR)
+        sort_group(1, front, 3, VECTOR)
         for g in range(GROUPS):
             turn(1, of_group(front, g), 4 + g)
             for piece in of_group(front, g):
@@ -419,13 +446,16 @@ def tile_weighted_diis_residuals_e3_kernel(tc, g_words, g_scales, errs, pair, co
         overlaps(0, range(4, 7), low, (6, 7, 0))
         for i in range(4, 7):
             overlaps(0, [i], high)
-            weigh(i)
+        weigh(4)
+        weigh(5)
         strip(0, (4, 5), 1)
+        hold_strip((0, 1))
+        hold_strip((2, 3))
         sort(1, of_row_tile(2, low), SCALAR)
         sort(1, of_row_tile(3, low), SCALAR)
         sort(1, of_row_tile(2, high), SCALAR)
         sort(1, of_row_tile(3, high), VECTOR)
-        for g, b in enumerate((2, 6, 7, 0)):
+        for g, b in enumerate((2, 4, 5, 6)):
             turn(1, of_group(back, g), b)
             for piece in of_group(back, g):
                 turn_piece(1, piece)
@@ -437,21 +467,23 @@ def tile_weighted_diis_residuals_e3_kernel(tc, g_words, g_scales, errs, pair, co
             interleave_coef(j, 0)
             interleave_coef(j, 1)
         strip(1, (0, 1), 2)
-        strip(1, (2, 3), 6)
+        strip(1, (2, 3), 4)
         strip(1, (4, 5), 7)
-        weigh_strip(0, (0, 1))
-        weigh_strip(0, (2, 3))
-        weigh_strip(1, (0, 1))
+        spent = errs_quads[1, (2, 3)][0].rearrange("p (a u h c) -> p a u h c", a=2, u=2, h=2)
+        weigh_held((0, 1), spent)
+        weigh_held((2, 3), sb([P, 2, 2, 2, P], BF16, "h12"))
+        weigh(6)
         weigh(7)
-        weigh_strip(1, (2, 3))
+        weigh_strip(1, (0, 1))
         weigh_strip(0, (4, 5))
+        weigh_strip(1, (2, 3))
 
-        turn_h(0, (0, 1), 0)
-        turn_h(1, (0, 1), 4)
-        turn_h(0, (2, 3), 5)
+        turn_h(0, (0, 1), 5)
+        turn_h(1, (0, 1), 6)
+        turn_h(0, (2, 3), 0)
         turn_h(0, (4, 5), 2)
         turn_h(0, (6, 7), 3)
-        turn_h(1, (2, 3), 6)
+        turn_h(1, (2, 3), 4)
         for j, tiles in ((0, (0, 1)), (1, (0, 1)), (0, (2, 3)), (1, (2, 3)), (0, (4, 5)), (0, (6, 7))):
             gather_h(j, tiles)
         quantise_coef(0, 0)
@@ -466,16 +498,16 @@ def tile_weighted_diis_residuals_e3_kernel(tc, g_words, g_scales, errs, pair, co
         quantise_h(1, (2, 3))
         weigh_whole(6)
         mix(0, (7,))
-        mix(1, (0,))
-        turn_h(1, (4, 5), 4)
-        turn_h(1, (6,), 5)
+        mix(1, (5,))
+        turn_h(1, (4, 5), 6)
+        turn_h(1, (6,), 0)
         gather_h(1, (4, 5))
         gather_h(1, (6,))
         quantise_h(0, (4, 5))
         quantise_h(0, (6, 7))
         store(0)
         store(1)
-        mix(2, (6,))
+        mix(2, (4,))
         mix(3, (2,))
         overlaps(1, [7], range(GROUPS), (3,))
         store(2)
@@ -485,13 +517,13 @@ def tile_weighted_diis_residuals_e3_kernel(tc, g_words, g_scales, errs, pair, co
         weigh_whole(7)
         mix(4, (1,))
         mix(5, (7,))
-        turn_h(1, (7,), 0)
+        turn_h(1, (7,), 5)
         gather_h(1, (7,))
         store(4)
-        mix(6, (4,))
+        mix(6, (6,))
         store(5)
         quantise_h(1, (7,))
-        mix(7, (5, 6))
+        mix(7, (0, 4))
         store(6)
         store(7, 0)
         store(7, 1)

import math
from contextlib import ExitStack

import concourse.mybir as mybir
from concourse.masks import make_identity

M, K, R = 1024, 2048, 512
FLOPS = 2 * M * M * K + 2 * M * M * R
BYTES = K * M + K * M // 32 + 2 * M * K + 2 * M * M + 2 * M * R + 2 * R + 4 * M * R

F32 = mybir.dt.float32
BF16 = mybir.dt.bfloat16
U32 = mybir.dt.uint32
I32 = mybir.dt.int32
U8 = mybir.dt.uint8
E4M3X4 = mybir.dt.float8_e4m3fn_x4
E5M2X4 = mybir.dt.float8_e5m2_x4
ALU = mybir.AluOpType

P = 128
PASS = 512
GROUPS = K // PASS
HALVES = M // PASS
ROW_TILES = PASS // P
STAGING = 8
VECTOR, SCALAR = "vector", "scalar"
MOVING, STATIONARY, MOVING_PLANE, STATIONARY_PLANE = 0, 64, 128, 192


def tile_weighted_diis_residuals_e3_kernel(tc, g_words, g_scales, errs, pair, coef, lam, out):
    nc = tc.nc
    with ExitStack() as ctx:
        keep = ctx.enter_context(tc.tile_pool(name="keep", bufs=1))
        stage = ctx.enter_context(tc.tile_pool(name="stage", bufs=STAGING))
        psum = ctx.enter_context(tc.psum_pool(name="psum", bufs=1))
        ctx.enter_context(tc.manual_schedule())

        def sb(shape, dtype, name):
            return keep.tile(shape, dtype, align_bytes=64, name=name)

        def placed(shape, dtype, name, past):
            pad = past // (1 if dtype == U8 else 4)
            t = keep.tile([P, pad + math.prod(shape[1:])], dtype, align_bytes=256, name=name)
            if len(shape) == 2:
                return t[:, pad:]
            return t[:, pad:].rearrange("p (a b) -> p a b", a=shape[1])

        def bank(b, shape):
            return psum.tile(shape, F32, name=f"bank{b}", tag=f"bank{b}")

        def move(engine, dst, src):
            if engine == VECTOR:
                nc.vector.tensor_copy(out=dst, in_=src)
            else:
                nc.scalar.copy(out=dst, in_=src)

        def mx_pass(acc, stationary, stationary_plane, moving, moving_plane, start, stop):
            nc.tensor.matmul_mx(
                out=acc,
                lhsT=stationary.bitcast(E5M2X4),
                lhsT_scale=stationary_plane,
                rhs=moving.bitcast(E4M3X4),
                rhs_scale=moving_plane,
                start=start,
                stop=stop,
            )

        ident = sb([P, P], F32, "ident")
        make_identity(nc, ident[:])
        lam_sb = sb([P, R], BF16, "lam_sb")

        front, back = range(0, 2), range(2, 4)
        near, far = range(0, 4), range(4, 8)
        low, high = range(0, 2), range(2, 4)
        first_half, second_half = range(0, 1), range(1, 2)

        raw_words, g_code, g_plane, plane_tile, pair_sb, coef_raw = {}, {}, {}, {}, {}, {}

        def load_errs(groups, rt):
            t = sb([P, len(groups) * PASS], BF16, f"errs0{rt}{groups[0]}")
            nc.sync.dma_start(out=t[:], in_=errs[rt * P : (rt + 1) * P, groups.start * PASS : groups.stop * PASS])
            for b, g in enumerate(groups):
                raw_words[0, rt, g] = (t[:].bitcast(F32), b)

        def load_strip(h, groups):
            t = sb([P, 2 * len(groups) * PASS], BF16, f"errs1{h}{groups[0]}")
            rows = errs[PASS + h * 2 * P : PASS + (h + 1) * 2 * P, groups.start * PASS : groups.stop * PASS]
            nc.sync.dma_start(out=t[:].rearrange("p (u k) -> p u k", u=2), in_=rows.rearrange("(p u) k -> p u k", u=2))
            for u in range(2):
                for b, g in enumerate(groups):
                    raw_words[1, 2 * h + u, g] = (t[:].bitcast(F32), u * len(groups) + b)

        def load_g(groups, tiles):
            t = placed([P, len(groups), len(tiles) * P], U32, f"g_code{groups[0]}{tiles[0]}", STATIONARY)
            as_bytes = g_words[groups.start : groups.stop].rearrange("g p n t -> p g (n t)")
            nc.sync.dma_start(out=t[:].bitcast(I32), in_=as_bytes[:, :, tiles.start * 4 * P : tiles.stop * 4 * P].bitcast(I32))
            for a, g in enumerate(groups):
                for b, i in enumerate(tiles):
                    g_code[i, g] = t[:, a, b * P : (b + 1) * P]

        def clear_plane(groups, tiles):
            t = placed([P, len(groups), len(tiles) * P], U8, f"g_plane{groups[0]}{tiles[0]}", STATIONARY_PLANE)
            nc.vector.memset(t[:].bitcast(I32), 0)
            plane_tile[groups, tiles] = t
            for a, g in enumerate(groups):
                for b, i in enumerate(tiles):
                    g_plane[i, g] = t[:, a, b * P : (b + 1) * P]

        def load_scales(groups, tiles, queue):
            for r in range(4):
                rows = g_scales[groups.start : groups.stop, r:16:4, tiles.start * P : tiles.stop * P]
                queue.dma_start(out=plane_tile[groups, tiles][r:P:32, :, :].bitcast(I32), in_=rows.rearrange("g q n -> q g n").bitcast(I32))

        def load_pair(halves, tiles):
            t = sb([P, len(tiles), len(halves) * PASS], BF16, f"pair{halves[0]}{tiles[0]}")
            piece = pair[tiles.start * P : tiles.stop * P, halves.start * PASS : halves.stop * PASS]
            nc.sync.dma_start(out=t[:], in_=piece.rearrange("(i p) n -> p i n", p=P))
            for b, j in enumerate(halves):
                for a, i in enumerate(tiles):
                    pair_sb[j, i] = (t[:, :, b * PASS : (b + 1) * PASS], a)

        def load_coef(j):
            coef_raw[j] = sb([P, 4, R], BF16, f"coef_raw{j}")
            nc.sync.dma_start(out=coef_raw[j][:], in_=coef[j * PASS : (j + 1) * PASS, :].rearrange("(p t) r -> p t r", t=4))

        sorted_words, errs_bank, errs_quads, errs_code, errs_plane = {}, {}, {}, {}, {}

        def group_words(j, rt, g, count=1):
            words, place = raw_words[j, rt, g]
            return words[:, place * 2 * P : (place + count) * 2 * P]

        def sort(j, pieces, engine):
            t = stage.tile([P, 2, 2, P], F32, align_bytes=64, name="sorted")
            rt, g = pieces[0]
            move(engine, t[:, : len(pieces)], group_words(j, rt, g, len(pieces)).rearrange("p (a w u) -> p a u w", a=len(pieces), u=2))
            for a, (rt, g) in enumerate(pieces):
                sorted_words[j, rt, g] = t[:, a]

        def sort_group(j, rts, g, engine):
            t = stage.tile([P, 2, 2, P], F32, align_bytes=64, name="sorted")
            words, place = raw_words[j, rts[0], g]
            move(engine, t[:], words.rearrange("p (a b w u) -> p a b u w", a=2, b=2, u=2)[:, :, place])
            for a, rt in enumerate(rts):
                sorted_words[j, rt, g] = t[:, a]

        def turn(j, pieces, b):
            t = bank(b, [P, 4, P])
            for a, piece in enumerate(pieces):
                errs_bank[j, piece] = (t, a)

        def turn_piece(j, piece):
            t, a = errs_bank[j, piece]
            rt, g = piece
            for u in range(2):
                if (j, rt, g) in sorted_words:
                    words = sorted_words[j, rt, g][:, u, :]
                else:
                    words = group_words(j, rt, g)[:, u : 2 * P : 2]
                nc.tensor.transpose(t[:, 2 * a + u, :], words, ident[:])

        def gathered(engine, source, count):
            t = stage.tile([P, 2 * P, 4], BF16, align_bytes=64, name="quads")
            words = t[:].rearrange("p n t -> p (n t)").bitcast(F32)[:, : 2 * count * P]
            move(
                engine,
                words.rearrange("p (b c i u) -> p b c u i", b=count, i=2, u=2),
                source.rearrange("p (b u) (c i) -> p b c u i", u=2, i=2),
            )
            return t[:, : count * P, :].rearrange("p n t -> p (n t)")

        def gather(j, pieces, engine):
            t, a = errs_bank[j, pieces[0]]
            quads = gathered(engine, t[:, 2 * a : 2 * (a + len(pieces)), :], len(pieces))
            for c, piece in enumerate(pieces):
                errs_quads[j, piece] = (quads, c)

        def quantise(j, pieces):
            rt, g = pieces[0]
            if (j, g) not in errs_code:
                errs_code[j, g] = placed([P, PASS], U32, f"errs_code{j}{g}", MOVING)
                errs_plane[j, g] = placed([P, PASS], U8, f"errs_plane{j}{g}", MOVING_PLANE)
            cols = slice(rt * P, (rt + len(pieces)) * P)
            quads, c = errs_quads[j, pieces[0]]
            nc.vector.quantize_mx(
                out=errs_code[j, g][:, cols].bitcast(E4M3X4), scales=errs_plane[j, g][:, cols], in_=quads[:, c * PASS : (c + len(pieces)) * PASS]
            )

        def of_group(rts, g):
            return [(rt, g) for rt in rts]

        def of_row_tile(rt, groups):
            return [(rt, g) for g in groups]

        held = {}
        b_acc, strip_acc, h_place, h_sb, h_bank, h_quads, h_code = {}, {}, {}, {}, {}, {}, {}

        def overlaps(j, tiles, groups, banks=None, rts=range(ROW_TILES)):
            cols = slice(rts.start * P, rts.stop * P)
            for g in groups:
                for a, i in enumerate(tiles):
                    first = g == 0 and rts.start == 0
                    last = g == GROUPS - 1 and rts.stop == ROW_TILES
                    if first:
                        b_acc[j, i] = bank(banks[a], [P, PASS])
                    mx_pass(b_acc[j, i][:, cols], g_code[i, g], g_plane[i, g], errs_code[j, g][:, cols], errs_plane[j, g][:, cols], first, last)

        def strip(h, tiles, b, groups=range(GROUPS)):
            if groups[0] == 0:
                strip_acc[h, tiles] = bank(b, [P, len(tiles), 2 * P])
            cols = slice(h * 2 * P, (h + 1) * 2 * P)
            for g in groups:
                for a, i in enumerate(tiles):
                    first, last = (g, a) == (0, 0), (g, a) == (GROUPS - 1, len(tiles) - 1)
                    acc = strip_acc[h, tiles][:, a, :]
                    mx_pass(acc, g_code[i, g], g_plane[i, g], errs_code[1, g][:, cols], errs_plane[1, g][:, cols], first, last)

        def weigh(i):
            t, a = pair_sb[0, i]
            h = sb([P, PASS], BF16, f"h0{i}")
            nc.vector.tensor_tensor(
                out=h[:].rearrange("p (u w e) -> p u w e", u=2, e=2),
                in0=b_acc[0, i][:].rearrange("p (w u e) -> p u w e", u=2, e=2),
                in1=t[:, a, :].rearrange("p (w u e) -> p u w e", u=2, e=2),
                op=ALU.mult,
            )
            for u in range(2):
                h_sb[0, i, u] = h[:, u * 2 * P : (u + 1) * 2 * P]

        def weigh_strip(h, tiles):
            if h == 0:
                both = sb([P, len(tiles), 2, 2, P], BF16, f"h1{tiles[0]}")
                for a, i in enumerate(tiles):
                    h_place[i] = (both, a)
                    for u in range(2):
                        h_sb[1, i, u] = both[:, a, u].rearrange("p h c -> p (h c)")
            both, first = h_place[tiles[0]]
            t, a = pair_sb[1, tiles[0]]
            nc.vector.tensor_tensor(
                out=both[:, first : first + len(tiles), :, h, :],
                in0=strip_acc[h, tiles][:].rearrange("p a (u c) -> p a u c", u=2),
                in1=t[:, a : a + len(tiles), h * 2 * P : (h + 1) * 2 * P].rearrange("p a (c u) -> p a u c", u=2),
                op=ALU.mult,
            )

        def hold_strip(tiles):
            held[tiles] = sb([P, len(tiles), 2 * P], F32, f"held{tiles[0]}")
            nc.scalar.copy(out=held[tiles][:], in_=strip_acc[0, tiles][:])

        def weigh_held(tiles, both):
            t, first = pair_sb[1, tiles[0]]
            for a, i in enumerate(tiles):
                h_place[i] = (both, a)
                for u in range(2):
                    h_sb[1, i, u] = both[:, a, u].rearrange("p h c -> p (h c)")
                nc.gpsimd.tensor_tensor(
                    out=both[:, a, :, 0, :],
                    in0=held[tiles][:, a, :].rearrange("p (u c) -> p u c", u=2),
                    in1=t[:, first + a, : 2 * P].rearrange("p (c u) -> p u c", u=2),
                    op=ALU.mult,
                )

        def weigh_whole(i):
            both = sb([P, 2, 2, P], BF16, f"h1{i}")
            for u in range(2):
                h_sb[1, i, u] = both[:, u].rearrange("p h c -> p (h c)")
            t, a = pair_sb[1, i]
            nc.vector.tensor_tensor(
                out=both[:].rearrange("p u h c -> p h u c"),
                in0=b_acc[1, i][:].rearrange("p (h u c) -> p h u c", h=2, u=2),
                in1=t[:, a, :].rearrange("p (h c u) -> p h u c", h=2, u=2),
                op=ALU.mult,
            )

        def turn_h(j, tiles, b):
            h_bank[j, tiles] = bank(b, [P, 4, P])
            for a, i in enumerate(tiles):
                for u in range(2):
                    nc.tensor.transpose(h_bank[j, tiles][:, 2 * a + u, :], h_sb[j, i, u].bitcast(F32), ident[:])

        def gather_h(j, tiles, engine=SCALAR):
            h_quads[j, tiles] = gathered(engine, h_bank[j, tiles][:, : 2 * len(tiles), :], len(tiles))

        def quantise_h(j, tiles):
            code = placed([P, len(tiles) * P], U32, f"h_code{j}{tiles[0]}", STATIONARY)
            plane = placed([P, len(tiles) * P], U8, f"h_plane{j}{tiles[0]}", STATIONARY_PLANE)
            nc.vector.quantize_mx(out=code[:].bitcast(E5M2X4), scales=plane[:], in_=h_quads[j, tiles])
            for a, i in enumerate(tiles):
                h_code[j, i] = (code[:, a * P : (a + 1) * P], plane[:, a * P : (a + 1) * P])

        coef_quads, coef_code, coef_plane, out_acc = {}, {}, {}, {}

        def interleave_coef(j, c, engine=SCALAR):
            coef_quads[j, c] = sb([P, R // 2, 4], BF16, f"coef_quads{j}{c}")
            rows = "(u e)" if j == 0 else "(e u)"
            move(
                engine,
                coef_quads[j, c][:].rearrange("p (a i) (u e) -> p a u e i", i=4, u=2),
                coef_raw[j][:, :, c * R // 2 : (c + 1) * R // 2].rearrange(f"p {rows} (a i) -> p a u e i", i=4, u=2),
            )

        def quantise_coef(j, c):
            if c == 0:
                coef_code[j] = placed([P, R], U32, f"coef_code{j}", MOVING)
                coef_plane[j] = placed([P, R], U8, f"coef_plane{j}", MOVING_PLANE)
            cols = slice(c * R // 2, (c + 1) * R // 2)
            nc.vector.quantize_mx(
                out=coef_code[j][:, cols].bitcast(E4M3X4),
                scales=coef_plane[j][:, cols],
                in_=coef_quads[j, c][:].rearrange("p n t -> p (n t)"),
            )

        def mix(i, banks, halves=range(HALVES)):
            width = R // len(banks)
            for j in halves:
                code, plane = h_code[j, i]
                for c, b in enumerate(banks):
                    if j == 0:
                        out_acc[i, c] = bank(b, [P, width])
                    cols = slice(c * width, (c + 1) * width)
                    mx_pass(out_acc[i, c][:], code, plane, coef_code[j][:, cols], coef_plane[j][:, cols], j == 0, j == HALVES - 1)

        def store(i, c=0):
            acc = out_acc[i, c]
            width = acc.shape[1]
            cols = slice(c * width, (c + 1) * width)
            res = sb([P, width], F32, f"res{i}{c}")
            nc.vector.tensor_tensor(out=res[:], in0=acc[:], in1=lam_sb[:, cols], op=ALU.subtract)
            nc.sync.dma_start(out=out[i * P : (i + 1) * P, cols], in_=res[:])

        clear_plane(high, near)
        zero_words = 64
        blank = sb([P, zero_words + (P + PASS) + (P + PASS) // 4], U32, "blank")
        nc.vector.memset(blank[:], 0)
        zeros = blank[:, :zero_words].bitcast(BF16)
        warm_code = blank[:, zero_words : zero_words + P + PASS]
        warm_plane = blank[:, zero_words + P + PASS :].bitcast(U8)
        for first, fmt in ((0, E5M2X4), (P, E4M3X4)):
            cols = slice(first, first + zero_words // 2)
            nc.vector.quantize_mx(out=warm_code[:, cols].bitcast(fmt), scales=warm_plane[:, cols], in_=zeros)

        def warm_up(count, b):
            t = bank(b, [P, PASS])
            for n in range(count):
                mx_pass(t[:], warm_code[:, :P], warm_plane[:, :P], warm_code[:, P:], warm_plane[:, P:], True, True)

        clear_plane(low, near)
        clear_plane(range(GROUPS), far)

        def load_quarter(groups):
            for rt in range(ROW_TILES):
                load_errs(groups, rt)

        load_quarter(low)
        load_scales(low, near, nc.sync)
        load_scales(high, near, nc.gpsimd)
        load_scales(range(GROUPS), far, nc.gpsimd)
        load_g(range(0, 1), near)
        load_g(range(1, 2), near)
        load_quarter(high)
        load_g(range(2, 3), near)
        load_g(range(3, 4), near)
        load_strip(0, low)
        load_strip(0, high)
        load_pair(first_half, near)
        load_g(low, far)
        load_g(high, far)
        load_pair(first_half, range(4, 6))
        load_strip(1, low)
        load_strip(1, high)
        load_pair(second_half, near)
        load_coef(0)
        load_pair(first_half, range(6, 8))
        load_pair(second_half, range(4, 6))
        load_coef(1)
        load_pair(second_half, range(6, 8))
        nc.sync.dma_start(out=lam_sb[:], in_=lam.partition_broadcast(P))

        warm_up(4, 0)
        for rt in range(3):
            sort(0, of_row_tile(rt, low), VECTOR)
        sort(0, [(3, 1)], VECTOR)
        for g in low:
            turn(0, of_group(front, g), 4 + g)
            for piece in of_group(front, g):
                turn_piece(0, piece)
            gather(0, of_group(front, g), SCALAR)
        for g in low:
            turn(0, of_group(back, g), 6 + g)
        for piece in ((2, 0), (2, 1), (3, 0), (3, 1)):
            turn_piece(0, piece)
        warm_up(1, 1)
        quantise(0, of_group(front, 0))
        quantise(0, of_group(front, 1))
        gather(0, of_group(back, 0), SCALAR)
        gather(0, of_group(back, 1), SCALAR)
        quantise(0, of_group(back, 0))
        overlaps(0, near, [0], near, front)
        overlaps(0, near, [1], rts=front)
        overlaps(0, near, [0], rts=back)

        sort(0, of_row_tile(0, high), VECTOR)
        quantise(0, of_group(back, 1))
        for rt in (1, 2):
            sort(0, of_row_tile(rt, high), VECTOR)
        for c, rts in enumerate((front, back)):
            for g in high:
                turn(0, of_group(rts, g), 2 + 2 * c + g)
        for piece in ((0, 2), (0, 3), (1, 2)):
            turn_piece(0, piece)
        gather(0, of_group(front, 2), SCALAR)
        turn_piece(0, (1, 3))
        gather(0, of_group(front, 3), SCALAR)
        sort(0, [(3, 2)], VECTOR)
        sort(0, [(3, 3)], VECTOR)
        overlaps(0, near, [1], rts=back)
        for piece in ((2, 2), (3, 2), (2, 3), (3, 3)):
            turn_piece(0, piece)
        for g in high:
            quantise(0, of_group(front, g))
        gather(0, of_group(back, 2), SCALAR)
        gather(0, of_group(back, 3), SCALAR)
        quantise(0, of_group(back, 2))
        overlaps(0, near, high, rts=front)
        overlaps(0, near, [2], rts=back)

        sort(1, of_row_tile(0, low), VECTOR)
        sort(1, of_row_tile(1, low), VECTOR)
        quantise(0, of_group(back, 3))
        sort(1, [(0, 2)], VECTOR)
        sort(1, [(1, 2)], SCALAR)
        sort_group(1, front, 3, VECTOR)
        for g in range(GROUPS):
            turn(1, of_group(front, g), 4 + g)
            for piece in of_group(front, g):
                turn_piece(1, piece)
            gather(1, of_group(front, g), VECTOR if g == 1 else SCALAR)
        for g in range(GROUPS):
            quantise(1, of_group(front, g))
        overlaps(0, near, [3], rts=back)
        for i in near:
            weigh(i)
        for g in range(GROUPS):
            strip(0, (0, 1), 4, [g])
            strip(0, (2, 3), 5, [g])

        overlaps(0, range(4, 7), low, (6, 7, 0))
        for i in range(4, 7):
            overlaps(0, [i], high)
        weigh(4)
        weigh(5)
        strip(0, (4, 5), 1)
        hold_strip((0, 1))
        hold_strip((2, 3))
        sort(1, of_row_tile(2, low), SCALAR)
        sort(1, of_row_tile(3, low), SCALAR)
        sort(1, of_row_tile(2, high), SCALAR)
        sort(1, of_row_tile(3, high), VECTOR)
        for g, b in enumerate((2, 4, 5, 6)):
            turn(1, of_group(back, g), b)
            for piece in of_group(back, g):
                turn_piece(1, piece)
            gather(1, of_group(back, g), VECTOR if g == 1 else SCALAR)
        for g in range(GROUPS):
            quantise(1, of_group(back, g))
        overlaps(0, [7], range(GROUPS), (3,))
        for j in range(HALVES):
            interleave_coef(j, 0)
            interleave_coef(j, 1)
        strip(1, (0, 1), 2)
        strip(1, (2, 3), 4)
        strip(1, (4, 5), 7)
        spent = errs_quads[1, (2, 3)][0].rearrange("p (a u h c) -> p a u h c", a=2, u=2, h=2)
        weigh_held((0, 1), spent)
        weigh_held((2, 3), sb([P, 2, 2, 2, P], BF16, "h12"))
        weigh(6)
        weigh(7)
        weigh_strip(1, (0, 1))
        weigh_strip(0, (4, 5))
        weigh_strip(1, (2, 3))

        turn_h(0, (0, 1), 5)
        turn_h(1, (0, 1), 6)
        turn_h(0, (2, 3), 0)
        turn_h(0, (4, 5), 2)
        turn_h(0, (6, 7), 3)
        turn_h(1, (2, 3), 4)
        for j, tiles in ((0, (0, 1)), (1, (0, 1)), (0, (2, 3)), (1, (2, 3)), (0, (4, 5)), (0, (6, 7))):
            gather_h(j, tiles)
        quantise_coef(0, 0)
        quantise_coef(0, 1)
        weigh_strip(1, (4, 5))
        quantise_coef(1, 0)
        quantise_coef(1, 1)
        overlaps(1, [6], range(GROUPS), (1,))
        quantise_h(0, (0, 1))
        quantise_h(1, (0, 1))
        quantise_h(0, (2, 3))
        quantise_h(1, (2, 3))
        weigh_whole(6)
        mix(0, (7,))
        mix(1, (5,))
        turn_h(1, (4, 5), 6)
        turn_h(1, (6,), 0)
        gather_h(1, (4, 5))
        gather_h(1, (6,))
        quantise_h(0, (4, 5))
        quantise_h(0, (6, 7))
        store(0)
        store(1)
        mix(2, (4,))
        mix(3, (2,))
        overlaps(1, [7], range(GROUPS), (3,))
        store(2)
        quantise_h(1, (4, 5))
        quantise_h(1, (6,))
        store(3)
        weigh_whole(7)
        mix(4, (1,))
        mix(5, (7,))
        turn_h(1, (7,), 5)
        gather_h(1, (7,))
        store(4)
        mix(6, (6,))
        store(5)
        quantise_h(1, (7,))
        mix(7, (0, 4))
        store(6)
        store(7, 0)
        store(7, 1)
